import numpy as np, ml_dtypes
CORES = [2,6,10,14,18,22,26,30]
N = 8
BF = ml_dtypes.bfloat16
W, C, L, CAP, H, RO = 4096, 2, 256, 32, 1, 3
def ends(a):
    return np.arange(W).reshape(L, C, N)[:, a].reshape(-1)
def pairs(rng):
    o = np.argsort(rng.random((8, W)), axis=1); b = np.zeros((8, W), np.int64)
    np.put_along_axis(b, o, np.concatenate([o[:, W // 2:], o[:, :W // 2]], axis=1), 1)
    return b
def mix(rng, p, z):
    a, b = pairs(rng)[None, :, None], pairs(rng)[None, :, None]; u = rng.random((N, 8, 16, W), dtype=np.float32)
    return np.where(u < p, a, np.where(u < p + (1 - p) * 0.8, b, z))
def odds(rng):
    k = np.array([0.95, 0.75, 0.5, 0.3, 0.1])
    return np.where(rng.random((N, 8, 1, W)) < 0.25, rng.choice(k, (N, 8, 1, W)), rng.choice(k, (1, 8, 1, W)))
def anyone(rng):
    return rng.integers(0, W, (N, 8, 16, W))
def pack(m, x, t):
    return {"mt": np.ascontiguousarray(m.reshape(N, 128, W)).astype(np.int32), "xv": np.ascontiguousarray(x.reshape(N, 128, W)).astype(np.float32).astype(BF),
            "th": np.ascontiguousarray(t.reshape(N, 8, 1)).astype(np.int32)}
def put(o, v, i):
    e = int(np.nonzero(o == v)[0][0]); o[e] = o[i]; o[i] = v
def brim(rng, mg, h, less):
    mg[:] = rng.integers(0, W, mg.shape); k = np.arange(N); n = np.arange(8); j = np.arange(12)
    p = N * C * rng.permutation(L)[:, None] + k; w = N * C * rng.permutation(L)[:, None] + N + k; p2 = p + N * (2 % C)
    v = p[:CAP].reshape(-1); c = rng.permutation(w[:CAP].reshape(-1)); mg[:, :, v] = c; mg[:, :, c] = v
    if less: mg[:, :, int(c[-1])] = int(v[0])
    far = rng.permutation(p[CAP:CAP + 12].reshape(-1)).reshape(12, N)
    for r in range(N):
        q = (r + 1 + 1 % (N - 1)) % N; u, d = w[CAP:CAP + 12, r], far[:, r]; o = np.argsort(rng.random((16, 12)), axis=0)
        mg[r][:, u] = d; mg[r][:, d] = u; mg[q][:, d] = np.where(o < h - 16 + j % 4, u, (u + 1) % W)
        q = (r + 1 + 2 % (N - 1)) % N; z, y = p2[CAP + 12:CAP + 20, r], w[CAP + 12:CAP + 20, q]; o = np.argsort(rng.random((16, 8)), axis=0); e = n * N + (q + 1) % N
        mg[r][:, z] = y; mg[r][:, y] = z; mg[q][:, v[e]] = z
        mg[q][:, y] = np.where(o < np.where(n % 2 == 0, 16, h - 16 + n // 2), c[e], mg[q][:, y])
def setup_inputs(rng):
    return pack(mix(rng, odds(rng), anyone(rng)), rng.integers(0, 256, (N, 8, 16, W)), rng.integers(6, 33, (N, 8, 1)))
def setup_inputs_spread(rng):
    p = np.exp2(-5 * rng.random((N, 8, 1, W))); z = (W * rng.random((N, 8, 16, W)) ** 4).astype(np.int64)
    x = np.floor(np.exp2(8 * rng.random((N, 8, 1, W))) * rng.random((N, 8, 16, W))) * (rng.random((N, 8, 1, W)) > 0.0625)
    return pack(mix(rng, p, z), x, (33 * rng.random((N, 8, 1)) ** 2).astype(np.int64))
def setup_inputs_ends(rng):
    k = rng.integers(0, 4, (N, 8, 1, W)); m = np.where(k < 2, k, rng.integers(0, 2, (N, 8, 16, W))) * (W - 1)
    x = rng.integers(0, 2, (N, 8, 16, W)) * 255; k = rng.integers(0, 4, (N, 8, 1, W)); last = x[..., W - 1:].copy()
    x = np.where(k == 0, last, np.where(k == 1, 255 - last, x)); n = W // (10 * C)
    for g in range(8):
        pr = []; mg, xg = m[:, g], x[:, g]
        for a in range(C):
            o = rng.permutation(ends(a)); put(o, W - N * C + N * a + N - 1, n if a == C - 1 else 0)
            if a == C - 1: put(o, N * a, 2 * n)
            pr.append(o)
        for a in range(C):
            v, c, b = pr[a][:n], pr[a - 1][n:2 * n], pr[a - 1][2 * n:3 * n]; kind = rng.integers(0, 4, n); kind[0] = 0
            first = rng.random((N, 16, n)) < 0.5; first[:, 0, 0] = g % 2 == 1; first[:, 15] = ~first[:, 0]
            mg[:, :, v] = np.where(first, c, b); mg[:, :, c] = v; mg[:, :, b] = v
            xc = xg[:, :, c]
            xg[:, :, v] = np.where(kind == 1, 255 - xc, np.where(kind == 2, xg[:, :, v], xc)); xg[:, :, b] = np.where(kind == 3, 255 - xc, xc)
    t = 32 * rng.integers(0, 2, (N, 8, 1)); t[:, 0] = 0; t[:, 7] = 32
    return pack(m, x, t)
def setup_inputs_corners(rng):
    z = ends(0); m = np.where(rng.random((N, 8, 16, W), dtype=np.float32) < 0.6, z[rng.integers(0, len(z), (N, 8, 16, W))], anyone(rng))
    x = rng.choice(np.array([0, 1, 254, 255]), (N, 8, 16, W)); t = rng.choice(np.array([1, 2, 7, 16, 17, 31, 32]), (N, 8, 1)); off = int(rng.integers(0, 6))
    for g in range(8):
        w = rng.permutation(ends(1))
        for r in range(N):
            v = z[r::N]; c = w[r * L:r * L + L]; h = int(t[r, g, 0]); q = (r + 1) % N
            ok = np.zeros(L, bool); ok[rng.permutation(L)[:(0, 1, CAP - 1, CAP, CAP + 1, L)[(g + r + off) % 6]]] = True
            s = np.where(ok, rng.integers(h, 33, L), rng.integers(0, h, L)); s = np.where(rng.random(L) < 0.6, h - 1 + ok, s)
            own = rng.integers(np.maximum(s - 16, 0), np.minimum(s, 16) + 1); o = np.argsort(rng.random((2, 16, L)), axis=1)
            for b, e, n in ((r, 0, own), (q, 1, s - own)):
                y = m[b, g][:, c]; y = np.where(y == v, (v + N * C) % W, y); m[b, g][:, c] = np.where(o[e] < n, v, y)
            m[r, g][:, v] = c
    return pack(m, x, t)
def setup_inputs_crowd(rng):
    m = mix(rng, odds(rng), anyone(rng)); x = rng.integers(0, 256, (N, 8, 16, W)); t = rng.integers(6, 33, (N, 8, 1))
    for g, h in ((0, 0), (1, 0), (2, 0), (4, 32), (5, 30), (6, 1)):
        mg = m[:, g]; late = []; t[:, g] = h
        for a in range(C):
            v = ends(a); w = rng.permutation(ends((a + 1) % C)); f = w[:4 if g % 4 == 2 else 1]
            mg[:, :, v] = f[rng.integers(0, len(f), len(v))]
            if g % 4 == 1: mg[:, :, int(v[int(rng.integers(0, N * CAP))])] = int(w[9])
            if a < C - 1: late.append((f, np.append(v[-1:], rng.choice(v, len(f) - 1))))
        for f, v in late:
            mg[:, :, f] = v
            if g % 4 == 1: mg[:, 5, f] = (v + 1) % W
    for g in (3, 7):
        h = int(rng.integers(18, 28)); t[:, g] = h; brim(rng, m[:, g], h, g == 7)
    return pack(m, x, t)
def setup_inputs_ties(rng):
    m = mix(rng, rng.choice(np.array([0.4, 0.5, 0.6]), (1, 8, 1, W)), anyone(rng))
    x = rng.integers(0, 255, (N, 8, 16, 1)) + rng.integers(0, 2, (N, 8, 1, W)) * (np.arange(8) % 2).reshape(1, 8, 1, 1)
    return pack(m, x, rng.integers(8, 20, (N, 8, 1)))
def check_inputs(d):
    bad = []
    for k, lo, hi in (("mt", 0, W - 1), ("xv", 0, 255), ("th", 0, 32)):
        a = np.asarray(d[k]).astype(np.float64)
        if not (np.min(a) >= lo and np.max(a) <= hi and np.all(a == np.floor(a))): bad.append("range of " + k)
    return bad
def reference(mt, xv, th):
    M = mt.astype(np.int64).reshape(N, 8, 16, W); X = xv.astype(np.float32).astype(np.int64).reshape(N, 8, 16, W); T = th.astype(np.int64).reshape(N, 8, 1)
    pi = np.full((8, W), -1, np.int64); grp = np.arange(8).reshape(8, 1, 1); A = 0
    for t in range(RO):
        a = t % C; lanes, cand, has, cnt = [], [], [], []
        for r in range(N):
            v = N * C * np.arange(L) + N * a + r; alive = pi[:, v] < 0
            old = M[r][:, :, v]; m = old
            for h in range(H):
                p = pi[grp, m]; m = np.where(p >= 0, np.take_along_axis(M[r], np.maximum(p, 0), 2), m)
            M[r][:, :, v] = np.where(alive[:, None], m, old)
            ix = m.reshape(8, 1, 16 * L)
            n = np.sum(np.take_along_axis(M[r], ix, 2).reshape(8, 16, 16, L) == v, axis=1)
            D = np.sum(np.abs(np.take_along_axis(X[r], ix, 2).reshape(8, 16, 16, L) - X[r][:, :, v][:, :, None, :]), axis=1)
            may = alive[:, None] & (pi[grp, m] < 0) & (m // N % C != a)
            k = np.argmax(np.where(may, 4096 * n - D, -2 ** 20), axis=1)[:, None]
            lanes.append(v); has.append(np.any(may, axis=1)); cand.append(np.take_along_axis(m, k, 1)[:, 0]); cnt.append(np.take_along_axis(n, k, 1)[:, 0])
        yes = []
        for r in range(N):
            q = (r + 1 + t % (N - 1)) % N
            s = cnt[r] + np.sum(np.take_along_axis(M[q], cand[r][:, None, :], 2) == lanes[r], axis=1)
            y = has[r] & (s >= T[r] + (A & 3)); before = np.add.accumulate(y.astype(np.int64), axis=1) - y
            yes.append(y & (before < CAP))
        cc = np.concatenate(cand, axis=1); yy = np.concatenate(yes, axis=1); vv = np.concatenate(lanes)
        won = np.zeros((8, N * L), bool)
        for g in range(8):
            j = np.nonzero(yy[g])[0]; u, first = np.unique(cc[g, j], return_index=True); won[g, j[first]] = True
        for r in range(N):
            v = lanes[r]; lose = has[r] & ~won[:, r * L:r * L + L]; x = X[r][:, :, v]
            X[r][:, :, v] = np.where(lose[:, None], (x + np.take_along_axis(X[r], cand[r][:, None, :], 2)) >> 1, x)
        gg, jj = np.nonzero(won); pi[gg, vv[jj]] = cc[gg, jj]; pi[gg, cc[gg, jj]] = vv[jj]; A = int(np.sum(won))
    ym = np.stack([M[r].reshape(128, W)[:, r::N] for r in range(N)]); yx = np.stack([X[r].reshape(128, W)[:, r::N] for r in range(N)])
    return {"yp": np.stack([pi] * N).astype(np.float32), "ym": ym.astype(np.float32), "yx": yx.astype(np.float32).astype(BF)}

@@ -1,0 +1,630 @@
+from concourse.bass import DstId, RemoteDMATransfer
+from concourse.mybir import AluOpType as A, AxisListType, ActivationFunctionType as AF
+
+W = 4096
+WD = 4608
+WX = 4864
+BIG = 16384.0
+F32, BF, F16, I32, U16 = "float32", "bfloat16", "float16", "int32", "uint16"
+
+SCRATCH = {
+    "MW": ("sbuf", [128, W], I32), "MF": ("sbuf", [128, WD], F32), "FT": ("sbuf", [128, WD], F32),
+    "IOT": ("sbuf", [128, WD], F32), "PI": ("sbuf", [128, WD], F32), "VT": ("sbuf", [128, W], F32),
+    "XR0": ("sbuf", [128, WX], BF), "XR1": ("sbuf", [128, WX], BF), "OWN": ("sbuf", [128, WD], BF),
+    "G16": ("sbuf", [128, W], F16), "G32": ("sbuf", [128, 1024], F32),
+    "EQ": ("sbuf", [128, W], BF), "GX": ("sbuf", [128, W], BF), "AB": ("sbuf", [128, W], BF),
+    "REP": ("sbuf", [128, 2048], BF), "DK16": ("sbuf", [128, 2048], F16), "DK32": ("sbuf", [128, 2048], F32),
+    "OFF": ("sbuf", [128, 256], U16), "M16": ("sbuf", [128, 256], F16), "OLD": ("sbuf", [128, 256], U16),
+    "XT0": ("sbuf", [128, 256], BF), "XT1": ("sbuf", [128, 256], BF), "XT2": ("sbuf", [128, 256], BF),
+    "SM": ("sbuf", [128, 256], BF), "XC": ("sbuf", [128, 256], BF), "QQ": ("sbuf", [128, 256], BF), "QY": ("sbuf", [128, 256], BF),
+    "YX": ("sbuf", [128, 512], BF), "YM": ("sbuf", [128, 512], F32),
+    "VAL": ("sbuf", [128, 512], F32), "PV0": ("sbuf", [128, 512], F32), "PV1": ("sbuf", [128, 512], F32),
+    "PV2": ("sbuf", [128, 512], F32),
+    "ID": ("sbuf", [128, 128], BF), "ONES": ("sbuf", [128, 128], BF), "ONE32": ("sbuf", [128, 128], F32),
+    "BLK": ("sbuf", [128, 128], BF), "WP": ("sbuf", [128, 128], BF), "PERM": ("sbuf", [128, 128], F16),
+    "KC": ("sbuf", [128, 128], BF), "QW": ("sbuf", [128, 240], F16),
+    "B8": ("sbuf", [128, 8], F32), "B8E": ("sbuf", [128, 8], BF), "B8A": ("sbuf", [128, 8], BF),
+    "KM": ("sbuf", [128, 16], F32), "PIDX": ("sbuf", [128, 4], I32), "PF": ("sbuf", [128, 4], F32),
+    "C1": ("sbuf", [128, 256], F32), "C2": ("sbuf", [128, 256], F32), "C3": ("sbuf", [128, 256], F32),
+    "C4": ("sbuf", [128, 128], F32), "C5": ("sbuf", [128, 128], F32), "C6": ("sbuf", [128, 48], F32),
+    "VB": ("sbuf", [128, 256], F32), "VC": ("sbuf", [128, 256], F32), "RST": ("sbuf", [128, 256], F32),
+    "ZERO": ("sbuf", [128, 256], F32),
+    "DIAG": ("sbuf", [128, 256], F32), "NSL": ("sbuf", [128, 256], BF), "EC": ("sbuf", [128, 256], F32),
+    "BIGS": ("sbuf", [128, 256], BF), "DUM": ("sbuf", [128, 48], F32), "T31": ("sbuf", [128, 2], F32),
+    "STEP": ("sbuf", [128, 64], F32),
+    "THR": ("sbuf", [128, 8], I32), "THB": ("sbuf", [128, 8], I32), "TH8": ("sbuf", [128, 8], F32),
+    "THC": ("sbuf", [128, 4], F32), "LT": ("sbuf", [128, 12], F32), "BIAS": ("sbuf", [128, 16], F32),
+    "PVN": ("sbuf", [128, 256], BF), "S1": ("sbuf", [128, 256], F32), "S2": ("sbuf", [128, 256], F32),
+    "S3": ("sbuf", [128, 256], F32), "SI": ("sbuf", [128, 256], I32), "SJ": ("sbuf", [128, 256], I32),
+    "CI": ("sbuf", [128, 16], I32), "CN": ("sbuf", [128, 32], I32), "RX": ("sbuf", [128, 4, 8, 8], F16),
+    "MSG0": ("sbuf", [128, 32], U16), "MSG1": ("sbuf", [128, 32], U16), "MSG2": ("sbuf", [128, 32], U16),
+    "LC0": ("sbuf", [128, 32], U16), "LC1": ("sbuf", [128, 32], U16), "LC2": ("sbuf", [128, 32], U16),
+    "ALL0": ("sbuf", [128, 8, 8], U16), "ALL1": ("sbuf", [128, 8, 8], U16), "ALL2": ("sbuf", [128, 8, 8], U16),
+    "EV": ("sbuf", [128, 256], BF), "NF": ("sbuf", [128, 256], BF), "EE": ("sbuf", [128, 260], F32),
+    "CT": ("sbuf", [128, 2, 260], F32), "SC": ("sbuf", [128, 2, 260], F32),
+    "EI": ("sbuf", [128, 8], I32), "C16": ("sbuf", [128, 2], U16), "CV4": ("sbuf", [128, 24], F32),
+    "NE": ("sbuf", [128, 128], F32), "CVL": ("sbuf", [128, 32], U16), "VCF": ("sbuf", [128, 96], F32),
+    "O20": ("sbuf", [128, 32], U16), "O21": ("sbuf", [128, 32], U16), "O22": ("sbuf", [128, 32], U16),
+    "WON": ("sbuf", [128, 16], F32), "AC": ("sbuf", [128, 4], F32), "AI": ("sbuf", [128, 4], I32),
+    "SO": ("sbuf", [128, 48], F32), "SOF": ("sbuf", [128, 16], U16),
+    "D0": ("psum", [128, 512], F32), "D1": ("psum", [128, 512], F32), "D2": ("psum", [128, 512], F32),
+    "D3": ("psum", [128, 512], F32), "D4": ("psum", [128, 512], F32),
+    "PS": ("psum", [128, 512], F32), "PA": ("psum", [128, 512], F32), "PB": ("psum", [128, 512], F32),
+}
+SEMAPHORES = ["qv", "qs", "qp", "qg", "lx", "lm0", "lm1", "lm2", "lm3", "lth", "out", "sent", "ath",
+              "ac0", "ac1", "ac2", "aa0", "aa1", "aa2"]
+PSUM = ("D0", "D1", "D2", "D3", "D4", "PS", "PA", "PB")
+
+
+def bits(m):
+    return bin(m).count("1")
+
+
+def spread(topo, src, dsts):
+    far = [d for d in dsts if topo.chip(d) != topo.chip(src)]
+    near = [d for d in dsts if topo.chip(d) == topo.chip(src)]
+    res = []
+    used = 0
+    if far:
+        used = topo.mask(src, far[0])
+        for d in far:
+            used &= topo.mask(src, d)
+        res.append((used, far))
+    if near:
+        res.append((topo.mask(src, near[0]) & ~used, near))
+    return res
+
+
+def rank_program(g, core, T, topo):
+    r = T.rank_of(core)
+    if r is None:
+        return
+    cores = list(T.cores)
+    N = len(cores)
+    eng = {"v": g.vector, "s": g.scalar, "p": g.tensor, "g": g, "y": g.sync}
+    cnt = {"v": 0, "s": 0, "p": 0, "g": 0}
+    seen = {q: {} for q in eng}
+    wr, rd = {}, {}
+    total = {}
+
+    def wait(q, sem, val):
+        if seen[q].get(sem, 0) < val:
+            eng[q].wait_ge(T.sem[sem], val)
+            seen[q][sem] = val
+
+    def parts(k):
+        b = k.split("#")
+        return b[0], (b[1] if len(b) > 1 else None)
+
+    def meet(table, k):
+        b, p = parts(k)
+        return [e for pp, es in table.get(b, {}).items() if p is None or pp is None or pp == p for e in es]
+
+    def order(q, reads, writes):
+        need = {}
+
+        def add(e):
+            need[e[1]] = max(need.get(e[1], 0), e[2])
+        for k in reads:
+            for e in meet(wr, k):
+                add(e)
+            if parts(k)[0] in PSUM:
+                for e in meet(rd, parts(k)[0]) + meet(wr, parts(k)[0]):
+                    if e[0] != q:
+                        add(e)
+        for k in writes:
+            for e in meet(wr, k) + meet(rd, k):
+                if not e[0] == q == "p":
+                    add(e)
+        for s, v in need.items():
+            wait(q, s, v)
+
+    def note(e, reads, writes):
+        for k in reads:
+            b, p = parts(k)
+            rd.setdefault(b, {}).setdefault(p, []).append(e)
+        for k in writes:
+            b, p = parts(k)
+            if p is None:
+                wr[b], rd[b] = {None: [e]}, {}
+            else:
+                wr.setdefault(b, {})[p] = [e]
+
+    def op(q, fn, reads, writes):
+        order(q, reads, writes)
+        cnt[q] += 1
+        fn().then_inc(T.sem["q" + q], 1)
+        total["q" + q] = cnt[q]
+        note((q, "q" + q, cnt[q]), reads, writes)
+
+    def dma(q, sem, fn, reads, writes):
+        order(q, reads, writes)
+        fn().then_inc(T.sem[sem], 16)
+        total[sem] = total.get(sem, 0) + 16
+        note(("d", sem, total[sem]), reads, writes)
+
+    def lands(sem, val, keys):
+        total[sem] = val
+        note(("d", sem, val), [], keys)
+
+    V, S, P = g.vector, g.scalar, g.tensor
+
+    def ts(out, in0, s1, s2, o0, o1, R, Wr):
+        if s2 is None:
+            op("v", lambda: V.tensor_scalar(out, in0, s1, None, o0), R, Wr)
+        else:
+            op("v", lambda: V.tensor_scalar(out, in0, s1, s2, o0, o1), R, Wr)
+
+    def tt(out, a, b, o, R, Wr):
+        op("v", lambda: V.tensor_tensor(out, a, b, o), R, Wr)
+
+    def cp(out, a, R, Wr):
+        op("v", lambda: V.tensor_copy(out, a), R, Wr)
+
+    def ms(out, c, Wr):
+        op("v", lambda: V.memset(out, c), [], Wr)
+
+    def scan(out, d0, d1, init, o0, o1, R, Wr):
+        op("v", lambda: V.tensor_tensor_scan(out, d0, d1, init, o0, o1), R, Wr)
+
+    def act(out, a, f, R, Wr, bias=0.0, scale=1.0):
+        op("s", lambda: S.activation(out, a, f, bias=bias, scale=scale), R, Wr)
+
+    def mm(out, l, rh, st, sp, R, Wr):
+        op("p", lambda: P.matmul(out, l, rh, st, sp), R, Wr)
+
+    def iota(out, pat, base, cm, Wr, flag=True):
+        if flag:
+            op("g", lambda: g.iota(out, pat, base, cm, allow_small_or_imprecise_dtypes=True), [], Wr)
+        else:
+            op("g", lambda: g.iota(out, pat, base, cm), [], Wr)
+
+    def send(src, pairs, sem, R):
+        order("g", R, [])
+        where = dict(pairs)
+        trs = []
+        for m, ds in spread(topo, core, [c for c, _ in pairs]):
+            ids = [DstId(rid=topo.addr(d)[0], pnc=topo.addr(d)[1]) for d in ds]
+            trs.append(RemoteDMATransfer(dst_ids=ids, dma_engine_mask=m, remote_sem=T.sem[sem], srcs=[src],
+                                         dsts=[where[d] for d in ds]))
+            total["sent"] = total.get("sent", 0) + bits(m)
+        g.remote_dma_fused(trs, local_sem=T.sem.sent)
+
+    def share(src, dsts):
+        for m, ds in spread(topo, src, dsts):
+            if core in ds:
+                return bits(m)
+        return 0
+
+    XR = [T.XR0, T.XR1]
+    XK = ["XR0", "XR1"]
+    XLK = ["XL0", "XL1"]
+    DB = [T.D0, T.D1, T.D2, T.D3, T.D4]
+    SB = [(T.PS, "PS"), (T.PB, "PB")]
+    PK, PG = T.PF[:, 0:1], T.PF[:, 1:2]
+    voters = [(r + 1 + t % (N - 1)) % N for t in range(3)]
+    clients = [(r - 1 - t % (N - 1)) % N for t in range(3)]
+
+    def lanes(buf, a):
+        return buf[:, 8 * a + r:W:16]
+
+    def xl(a):
+        return XR[1 - a][:, WD:WX]
+
+    def xtrans(t, a, bank, bk):
+        for h in range(2):
+            mm(bank[:, 128 * h:128 * h + 128], XR[1 - a][:, WD + 128 * h:WD + 128 * h + 128], T.ID[:], True, True,
+               [XLK[1 - a], "ID"], [bk])
+        act(T["XT%d" % t][:], bank[:, 0:256], AF.Copy, [bk], ["XT%d" % t])
+
+    def pre(t, j):
+        mm(DB[j % 5][:], T["XT%d" % t][:, 128 * (j // 4):128 * (j // 4) + 128],
+           T.REP[:, 512 * (j % 4):512 * (j % 4) + 512], True, False, ["XT%d" % t, "REP"], ["D%d" % (j % 5)])
+
+    def offs0(q):
+        cp(T.OFF[:, 64 * q:64 * q + 64], T.MW[:, 1024 * q + r:1024 * q + 1024:16], ["MW#%d" % q], ["OFF#%d" % q])
+
+    def gx(t, j, on_vector=False):
+        a = t % 2
+        if on_vector:
+            return cp(T.GX[:, 512 * j:512 * j + 512], XR[1 - a][:, 0:W].indirect(T.OFF[:, 32 * j:32 * j + 32]),
+                      [XK[1 - a], "OFF#%d" % (j // 2)], ["GX#%d" % j])
+        act(T.GX[:, 512 * j:512 * j + 512], XR[1 - a][:, 0:W].indirect(T.OFF[:, 32 * j:32 * j + 32]), AF.Copy,
+            [XK[1 - a], "OFF#%d" % (j // 2)], ["GX#%d" % j])
+
+    def dmm(t, j):
+        if j >= 5:
+            pre(t, j)
+        mm(DB[j % 5][:], T.ID[:], T.GX[:, 512 * j:512 * j + 512], False, True, ["ID", "GX#%d" % j], ["D%d" % (j % 5)])
+
+    def ab(j):
+        act(T.AB[:, 512 * j:512 * j + 512], DB[j % 5][:], AF.Abs, ["D%d" % (j % 5)], ["AB#%d" % j])
+
+    def mwin(t):
+        return (T.MW[:, 0:W], ["MW"]) if t == 0 else (T.MF[:, 0:W], ["MF"])
+
+    def eq(t, q):
+        win, R = mwin(t)
+        tt(T.EQ[:, 1024 * q:1024 * q + 1024], win.indirect(T.OFF[:, 64 * q:64 * q + 64]),
+           T.VT[:, 1024 * q:1024 * q + 1024], A.is_equal, R + ["OFF#%d" % q, "VT#%d" % q], ["EQ#%d" % q])
+
+    def pvn(t):
+        tt(T.PVN[:], lanes(T.FT, t % 2), T.C3[:], A.not_equal, ["FT", "C3"], ["PVN"])
+
+    def pen(h):
+        mm(SB[h][0][:, 0:128], T.PVN[:, 128 * h:128 * h + 128], T.WP[:], True, False, ["PVN", "WP"], [SB[h][1]])
+
+    def score(h, eqs):
+        src, wt, keys = (T.EQ, T.B8E, ["EQ#%d" % (2 * h), "EQ#%d" % (2 * h + 1), "B8E"]) if eqs else \
+            (T.AB, T.B8A, ["AB#%d" % (4 * h + i) for i in range(4)] + ["B8A"])
+        for k in range(16):
+            mm(SB[h][0][:, 15 - k:128:16], src[:, 2048 * h + k:2048 * h + 2048:16], wt[:], False, eqs and k == 15,
+               keys, [SB[h][1]])
+
+    def names():
+        for h in range(2):
+            mm(T.PA[:, 128 * h:128 * h + 128], T.ONES[:], T.KC[:], True, False, ["ONES", "KC"], ["PA"])
+            mm(T.PA[:, 128 * h:128 * h + 128], T.M16[:, 128 * h:128 * h + 128], T.PERM[:], False, True,
+               ["M16", "PERM"], ["PA"])
+
+    def m16():
+        ts(T.M16[:], T.OFF[:], -2048.0, None, A.add, None, ["OFF"], ["M16"])
+
+    def best(h):
+        c = slice(128 * h, 128 * h + 128)
+        bank, bk = SB[h]
+        k = "#%d" % h
+        scan(T.S1[:, c], T.RST[:, 0:128], bank[:, 0:128], 0.0, A.add, A.max, ["RST", bk], ["S1" + k])
+        tt(T.S2[:, c], T.S1[:, c], bank[:, 0:128], A.subtract, ["S1" + k, bk], ["S2" + k])
+        if h == 1:
+            ts(T.CN[:, 16:32], T.S1[:, 15:256:16], 2.0 ** -28, 64.498, A.mult, A.add, ["S1"], ["CN#n"])
+        scan(T.S3[:, c], T.S2[:, c], T.PA[:, c], 0.0, A.min, A.max, ["S2" + k, "PA"], ["S3" + k])
+        if h == 1:
+            cp(T.CI[:], T.S3[:, 15:256:16], ["S3"], ["CI"])
+            ts(T.CN[:, 0:16], T.CI[:], 4095, None, A.bitwise_and, None, ["CI"], ["CN#c"])
+
+    dma("y", "lx", lambda: g.sync.dma_start(T.XR1[:, 0:W], T.xv[:]), [], ["XR1#x"])
+    for q in range(4):
+        dma("y", "lm%d" % q, lambda q=q: g.sync.dma_start(T.MW[:, 1024 * q:1024 * q + 1024],
+                                                         T.mt[:, 1024 * q:1024 * q + 1024]), [], ["MW#%d" % q])
+    dma("g", "lth", lambda: g.dma_start(T.THR[0:1, 0:8], T.th[:], allow_slow_non_contiguous=True), [], ["THR"])
+
+    ms(T.ONES[:], 1.0, ["ONES"])
+    iota(T.PIDX[:, 0:1], [[1, 1]], 0, 1, ["PIDX#0"], False)
+    op("g", lambda: g.affine_select(T.ID[:], T.ONES[:], [[-1, 128]], A.is_equal, 0.0, 0, 1), ["ONES"], ["ID"])
+    iota(T.IOT[:, 0:512], [[1, 512]], 0, 0, ["IOT#0"])
+    iota(T.C4[:], [[1, 8], [0, 16]], 0, 0, ["C4"])
+    iota(T.C2[:], [[0, 16], [1, 16]], 0, 0, ["C2"])
+    for q in range(4):
+        iota(T.VT[:, 1024 * q:1024 * q + 1024], [[16, 64], [0, 16]], 1024 * q + r, 0, ["VT#%d" % q])
+    iota(T.C5[:], [[16, 8], [-1, 16]], 15, 0, ["C5"])
+    iota(T.KC[:], [[0, 8], [-32, 16]], 496, 0, ["KC"])
+    op("g", lambda: g.partition_broadcast(T.THB[:], T.THR[0:1, :], 128), ["THR"], ["THB"])
+
+    ms(T.BIAS[:, 9:10], BIG, ["BIAS#9"])
+    ms(T.BIAS[:, 10:11], W - 0.5, ["BIAS#10"])
+    ms(T.XR1[:, W:WD], BIG, ["XR1#d"])
+    ms(T.RST[:], 0.0, ["RST"])
+    ts(T.PIDX[:, 1:2], T.PIDX[:, 0:1], 15, None, A.bitwise_and, None, ["PIDX#0"], ["PIDX#1"])
+    ts(T.PIDX[:, 2:3], T.PIDX[:, 0:1], 4, None, A.arith_shift_right, None, ["PIDX#0"], ["PIDX#2"])
+    for k in range(16):
+        ts(T.REP[:, k:2048:16], T.ID[:], -1.0, None, A.mult, None, ["ID"], ["REP#%d" % k])
+    cp(T.PF[:, 2:3], T.PIDX[:, 0:1], ["PIDX#0"], ["PF#2"])
+    cp(T.PF[:, 0:2], T.PIDX[:, 1:3], ["PIDX#1", "PIDX#2"], ["PF#0"])
+    ms(T.RST[:, 0:256:16], -1e20, ["RST"])
+    ms(T.PVN[:], 0.0, ["PVN"])
+    ms(T.ZERO[:], 0.0, ["ZERO"])
+    ms(T.BIGS[:], BIG, ["BIGS"])
+    ts(T.B8[:], T.IOT[:, 0:8], PG, None, A.is_equal, None, ["IOT#0", "PF"], ["B8"])
+    ts(T.KM[:], T.IOT[:, 0:16], PK, None, A.is_equal, None, ["IOT#0", "PF"], ["KM"])
+    ts(T.VB[:], T.IOT[:, 0:256], 16.0, float(r), A.mult, A.add, ["IOT#0"], ["VB"])
+    ts(T.B8E[:], T.B8[:], 2.0 ** 28, None, A.mult, None, ["B8"], ["B8E"])
+    ts(T.B8A[:], T.B8[:], -2.0 ** 16, None, A.mult, None, ["B8"], ["B8A"])
+    ts(T.WP[:], T.C4[:], PG, -2.0 ** 37, A.is_equal, A.mult, ["C4", "PF"], ["WP"])
+    ts(T.BLK[:], T.C4[:], PG, None, A.is_equal, None, ["C4", "PF"], ["BLK"])
+    ts(T.QW[:], T.IOT[:, 0:240], -112.0, PK, A.add, A.is_equal, ["IOT#0", "PF"], ["QW"])
+    for j in range(8, 16):
+        ms(T.XR0[:, j:W:16], BIG, ["XR0#%d" % j])
+    ms(T.XR0[:, W:WD], BIG, ["XR0#d"])
+    cp(xl(0), lanes(T.XR1, 0), ["XR1#x"], ["XL1"])
+    cp(xl(1), lanes(T.XR1, 1), ["XR1#x"], ["XL0"])
+    xtrans(0, 0, T.PA, "PA")
+    xtrans(1, 1, T.PB, "PB")
+    for j in range(8):
+        cp(T.XR0[:, j:W:16], T.XR1[:, j:W:16], ["XR1#x"], ["XR0#%d" % j])
+    order("v", [], ["XR1#x"])
+    for j in range(8):
+        ms(T.XR1[:, j:W:16], BIG, ["XR1#%d" % j])
+    for j in range(5):
+        pre(0, j)
+
+    offs0(0)
+    gx(0, 0)
+    gx(0, 1, True)
+    for k in range(16):
+        ts(T.DK16[:, 128 * k:128 * k + 128], T.ID[:], T.KM[:, k:k + 1], None, A.mult, None, ["ID", "KM"],
+           ["DK16#%d" % k])
+    offs0(1)
+    dmm(0, 0)
+    ab(0)
+    dmm(0, 1)
+    ab(1)
+    gx(0, 2)
+    gx(0, 3, True)
+    ts(T.C2[:], T.C2[:], PK, -1e7, A.not_equal, A.mult, ["C2", "PF"], ["C2"])
+    ts(T.C3[:], T.IOT[:, 0:256], 8192.0, None, A.mult, None, ["IOT#0"], ["C3"])
+    offs0(2)
+    dmm(0, 2)
+    ab(2)
+    dmm(0, 3)
+    ab(3)
+    gx(0, 4)
+    gx(0, 5, True)
+    tt(T.DIAG[:], T.C2[:], T.C3[:], A.add, ["C2", "C3"], ["DIAG"])
+    offs0(3)
+    dmm(0, 4)
+    pen(0)
+    score(0, False)
+    ab(4)
+    dmm(0, 5)
+    ab(5)
+    gx(0, 6)
+    gx(0, 7)
+    dmm(0, 6)
+    ab(6)
+    dmm(0, 7)
+    ab(7)
+    eq(0, 0)
+    m16()
+    eq(0, 1)
+    ts(T.PERM[:], T.C5[:], T.PF[:, 2:3], None, A.is_equal, None, ["C5", "PF"], ["PERM"])
+    tt(T.TH8[:], T.THB[:], T.B8[:], A.mult, ["THB", "B8"], ["TH8"])
+    op("v", lambda: V.tensor_reduce(T.THC[:, 0:1], T.TH8[:], AxisListType.X, A.add), ["TH8"], ["THC"])
+    iota(T.C6[:, 0:32], [[-256, 2], [16, 16]], W + 256, 0, ["C6#a"])
+    iota(T.C6[:, 32:48], [[16, 16]], WD - 2048, 0, ["C6#b"])
+    iota(T.EC[:], [[-4096, 256]], 4096 * 256, 0, ["EC"])
+    iota(T.NSL[:], [[-8192, 256]], 0, 0, ["NSL"])
+    send(T.THC[:, 0:1], [(cores[voters[t]], T.LT[:, 4 * t:4 * t + 1]) for t in range(3)], "ath", ["THC"])
+    lands("ath", sum(share(cores[c], [cores[(c + 1 + t % (N - 1)) % N] for t in range(3)]) for c in clients), ["LT"])
+    names()
+    eq(0, 2)
+    eq(0, 3)
+    pen(1)
+    score(0, True)
+    score(1, False)
+    score(1, True)
+    for b in range(1, 9):
+        act(T.IOT[:, 512 * b:512 * b + 512], T.IOT[:, 0:512], AF.Identity, ["IOT#0"], ["IOT#%d" % b], bias=512.0 * b)
+
+    for t in range(3):
+        a = t % 2
+        MSG, LC, ALL, O2, PV = (T[n + str(t)] for n in ("MSG", "LC", "ALL", "O2", "PV"))
+        q, rho = voters[t], clients[t]
+        act(T.VC[:], T.VB[:], AF.Identity, ["VB"], ["VC"], bias=float(8 * a + rho - r))
+        best(0)
+        best(1)
+        for c in range(8):
+            ts(T.RX[:, :, :, c], T.CN[:], -2048.0, T.B8[:, c:c + 1], A.add, A.mult, ["CN", "B8"], ["RX#%d" % c])
+        for gg in range(8):
+            mm(T.PS[:, 0:32], T.QW[:, 112 - 16 * gg:240 - 16 * gg], T.RX[:, :, gg, :], gg == 0, gg == 7,
+               ["QW", "RX"], ["PS"])
+        ts(MSG[:], T.PS[:, 0:32], 2048.0, None, A.add, None, ["PS"], ["MSG"])
+        send(MSG[:], [(cores[q], LC[:])], "ac%d" % t, ["MSG"])
+        lands("ac%d" % t, share(cores[rho], [core]), ["LC"])
+
+        if t == 0:
+            iota(T.FT[:, 0:2304], [[1, 2304]], -2048, 0, ["FT#a"])
+            ts(T.BIAS[:, 0:1], T.LT[:, 0:1], -1.0, -64.0, A.mult, A.add, ["LT"], ["BIAS#0"])
+            ts(T.BIAS[:, 4:6], T.LT[:, 4:12:4], -1.0, -64.0, A.mult, A.add, ["LT"], ["BIAS#4"])
+            ts(T.DUM[:], T.C6[:], PK, None, A.add, None, ["C6", "PF"], ["DUM"])
+            ms(T.EE[:, 256:257], 0.0, ["EE#s"])
+            ts(T.CT[:, 0, 0:1], PK, -2.0 ** 21, None, A.mult, None, ["PF"], ["CT#i0"])
+            ts(T.CT[:, 1, 0:1], PK, 16.0, -2.0 ** 21, A.add, A.mult, ["PF"], ["CT#i1"])
+            ts(T.T31[:, 0:1], PK, -1.0, 31.0, A.mult, A.add, ["PF"], ["T31#0"])
+            ts(T.T31[:, 1:2], PK, -1.0, 15.0, A.mult, A.add, ["PF"], ["T31#1"])
+            ms(T.STEP[:], 1.0, ["STEP"])
+            ms(T.ONE32[:], 1.0, ["ONE32"])
+            ms(T.STEP[:, 0:64:32], -1e4, ["STEP"])
+        else:
+            ts(T.AI[:, 0:1], T.PA[:, 256:257], 0.5, 1024.0, A.mult, A.add, ["PA"], ["AI#0"])
+            ts(T.AI[:, 1:2], T.AI[:, 0:1], 3, None, A.bitwise_and, None, ["AI#0"], ["AI#1"])
+            ts(T.BIAS[:, 0:1], T.AI[:, 1:2], -1.0, T.BIAS[:, 3 + t:4 + t], A.mult, A.add, ["AI#1", "BIAS#4"],
+               ["BIAS#0"])
+        ts(T.SO[:, 0:16], T.PS[:, 16:32], 40.0 - 2048.0, 1e4, A.is_lt, A.mult, ["PS"], ["SO#0"])
+        tt(T.SO[:, 16:32], T.PS[:, 0:16], T.SO[:, 0:16], A.add, ["PS", "SO#0"], ["SO#1"])
+        tt(T.SO[:, 32:48], T.SO[:, 16:32], T.DUM[:, 32:48], A.min, ["SO#1", "DUM"], ["SO#2"])
+        ts(T.SOF[:], T.SO[:, 32:48], 2048.0, None, A.add, None, ["SO#2"], ["SOF"])
+        act(T.XC[:], XR[1 - a][:].indirect(T.SOF[:]), AF.Copy, [XK[1 - a], XLK[1 - a], "SOF"], ["XC"])
+        if t > 0:
+            tt(T.QY[:], xl(1 - a), T.QQ[:], A.max, [XLK[a], "QQ"], ["QY"])
+            if t == 1:
+                tt(xl(0), T.QY[:], lanes(T.XR0, 0), A.min, ["QY", "XR0"], ["XL1"])
+                xtrans(2, 0, T.PB, "PB")
+            else:
+                tt(T.YX[:, 1:512:2], T.QY[:], lanes(T.XR1, 1), A.min, ["QY", "XR1"], ["YX#b"])
+        tt(T.SI[:], T.XC[:], xl(a), A.add, ["XC", XLK[1 - a]], ["SI"])
+        ts(T.SJ[:], T.SI[:], 1, None, A.arith_shift_right, None, ["SI"], ["SJ"])
+        cp(T.SM[:], T.SJ[:], ["SJ"], ["SM"])
+        if t == 0:
+            cp(T.MF[:, 0:1024], T.MW[:, 0:1024], ["MW"], ["MF#0"])
+
+        win, R = mwin(t)
+        tt(T.EV[:], win.indirect(LC[:, 0:16]), T.VC[:], A.is_equal, R + ["LC", "VC"], ["EV"])
+        act(T.NF[:], T.IOT[:, 0:512].indirect(LC[:, 16:32]), AF.Identity, ["IOT#0", "LC", "BIAS#0"], ["NF"],
+            bias=T.BIAS[:, 0:1])
+        mm(T.PA[:, 0:256], T.ID[:], T.NF[:], True, False, ["ID", "NF"], ["PA"])
+        mm(T.PA[:, 0:256], T.BLK[:], T.EV[:], False, True, ["BLK", "EV"], ["PA"])
+        tt(T.EE[:, 0:256], T.IOT[:, 0:W].indirect(LC[:, 0:16]), T.EC[:], A.add, ["IOT", "LC", "EC"], ["EE#e"])
+        ts(T.S2[:], T.PA[:, 0:256], 0.0, 2.0 ** 21, A.is_ge, A.mult, ["PA"], ["S2"])
+        for c in range(2):
+            scan(T.CT[:, c, 1:257], T.ZERO[:], T.S2[:], T.CT[:, c, 0:1], A.add, A.add,
+                 ["ZERO", "S2", "CT#i%d" % c], ["CT#%d" % c])
+        for c in range(2):
+            scan(T.SC[:, c, 0:257], T.CT[:, c, 0:257], T.EE[:, 0:257], 0.0, A.min, A.max,
+                 ["CT#%d" % c, "CT#i%d" % c, "EE"], ["SC#%d" % c])
+        cp(T.EI[:, 0:2], T.SC[:, :, 256], ["SC"], ["EI#0"])
+        ts(T.EI[:, 2:4], T.EI[:, 0:2], 4095, None, A.bitwise_and, None, ["EI#0"], ["EI#1"])
+        ts(T.EI[:, 4:6], T.EI[:, 0:2], 12, None, A.arith_shift_right, None, ["EI#0"], ["EI#2"])
+        cp(T.C16[:], T.EI[:, 2:4], ["EI#1"], ["C16"])
+        cp(T.CV4[:, 0:2], T.EI[:, 2:4], ["EI#1"], ["CV4#c"])
+        ts(T.CV4[:, 4:6], T.EI[:, 4:6], 1e4, -5e3, A.mult, A.add, ["EI#2"], ["CV4#t"])
+        for c in range(2):
+            ts(T.NE[:, 32 * c:32 * c + 32], T.IOT[:, 0:W].indirect(T.C16[:]), T.CV4[:, c:c + 1], -1000.0,
+               A.not_equal, A.mult, ["IOT", "C16", "CV4#c"], ["NE#%d" % c])
+        tt(T.CV4[:, 6:8], T.CV4[:, 4:6], T.T31[:], A.min, ["CV4#t", "T31"], ["CV4#u"])
+        ts(T.CV4[:, 2:4], T.EI[:, 4:6], -16.0, float(W + 8 * a + rho), A.mult, A.add, ["EI#2"], ["CV4#v"])
+        scan(T.NE[:, 64:128], T.STEP[:], T.NE[:, 0:64], 0.0, A.add, A.max, ["STEP", "NE#0", "NE#1"], ["NE#s"])
+        tt(T.CV4[:, 8:10], T.NE[:, 95:128:32], T.CV4[:, 6:8], A.is_gt, ["NE#s", "CV4#u"], ["CV4#b"])
+        tt(T.CV4[:, 12:14], T.CV4[:, 8:10], T.DUM[:, 16 + 2 * rho:18 + 2 * rho], A.mult, ["CV4#b", "DUM"], ["CV4#x"])
+        tt(T.CV4[:, 14:16], T.CV4[:, 8:10], T.DUM[:, 2 * rho:2 * rho + 2], A.mult, ["CV4#b", "DUM"], ["CV4#y"])
+        tt(T.CV4[:, 16:20], T.CV4[:, 0:4], T.CV4[:, 12:16], A.max, ["CV4#c", "CV4#v", "CV4#x", "CV4#y"], ["CV4#z"])
+        cp(ALL[:, rho, 0:4], T.CV4[:, 16:20], ["CV4#z"], ["ALL#o"])
+        others = [cores[(r + i) % N] for i in range(1, N)]
+        send(ALL[:, rho, 0:4], [(c, ALL[:, rho, 0:4]) for c in others], "aa%d" % t, ["ALL#o"])
+        lands("aa%d" % t, sum(share(c, [d for d in cores if d != c]) for c in others), ["ALL#r"])
+
+        if t == 0:
+            iota(T.FT[:, 2304:WD], [[1, 2304]], 256, 0, ["FT#b"])
+            ms(T.MF[:, W:WD], 0.0, ["MFd"])
+            for b in range(1, 4):
+                cp(T.MF[:, 1024 * b:1024 * b + 1024], T.MW[:, 1024 * b:1024 * b + 1024], ["MW"], ["MF#%d" % b])
+            cp(T.OLD[:], lanes(T.MW, 1), ["MW"], ["OLD"])
+            cp(lanes(T.XR0, 0), T.SM[:], ["SM"], ["XR0"])
+            act(T.OWN[:], T.IOT[:], AF.Copy, ["IOT"], ["OWN"], scale=0.0)
+            act(T.VT[:], T.VT[:], AF.Identity, ["VT"], ["VT"], bias=8.0)
+        else:
+            cp(T.C1[:], T.OFF[:], ["OFF"], ["C1"])
+            tt(T.S2[:], lanes(T.MF, a), T.C1[:], A.subtract, ["MF", "C1"], ["S2"])
+            if t == 1:
+                act(lanes(T.MF, a), T.C1[:], AF.Copy, ["C1"], ["MF"])
+                act(T.VT[:], T.VT[:], AF.Identity, ["VT"], ["VT"], bias=-8.0)
+                cp(T.OLD[:], lanes(T.MW, 0), ["MW"], ["OLD"])
+                cp(lanes(T.XR1, 1), T.SM[:], ["SM"], ["XR1"])
+                cp(T.XR1[:, 0:WD].indirect(T.O20[:, 16:32]), T.BIGS[:], ["O20", "BIGS"], ["XR1"])
+            tt(T.S3[:], T.S2[:], T.PVN[:], A.mult, ["PVN", "S2"], ["S3"])
+            tt(T.YM[:, a:512:2], T.S3[:], T.C1[:], A.add, ["S3", "C1"], ["YM#%d" % a])
+            if t == 1:
+                cp(T.PI[:].indirect(T.O20[:]), T.PV0[:], ["O20", "PV0"], ["PI"])
+            else:
+                dma("y", "out", lambda: g.sync.dma_start(T.ym[:], T.YM[:]), ["YM"], [])
+                tt(T.C2[:], xl(0), T.SM[:], A.subtract, ["XL1", "SM"], ["C2"])
+                cp(T.PI[:].indirect(T.O21[:]), T.PV1[:], ["O21", "PV1"], ["PI"])
+        if t < 2:
+            for j in range(5):
+                pre(t + 1, j)
+
+        cp(T.CVL[:, 0:16], ALL[:, :, 0:2], ["ALL"], ["CVL#c"])
+        cp(T.CVL[:, 16:32], ALL[:, :, 2:4], ["ALL"], ["CVL#v"])
+        if t < 2:
+            act(T.VAL[:], T.MF[:].indirect(T.CVL[:]), AF.Identity, ["MF", "MFd", "CVL"], ["VAL"], bias=-2047.9375)
+            act(T.C3[:], T.VB[:], AF.Identity, ["VB"], ["C3"], bias=8.0 * (1 - a) - 2048.0)
+        act(PV[:], T.IOT[:].indirect(T.CVL[:]), AF.Copy, ["IOT", "CVL"], ["PV%d" % t])
+        if t == 0:
+            for k in range(16):
+                act(T.DK32[:, 128 * k:128 * k + 128], T.ID[:], AF.Identity, ["ID", "KM"], ["DK32#%d" % k],
+                    scale=T.KM[:, k:k + 1])
+        for p in range(N - 1, -1, -1):
+            cp(T.OWN[:].indirect(ALL[:, p, 0:2]), T.NSL[:, 32 * p:32 * p + 32], ["ALL", "NSL"], ["OWN"])
+            if p == N - 1:
+                cp(T.VCF[:, 0:16], ALL[:, :, 2:4], ["ALL"], ["VCF#v"])
+            if p == N - 2:
+                cp(T.VCF[:, 16:32], ALL[:, :, 0:2], ["ALL"], ["VCF#c"])
+        tt(T.S1[:], T.OWN[:].indirect(T.CVL[:, 0:16]), T.DIAG[:], A.add, ["OWN", "CVL#c", "DIAG"], ["S1"])
+        scan(T.S2[:], T.RST[:], T.S1[:], 0.0, A.add, A.max, ["RST", "S1"], ["S2"])
+        tt(T.VCF[:, 32:48], T.VCF[:, 0:16], T.S2[:, 15:256:16], A.max, ["VCF#v", "S2"], ["VCF#a"])
+        tt(T.VCF[:, 48:64], T.VCF[:, 16:32], T.S2[:, 15:256:16], A.max, ["VCF#c", "S2"], ["VCF#b"])
+        tt(T.VCF[:, 64:96], T.VCF[:, 32:64], T.DUM[:, 0:32], A.min, ["VCF#a", "VCF#b", "DUM"], ["VCF#2"])
+        ok = "O2%d" % t
+        cp(O2[:], T.VCF[:, 64:96], ["VCF#2"], [ok])
+        if t == 2:
+            cp(T.PI[:].indirect(O2[:]), PV[:], [ok, "PV2"], ["PI"])
+            dma("y", "out", lambda: g.sync.dma_start(T.yp[:], T.PI[0:128:16, 0:W]), ["PI"], [])
+            ts(T.S1[:], lanes(T.PI, 0), 0.0, None, A.is_ge, None, ["PI"], ["S1"])
+            tt(T.S3[:], T.S1[:], T.C2[:], A.mult, ["S1", "C2"], ["S3"])
+            tt(T.YX[:, 0:512:2], T.S3[:], T.SM[:], A.add, ["S3", "SM"], ["YX#a"])
+            dma("s", "out", lambda: g.scalar.dma_start(T.yx[:], T.YX[:]), ["YX"], [])
+            break
+        cp(T.FT[:].indirect(O2[:]), T.VAL[:], [ok, "VAL"], ["FT"])
+        op("s", lambda: S.activation(T.WON[:], T.VCF[:, 64:80], AF.Sign, bias=T.BIAS[:, 10:11], scale=-1.0,
+                                     accum_out=T.AC[:, 0:1]), ["VCF#2", "BIAS#10"], ["WON", "AC"])
+
+        u = t + 1
+
+        def follow(q):
+            win = T.FT[:, 0:W].indirect(T.OLD[:, 64 * q:64 * q + 64])
+            if q == 1:
+                act(T.G32[:], win, AF.Copy, ["FT", "OLD"], ["G16#1"])
+            else:
+                cp(T.G16[:, 1024 * q:1024 * q + 1024], win, ["FT", "OLD"], ["G16#%d" % q])
+
+        def keep(q):
+            bank, bk = (T.PA, "PA") if q % 2 == 0 else (T.PB, "PB")
+            for k in range(16):
+                if q == 1:
+                    mm(bank[:, 0:64], T.DK32[:, 128 * k:128 * k + 128], T.G32[:, k:1024:16], k == 0, k == 15,
+                       ["DK32", "G16#1"], [bk])
+                else:
+                    mm(bank[:, 0:64], T.DK16[:, 128 * k:128 * k + 128], T.G16[:, 1024 * q + k:1024 * q + 1024:16],
+                       k == 0, k == 15, ["DK16", "G16#%d" % q], [bk])
+
+        def offs(q):
+            bank, bk = (T.PA, "PA") if q % 2 == 0 else (T.PB, "PB")
+            ts(T.OFF[:, 64 * q:64 * q + 64], bank[:, 0:64], 2048.0, None, A.add, None, [bk], ["OFF#%d" % q])
+
+        follow(0)
+        follow(1)
+        keep(0)
+        cp(XR[a][:, 0:WD].indirect(O2[:, 0:16]), T.BIGS[:], [ok, "BIGS"], [XK[a]])
+        offs(0)
+        keep(1)
+        gx(u, 0)
+        gx(u, 1)
+        follow(2)
+        offs(1)
+        dmm(u, 0)
+        ab(0)
+        dmm(u, 1)
+        keep(2)
+        gx(u, 2)
+        ab(1)
+        eq(u, 0)
+        offs(2)
+        follow(3)
+        dmm(u, 2)
+        gx(u, 3)
+        ab(2)
+        dmm(u, 3)
+        keep(3)
+        gx(u, 4)
+        ab(3)
+        pvn(u)
+        offs(3)
+        m16()
+        dmm(u, 4)
+        gx(u, 5)
+        ab(4)
+        dmm(u, 5)
+        eq(u, 1)
+        pen(0)
+        score(0, False)
+        gx(u, 6)
+        ab(5)
+        dmm(u, 6)
+        names()
+        mm(T.PA[:, 256:257], T.ONE32[:], T.AC[:, 0:1], True, True, ["ONE32", "AC"], ["PA"])
+        score(0, True)
+        gx(u, 7)
+        ab(6)
+        dmm(u, 7)
+        ab(7)
+        eq(u, 2)
+        eq(u, 3)
+        pen(1)
+        score(1, False)
+        score(1, True)
+        act(T.QQ[:], lanes(XR[a], a), AF.Relu, [XK[a], "BIAS#9"], ["QQ"], bias=T.BIAS[:, 9:10], scale=-1.0)
+        if u == 1:
+            iota(T.PI[:], [[0, WD]], -1, 0, ["PI"])
+
+    for s, v in total.items():
+        wait("g", s, v)

@@ -2,58 +2,57 @@ from concourse.bass import DstId, RemoteDMATransfer
 from concourse.mybir import AluOpType as A, AxisListType, ActivationFunctionType as AF
 
 W = 4096
-WD = 4608
-WX = 4864
+WD = 4352
+WX = 4608
 BIG = 16384.0
+FO = 32.0
+STEPC = 4096 * 257
+B2 = 8192.0
+RND = 12582912.0
 F32, BF, F16, I32, U16 = "float32", "bfloat16", "float16", "int32", "uint16"
 
+
+def sb(cols, dtype):
+    return ("sbuf", [128] + (cols if isinstance(cols, list) else [cols]), dtype)
+
+
 SCRATCH = {
-    "MW": ("sbuf", [128, W], I32), "MF": ("sbuf", [128, WD], F32), "FT": ("sbuf", [128, WD], F32),
-    "IOT": ("sbuf", [128, WD], F32), "PI": ("sbuf", [128, WD], F32), "VT": ("sbuf", [128, W], F32),
-    "XR0": ("sbuf", [128, WX], BF), "XR1": ("sbuf", [128, WX], BF), "OWN": ("sbuf", [128, WD], BF),
-    "G16": ("sbuf", [128, W], F16), "G32": ("sbuf", [128, 1024], F32),
-    "EQ": ("sbuf", [128, W], BF), "GX": ("sbuf", [128, W], BF), "AB": ("sbuf", [128, W], BF),
-    "REP": ("sbuf", [128, 2048], BF), "DK16": ("sbuf", [128, 2048], F16), "DK32": ("sbuf", [128, 2048], F32),
-    "OFF": ("sbuf", [128, 256], U16), "M16": ("sbuf", [128, 256], F16), "OLD": ("sbuf", [128, 256], U16),
-    "XT0": ("sbuf", [128, 256], BF), "XT1": ("sbuf", [128, 256], BF), "XT2": ("sbuf", [128, 256], BF),
-    "SM": ("sbuf", [128, 256], BF), "XC": ("sbuf", [128, 256], BF), "QQ": ("sbuf", [128, 256], BF), "QY": ("sbuf", [128, 256], BF),
-    "YX": ("sbuf", [128, 512], BF), "YM": ("sbuf", [128, 512], F32),
-    "VAL": ("sbuf", [128, 512], F32), "PV0": ("sbuf", [128, 512], F32), "PV1": ("sbuf", [128, 512], F32),
-    "PV2": ("sbuf", [128, 512], F32),
-    "ID": ("sbuf", [128, 128], BF), "ONES": ("sbuf", [128, 128], BF), "ONE32": ("sbuf", [128, 128], F32),
-    "BLK": ("sbuf", [128, 128], BF), "WP": ("sbuf", [128, 128], BF), "PERM": ("sbuf", [128, 128], F16),
-    "KC": ("sbuf", [128, 128], BF), "QW": ("sbuf", [128, 240], F16),
-    "B8": ("sbuf", [128, 8], F32), "B8E": ("sbuf", [128, 8], BF), "B8A": ("sbuf", [128, 8], BF),
-    "KM": ("sbuf", [128, 16], F32), "PIDX": ("sbuf", [128, 4], I32), "PF": ("sbuf", [128, 4], F32),
-    "C1": ("sbuf", [128, 256], F32), "C2": ("sbuf", [128, 256], F32), "C3": ("sbuf", [128, 256], F32),
-    "C4": ("sbuf", [128, 128], F32), "C5": ("sbuf", [128, 128], F32), "C6": ("sbuf", [128, 48], F32),
-    "VB": ("sbuf", [128, 256], F32), "VC": ("sbuf", [128, 256], F32), "RST": ("sbuf", [128, 256], F32),
-    "ZERO": ("sbuf", [128, 256], F32),
-    "DIAG": ("sbuf", [128, 256], F32), "NSL": ("sbuf", [128, 256], BF), "EC": ("sbuf", [128, 256], F32),
-    "BIGS": ("sbuf", [128, 256], BF), "DUM": ("sbuf", [128, 48], F32), "T31": ("sbuf", [128, 2], F32),
-    "STEP": ("sbuf", [128, 64], F32),
-    "THR": ("sbuf", [128, 8], I32), "THB": ("sbuf", [128, 8], I32), "TH8": ("sbuf", [128, 8], F32),
-    "THC": ("sbuf", [128, 4], F32), "LT": ("sbuf", [128, 12], F32), "BIAS": ("sbuf", [128, 16], F32),
-    "PVN": ("sbuf", [128, 256], BF), "S1": ("sbuf", [128, 256], F32), "S2": ("sbuf", [128, 256], F32),
-    "S3": ("sbuf", [128, 256], F32), "SI": ("sbuf", [128, 256], I32), "SJ": ("sbuf", [128, 256], I32),
-    "CI": ("sbuf", [128, 16], I32), "CN": ("sbuf", [128, 32], I32), "RX": ("sbuf", [128, 4, 8, 8], F16),
-    "MSG0": ("sbuf", [128, 32], U16), "MSG1": ("sbuf", [128, 32], U16), "MSG2": ("sbuf", [128, 32], U16),
-    "LC0": ("sbuf", [128, 32], U16), "LC1": ("sbuf", [128, 32], U16), "LC2": ("sbuf", [128, 32], U16),
-    "ALL0": ("sbuf", [128, 8, 8], U16), "ALL1": ("sbuf", [128, 8, 8], U16), "ALL2": ("sbuf", [128, 8, 8], U16),
-    "EV": ("sbuf", [128, 256], BF), "NF": ("sbuf", [128, 256], BF), "EE": ("sbuf", [128, 260], F32),
-    "CT": ("sbuf", [128, 2, 260], F32), "SC": ("sbuf", [128, 2, 260], F32),
-    "EI": ("sbuf", [128, 8], I32), "C16": ("sbuf", [128, 2], U16), "CV4": ("sbuf", [128, 24], F32),
-    "NE": ("sbuf", [128, 128], F32), "CVL": ("sbuf", [128, 32], U16), "VCF": ("sbuf", [128, 96], F32),
-    "O20": ("sbuf", [128, 32], U16), "O21": ("sbuf", [128, 32], U16), "O22": ("sbuf", [128, 32], U16),
-    "WON": ("sbuf", [128, 16], F32), "AC": ("sbuf", [128, 4], F32), "AI": ("sbuf", [128, 4], I32),
-    "SO": ("sbuf", [128, 48], F32), "SOF": ("sbuf", [128, 16], U16),
-    "D0": ("psum", [128, 512], F32), "D1": ("psum", [128, 512], F32), "D2": ("psum", [128, 512], F32),
-    "D3": ("psum", [128, 512], F32), "D4": ("psum", [128, 512], F32),
-    "PS": ("psum", [128, 512], F32), "PA": ("psum", [128, 512], F32), "PB": ("psum", [128, 512], F32),
+    "MW": sb(W, I32), "MF": sb(WD, F32), "FT": sb(WD, F32), "IOT": sb(WD, F32), "PI": sb(WD, F32), "VT": sb(W, F32),
+    "XR0": sb(WX, BF), "XR1": sb(WX, BF), "G16": sb(W, F16), "G32": sb(1024, F32),
+    "EQ": sb(W, BF), "GX": sb(W, BF), "AB": sb(W, BF),
+    "REP": sb(2048, BF), "DK16": sb(2048, F16), "DK32": sb(2048, F32),
+    "OFF": sb(256, U16), "M16": sb(256, F16), "OLD0": sb(256, U16), "OLD1": sb(256, U16),
+    "O160": sb(256, F16), "O161": sb(256, F16), "CLS": sb(256, I32), "NCL": sb(256, BF),
+    "XT": sb([3, 256], BF),
+    "SM0": sb(256, BF), "SM1": sb(256, BF), "XC": sb(256, BF), "T1": sb(256, F32), "UU": sb(512, BF), "RY": sb(256, F32),
+    "YX": sb(768, BF), "YM": sb(512, F32), "OX": sb(128, BF), "OI": sb(2, U16), "OY": sb(2, U16), "TY": sb(2, F32),
+    "VALV": sb(256, F32), "VALC": sb(256, F32), "PV": sb(512, F32),
+    "ID": sb(128, BF), "NID": sb(128, BF), "ID8K": sb(128, BF), "NID4K": sb(128, BF),
+    "ID16": sb(128, F16), "NID16": sb(128, F16), "ID32": sb(128, F32),
+    "ONES": sb(128, BF), "ONE32": sb(128, F32),
+    "BLK": sb(128, BF), "WP": sb(128, BF), "PERM": sb(128, F16), "PERMB": sb(128, BF),
+    "KC": sb(128, BF), "QW": sb(240, F16),
+    "B8": sb(8, F32), "B8E": sb(8, BF), "B8A": sb(8, BF),
+    "KM": sb(16, F32), "PIDX": sb(4, I32), "PF": sb(4, F32),
+    "C2": sb(256, F32), "C4": sb(128, F32), "C5": sb(128, F32), "C6": sb([8, 4], F32), "C7": sb(16, F32),
+    "VB": sb(256, F32), "VC": sb([3, 256], F32),
+    "RST": sb(128, F32), "ZERO": sb(256, F32), "SCN": sb(256, F32), "EC": sb(256, F32), "BIGS": sb(256, BF),
+    "DUM": sb([8, 4], F32), "DUM2": sb([8, 4], F32), "DUL": sb(16, F32), "STEP": sb(68, F32), "OFS": sb(2, F32),
+    "THR": sb(8, I32), "THB": sb(8, I32), "TH8": sb(8, F32), "THC": sb(4, F32), "LT": sb(12, F32), "BIAS": sb(16, F32),
+    "PVN": sb(256, BF), "S1": sb(256, F32), "S2": sb(256, F32), "S3": sb(256, F32), "RR": sb(256, F32),
+    "CI": sb(16, I32), "CN": sb(32, I32), "RX": sb([4, 8, 8], F16),
+    "MSG": sb([3, 32], U16), "LC": sb([3, 32], U16),
+    "ALL0": sb([8, 8], U16), "ALL1": sb([8, 8], U16), "ALL2": sb([8, 8], U16),
+    "EV": sb(256, BF), "NF": sb(256, BF), "EE": sb([2, 260], F32), "CT": sb(260, F32), "SC": sb([2, 260], F32),
+    "EI": sb(8, I32), "C16": sb(2, U16), "CVF": sb(4, F32), "NE": sb(68, F32), "NS": sb(68, F32),
+    "CVL": sb(32, U16), "VCF": sb([8, 4], F32), "DL": sb([8, 4], F32), "VP": sb([8, 4], F32),
+    "TV": sb(32, F32), "TC": sb(32, F32), "O2V": sb(16, U16), "O2C": sb(16, U16),
+    "WON": sb(16, F32), "AC": sb(4, F32), "AI": sb(4, I32), "SO": sb(48, F32), "SOF": sb(16, U16),
 }
+PSUM = ("D0", "D1", "D2", "D3", "D4", "PS", "PA", "PB")
+SCRATCH.update({n: ("psum", [128, 512], F32) for n in PSUM})
 SEMAPHORES = ["qv", "qs", "qp", "qg", "lx", "lm0", "lm1", "lm2", "lm3", "lth", "out", "sent", "ath",
               "ac0", "ac1", "ac2", "aa0", "aa1", "aa2"]
-PSUM = ("D0", "D1", "D2", "D3", "D4", "PS", "PA", "PB")
 
 
 def bits(m):
@@ -173,6 +172,10 @@ def rank_program(g, core, T, topo):
     def mm(out, l, rh, st, sp, R, Wr):
         op("p", lambda: P.matmul(out, l, rh, st, sp), R, Wr)
 
+    def mms(bank, cols, terms):
+        for i, (wt, data, keys) in enumerate(terms):
+            mm(T[bank][:, cols], T[wt][:], data, i == 0, i == len(terms) - 1, [wt] + keys, [bank])
+
     def iota(out, pat, base, cm, Wr, flag=True):
         if flag:
             op("g", lambda: g.iota(out, pat, base, cm, allow_small_or_imprecise_dtypes=True), [], Wr)
@@ -204,6 +207,10 @@ def rank_program(g, core, T, topo):
     PK, PG = T.PF[:, 0:1], T.PF[:, 1:2]
     voters = [(r + 1 + t % (N - 1)) % N for t in range(3)]
     clients = [(r - 1 - t % (N - 1)) % N for t in range(3)]
+    lo, hi = slice(0, 256), slice(256, 512)
+
+    def ks(name, j0, j1):
+        return ["%s#%d" % (name, j) for j in range(j0, j1)]
 
     def lanes(buf, a):
         return buf[:, 8 * a + r:W:16]
@@ -211,26 +218,30 @@ def rank_program(g, core, T, topo):
     def xl(a):
         return XR[1 - a][:, WD:WX]
 
-    def xtrans(t, a, bank, bk):
+    def xtrans(t, halves, R, bank):
         for h in range(2):
-            mm(bank[:, 128 * h:128 * h + 128], XR[1 - a][:, WD + 128 * h:WD + 128 * h + 128], T.ID[:], True, True,
-               [XLK[1 - a], "ID"], [bk])
-        act(T["XT%d" % t][:], bank[:, 0:256], AF.Copy, [bk], ["XT%d" % t])
+            mm(T[bank][:, 128 * h:128 * h + 128], halves[h], T.ID[:], True, True, R + ["ID"], [bank])
+        act(T.XT[:, t, :], T[bank][:, lo], AF.Copy, [bank], ["XT%d" % t])
+
+    def raw(a):
+        return [T.XR1[:, 2048 * h + 8 * a + r:2048 * h + 2048:16] for h in range(2)]
 
     def pre(t, j):
-        mm(DB[j % 5][:], T["XT%d" % t][:, 128 * (j // 4):128 * (j // 4) + 128],
+        mm(DB[j % 5][:], T.XT[:, t, 128 * (j // 4):128 * (j // 4) + 128],
            T.REP[:, 512 * (j % 4):512 * (j % 4) + 512], True, False, ["XT%d" % t, "REP"], ["D%d" % (j % 5)])
 
-    def offs0(q):
-        cp(T.OFF[:, 64 * q:64 * q + 64], T.MW[:, 1024 * q + r:1024 * q + 1024:16], ["MW#%d" % q], ["OFF#%d" % q])
+    def names_of(t):
+        return (T.OLD0, "OLD0") if t == 0 else (T.OFF, "OFF")
 
-    def gx(t, j, on_vector=False):
-        a = t % 2
-        if on_vector:
-            return cp(T.GX[:, 512 * j:512 * j + 512], XR[1 - a][:, 0:W].indirect(T.OFF[:, 32 * j:32 * j + 32]),
-                      [XK[1 - a], "OFF#%d" % (j // 2)], ["GX#%d" % j])
-        act(T.GX[:, 512 * j:512 * j + 512], XR[1 - a][:, 0:W].indirect(T.OFF[:, 32 * j:32 * j + 32]), AF.Copy,
-            [XK[1 - a], "OFF#%d" % (j // 2)], ["GX#%d" % j])
+    def gx(t, j, q="s"):
+        off, ok = names_of(t)
+        xk = "XR1#x" if t == 0 else XK[1 - t % 2]
+        win = XR[1 - t % 2][:, 0:W].indirect(off[:, 32 * j:32 * j + 32])
+        out = T.GX[:, 512 * j:512 * j + 512]
+        if q == "v":
+            cp(out, win, [xk, "%s#%d" % (ok, j)], ["GX#%d" % j])
+        else:
+            act(out, win, AF.Copy, [xk, "%s#%d" % (ok, j)], ["GX#%d" % j])
 
     def dmm(t, j):
         if j >= 5:
@@ -243,38 +254,36 @@ def rank_program(g, core, T, topo):
     def mwin(t):
         return (T.MW[:, 0:W], ["MW"]) if t == 0 else (T.MF[:, 0:W], ["MF"])
 
-    def eq(t, q):
+    def eq(t, j0, j1):
         win, R = mwin(t)
-        tt(T.EQ[:, 1024 * q:1024 * q + 1024], win.indirect(T.OFF[:, 64 * q:64 * q + 64]),
-           T.VT[:, 1024 * q:1024 * q + 1024], A.is_equal, R + ["OFF#%d" % q, "VT#%d" % q], ["EQ#%d" % q])
+        off, ok = names_of(t)
+        vt, vk = (T.VT, "VT") if t % 2 == 0 else (T.MW, "MW")
+        c = slice(512 * j0, 512 * j1)
+        tt(T.EQ[:, c], win.indirect(off[:, 32 * j0:32 * j1]), vt[:, c], A.is_equal,
+           R + ks(ok, j0, j1) + ["%s#%d" % (vk, q) for q in range(j0 // 2, (j1 + 1) // 2)], ks("EQ", j0, j1))
 
-    def pvn(t):
-        tt(T.PVN[:], lanes(T.FT, t % 2), T.C3[:], A.not_equal, ["FT", "C3"], ["PVN"])
+    def pen(t, h):
+        src, wt = ("NCL", "PERMB") if t == 0 else ("PVN", "WP")
+        mm(SB[h][0][:, 0:128], T[src][:, 128 * h:128 * h + 128], T[wt][:], True, False, [src, wt], [SB[h][1]])
 
-    def pen(h):
-        mm(SB[h][0][:, 0:128], T.PVN[:, 128 * h:128 * h + 128], T.WP[:], True, False, ["PVN", "WP"], [SB[h][1]])
-
-    def score(h, eqs):
-        src, wt, keys = (T.EQ, T.B8E, ["EQ#%d" % (2 * h), "EQ#%d" % (2 * h + 1), "B8E"]) if eqs else \
-            (T.AB, T.B8A, ["AB#%d" % (4 * h + i) for i in range(4)] + ["B8A"])
+    def score(h, eqs, last):
+        src, wt = ("EQ", "B8E") if eqs else ("AB", "B8A")
         for k in range(16):
-            mm(SB[h][0][:, 15 - k:128:16], src[:, 2048 * h + k:2048 * h + 2048:16], wt[:], False, eqs and k == 15,
-               keys, [SB[h][1]])
+            mm(SB[h][0][:, 15 - k:128:16], T[src][:, 2048 * h + k:2048 * h + 2048:16], T[wt][:], False,
+               last and k == 15, ks(src, 4 * h, 4 * h + 4) + [wt], [SB[h][1]])
 
-    def names():
+    def names(t):
+        src = "O160" if t == 0 else "M16"
         for h in range(2):
             mm(T.PA[:, 128 * h:128 * h + 128], T.ONES[:], T.KC[:], True, False, ["ONES", "KC"], ["PA"])
-            mm(T.PA[:, 128 * h:128 * h + 128], T.M16[:, 128 * h:128 * h + 128], T.PERM[:], False, True,
-               ["M16", "PERM"], ["PA"])
-
-    def m16():
-        ts(T.M16[:], T.OFF[:], -2048.0, None, A.add, None, ["OFF"], ["M16"])
+            mm(T.PA[:, 128 * h:128 * h + 128], T[src][:, 128 * h:128 * h + 128], T.PERM[:], False, True,
+               [src, "PERM"], ["PA"])
 
     def best(h):
         c = slice(128 * h, 128 * h + 128)
         bank, bk = SB[h]
         k = "#%d" % h
-        scan(T.S1[:, c], T.RST[:, 0:128], bank[:, 0:128], 0.0, A.add, A.max, ["RST", bk], ["S1" + k])
+        scan(T.S1[:, c], T.RST[:], bank[:, 0:128], 0.0, A.add, A.max, ["RST", bk], ["S1" + k])
         tt(T.S2[:, c], T.S1[:, c], bank[:, 0:128], A.subtract, ["S1" + k, bk], ["S2" + k])
         if h == 1:
             ts(T.CN[:, 16:32], T.S1[:, 15:256:16], 2.0 ** -28, 64.498, A.mult, A.add, ["S1"], ["CN#n"])
@@ -282,6 +291,17 @@ def rank_program(g, core, T, topo):
         if h == 1:
             cp(T.CI[:], T.S3[:, 15:256:16], ["S3"], ["CI"])
             ts(T.CN[:, 0:16], T.CI[:], 4095, None, A.bitwise_and, None, ["CI"], ["CN#c"])
+
+    def mfloat(q):
+        cp(T.MF[:, 1024 * q:1024 * q + 1024], T.MW[:, 1024 * q:1024 * q + 1024], ["MW#%d" % q], ["MF#%d" % q])
+
+    def block0(q):
+        c = slice(64 * q, 64 * q + 64)
+        src = T.MW[:, 1024 * q + r:1024 * q + 1024:16]
+        cp(T.OLD0[:, c], src, ["MW#%d" % q], ks("OLD0", 2 * q, 2 * q + 2))
+        ts(T.CLS[:, c], src, 3, 1, A.arith_shift_right, A.bitwise_and, ["MW#%d" % q], ["CLS#%d" % q])
+        ts(T.O160[:, c], src, -2048.0, None, A.add, None, ["MW#%d" % q], ["O160#%d" % q])
+        ts(T.NCL[:, c], T.CLS[:, c], -1.0, None, A.add, None, ["CLS#%d" % q], ["NCL#%d" % q])
 
     dma("y", "lx", lambda: g.sync.dma_start(T.XR1[:, 0:W], T.xv[:]), [], ["XR1#x"])
     for q in range(4):
@@ -292,339 +312,365 @@ def rank_program(g, core, T, topo):
     ms(T.ONES[:], 1.0, ["ONES"])
     iota(T.PIDX[:, 0:1], [[1, 1]], 0, 1, ["PIDX#0"], False)
     op("g", lambda: g.affine_select(T.ID[:], T.ONES[:], [[-1, 128]], A.is_equal, 0.0, 0, 1), ["ONES"], ["ID"])
-    iota(T.IOT[:, 0:512], [[1, 512]], 0, 0, ["IOT#0"])
+    iota(T.IOT[:, 0:256], [[1, 256]], 0, 0, ["IOT#0"])
+    iota(T.VT[:, 0:512], [[16, 32], [0, 16]], r, 0, ["VT#a"])
     iota(T.C4[:], [[1, 8], [0, 16]], 0, 0, ["C4"])
-    iota(T.C2[:], [[0, 16], [1, 16]], 0, 0, ["C2"])
-    for q in range(4):
-        iota(T.VT[:, 1024 * q:1024 * q + 1024], [[16, 64], [0, 16]], 1024 * q + r, 0, ["VT#%d" % q])
     iota(T.C5[:], [[16, 8], [-1, 16]], 15, 0, ["C5"])
     iota(T.KC[:], [[0, 8], [-32, 16]], 496, 0, ["KC"])
-    op("g", lambda: g.partition_broadcast(T.THB[:], T.THR[0:1, :], 128), ["THR"], ["THB"])
 
-    ms(T.BIAS[:, 9:10], BIG, ["BIAS#9"])
-    ms(T.BIAS[:, 10:11], W - 0.5, ["BIAS#10"])
-    ms(T.XR1[:, W:WD], BIG, ["XR1#d"])
-    ms(T.RST[:], 0.0, ["RST"])
     ts(T.PIDX[:, 1:2], T.PIDX[:, 0:1], 15, None, A.bitwise_and, None, ["PIDX#0"], ["PIDX#1"])
     ts(T.PIDX[:, 2:3], T.PIDX[:, 0:1], 4, None, A.arith_shift_right, None, ["PIDX#0"], ["PIDX#2"])
-    for k in range(16):
-        ts(T.REP[:, k:2048:16], T.ID[:], -1.0, None, A.mult, None, ["ID"], ["REP#%d" % k])
     cp(T.PF[:, 2:3], T.PIDX[:, 0:1], ["PIDX#0"], ["PF#2"])
     cp(T.PF[:, 0:2], T.PIDX[:, 1:3], ["PIDX#1", "PIDX#2"], ["PF#0"])
-    ms(T.RST[:, 0:256:16], -1e20, ["RST"])
-    ms(T.PVN[:], 0.0, ["PVN"])
+    for j in range(8, 16):
+        ms(T.XR0[:, j:W:16], BIG, ["XR0#%d" % j])
+    ms(T.XR0[:, W:WD], BIG, ["XR0#d"])
+    ms(T.XR1[:, W:WD], BIG, ["XR1#d"])
+    ms(T.MF[:, W:WD], 0.0, ["MFd"])
+    ms(T.YX[:, 512:768], 0.0, ["YX#d"])
+    ms(T.RST[:], 0.0, ["RST"])
     ms(T.ZERO[:], 0.0, ["ZERO"])
     ms(T.BIGS[:], BIG, ["BIGS"])
+    ms(T.ONE32[:], 1.0, ["ONE32"])
+    ms(T.STEP[:], 0.0, ["STEP"])
+    ms(T.NE[:], 0.0, ["NE"])
+    ms(T.BIAS[:, 10:11], W - 0.5, ["BIAS#10"])
+    ms(T.RST[:, 0:128:16], -1e20, ["RST"])
+    for k in range(16):
+        ts(T.REP[:, k:2048:16], T.ID[:], -1.0, None, A.mult, None, ["ID"], ["REP#%d" % k])
     ts(T.B8[:], T.IOT[:, 0:8], PG, None, A.is_equal, None, ["IOT#0", "PF"], ["B8"])
     ts(T.KM[:], T.IOT[:, 0:16], PK, None, A.is_equal, None, ["IOT#0", "PF"], ["KM"])
+    iota(T.C2[:], [[0, 16], [1, 16]], 0, 0, ["C2"])
+    iota(T.C6[:], [[32, 8], [0, 2], [16, 2]], W, 0, ["C6"])
+    iota(T.C7[:], [[16, 16]], WD - 2048, 0, ["C7"])
+    iota(T.EC[:], [[-4096, 256]], 4096 * 256 - 8 * STEPC, 0, ["EC"])
+    iota(T.FT[:, 0:2048], [[1, 2048]], int(FO), 0, ["FT#a"])
+    iota(T.FT[:, 2048:W], [[1, 2048]], 2048 + int(FO), 0, ["FT#b"])
+    op("g", lambda: g.partition_broadcast(T.THB[:], T.THR[0:1, :], 128), ["THR"], ["THB"])
+
+    act(T.VT[:, 512:1024], T.VT[:, 0:512], AF.Identity, ["VT#a"], ["VT#0"], bias=512.0)
+    for q in range(1, 4):
+        act(T.VT[:, 1024 * q:1024 * q + 1024], T.VT[:, 0:1024], AF.Identity, ["VT#a", "VT#0"], ["VT#%d" % q],
+            bias=1024.0 * q)
+    n = 256
+    while n < WD:
+        m = min(n, WD - n)
+        act(T.IOT[:, n:n + m], T.IOT[:, 0:m], AF.Identity, ["IOT"], ["IOT#%d" % n], bias=float(n))
+        n += m
     ts(T.VB[:], T.IOT[:, 0:256], 16.0, float(r), A.mult, A.add, ["IOT#0"], ["VB"])
+
+    for name, f in (("NID", -1.0), ("ID8K", 8192.0), ("NID4K", -4096.0), ("ID16", 1.0), ("NID16", -1.0), ("ID32", 1.0)):
+        ts(T[name][:], T.ID[:], f, None, A.mult, None, ["ID"], [name])
     ts(T.B8E[:], T.B8[:], 2.0 ** 28, None, A.mult, None, ["B8"], ["B8E"])
     ts(T.B8A[:], T.B8[:], -2.0 ** 16, None, A.mult, None, ["B8"], ["B8A"])
     ts(T.WP[:], T.C4[:], PG, -2.0 ** 37, A.is_equal, A.mult, ["C4", "PF"], ["WP"])
     ts(T.BLK[:], T.C4[:], PG, None, A.is_equal, None, ["C4", "PF"], ["BLK"])
     ts(T.QW[:], T.IOT[:, 0:240], -112.0, PK, A.add, A.is_equal, ["IOT#0", "PF"], ["QW"])
-    for j in range(8, 16):
-        ms(T.XR0[:, j:W:16], BIG, ["XR0#%d" % j])
-    ms(T.XR0[:, W:WD], BIG, ["XR0#d"])
-    cp(xl(0), lanes(T.XR1, 0), ["XR1#x"], ["XL1"])
-    cp(xl(1), lanes(T.XR1, 1), ["XR1#x"], ["XL0"])
-    xtrans(0, 0, T.PA, "PA")
-    xtrans(1, 1, T.PB, "PB")
-    for j in range(8):
-        cp(T.XR0[:, j:W:16], T.XR1[:, j:W:16], ["XR1#x"], ["XR0#%d" % j])
-    order("v", [], ["XR1#x"])
-    for j in range(8):
-        ms(T.XR1[:, j:W:16], BIG, ["XR1#%d" % j])
-    for j in range(5):
-        pre(0, j)
-
-    offs0(0)
-    gx(0, 0)
-    gx(0, 1, True)
+    ts(T.PERM[:], T.C5[:], T.PF[:, 2:3], None, A.is_equal, None, ["C5", "PF"], ["PERM"])
+    ts(T.PERMB[:], T.C5[:], T.PF[:, 2:3], 2.0 ** 37, A.is_equal, A.mult, ["C5", "PF"], ["PERMB"])
     for k in range(16):
         ts(T.DK16[:, 128 * k:128 * k + 128], T.ID[:], T.KM[:, k:k + 1], None, A.mult, None, ["ID", "KM"],
            ["DK16#%d" % k])
-    offs0(1)
-    dmm(0, 0)
-    ab(0)
-    dmm(0, 1)
-    ab(1)
-    gx(0, 2)
-    gx(0, 3, True)
-    ts(T.C2[:], T.C2[:], PK, -1e7, A.not_equal, A.mult, ["C2", "PF"], ["C2"])
-    ts(T.C3[:], T.IOT[:, 0:256], 8192.0, None, A.mult, None, ["IOT#0"], ["C3"])
-    offs0(2)
-    dmm(0, 2)
-    ab(2)
-    dmm(0, 3)
-    ab(3)
-    gx(0, 4)
-    gx(0, 5, True)
-    tt(T.DIAG[:], T.C2[:], T.C3[:], A.add, ["C2", "C3"], ["DIAG"])
-    offs0(3)
-    dmm(0, 4)
-    pen(0)
-    score(0, False)
-    ab(4)
-    dmm(0, 5)
-    ab(5)
-    gx(0, 6)
-    gx(0, 7)
-    dmm(0, 6)
-    ab(6)
-    dmm(0, 7)
-    ab(7)
-    eq(0, 0)
-    m16()
-    eq(0, 1)
-    ts(T.PERM[:], T.C5[:], T.PF[:, 2:3], None, A.is_equal, None, ["C5", "PF"], ["PERM"])
+    ts(T.STEP[:, 0:16], T.KM[:], 2 * B2, None, A.mult, None, ["KM"], ["STEP"])
+    ts(T.STEP[:, 50:66], T.KM[:], 2 * B2, None, A.mult, None, ["KM"], ["STEP"])
+    ms(T.STEP[:, 32:67:34], -2 * B2, ["STEP"])
+    ms(T.STEP[:, 33:34], -4 * B2, ["STEP"])
+    ms(T.EE[:, 0, 256:257], -8.0 * STEPC, ["EE#s"])
+    ms(T.OFS[:, 0:1], 8.0 * STEPC, ["OFS#0"])
+    ms(T.OFS[:, 1:2], -8.0 * STEPC, ["OFS#1"])
+    ts(T.CT[:, 0:1], PK, 8.0, -1.0 * STEPC, A.add, A.mult, ["PF"], ["CT#i"])
+    ts(T.S1[:], T.C2[:], PK, -1.0, A.is_lt, A.mult, ["C2", "PF"], ["S1"])
+    ts(T.S2[:], T.C2[:], PK, None, A.is_equal, None, ["C2", "PF"], ["S2"])
+    tt(T.SCN[:], T.S1[:], T.S2[:], A.add, ["S1", "S2"], ["SCN"])
+    ts(T.DUM[:], T.C6[:], PK, None, A.add, None, ["C6", "PF"], ["DUM"])
+    ts(T.DUM2[:], T.C6[:], PK, 2.0, A.add, A.mult, ["C6", "PF"], ["DUM2"])
+    ts(T.DUL[:], T.C7[:], PK, None, A.add, None, ["C7", "PF"], ["DUL"])
+    ts(T.SCN[:, 15:256:16], T.SCN[:, 15:256:16], -3.0, None, A.add, None, ["SCN"], ["SCN"])
+
+    xtrans(0, raw(0), ["XR1#x"], "D4")
+    for j in range(5):
+        pre(0, j)
+    for q in range(4):
+        block0(q)
+        for j in (2 * q, 2 * q + 1):
+            gx(0, j)
+            dmm(0, j)
+        if q < 3:
+            mfloat(q)
+        else:
+            eq(0, 0, 2)
+            pen(0, 0)
+            pen(0, 1)
+            names(0)
+            score(0, False, False)
+        ab(2 * q)
+        ab(2 * q + 1)
     tt(T.TH8[:], T.THB[:], T.B8[:], A.mult, ["THB", "B8"], ["TH8"])
     op("v", lambda: V.tensor_reduce(T.THC[:, 0:1], T.TH8[:], AxisListType.X, A.add), ["TH8"], ["THC"])
-    iota(T.C6[:, 0:32], [[-256, 2], [16, 16]], W + 256, 0, ["C6#a"])
-    iota(T.C6[:, 32:48], [[16, 16]], WD - 2048, 0, ["C6#b"])
-    iota(T.EC[:], [[-4096, 256]], 4096 * 256, 0, ["EC"])
-    iota(T.NSL[:], [[-8192, 256]], 0, 0, ["NSL"])
     send(T.THC[:, 0:1], [(cores[voters[t]], T.LT[:, 4 * t:4 * t + 1]) for t in range(3)], "ath", ["THC"])
     lands("ath", sum(share(cores[c], [cores[(c + 1 + t % (N - 1)) % N] for t in range(3)]) for c in clients), ["LT"])
-    names()
-    eq(0, 2)
-    eq(0, 3)
-    pen(1)
-    score(0, True)
-    score(1, False)
-    score(1, True)
-    for b in range(1, 9):
-        act(T.IOT[:, 512 * b:512 * b + 512], T.IOT[:, 0:512], AF.Identity, ["IOT#0"], ["IOT#%d" % b], bias=512.0 * b)
+    eq(0, 2, 4)
+    score(0, True, True)
+    eq(0, 4, 6)
+    score(1, False, False)
+    eq(0, 6, 8)
+    best(0)
+    score(1, True, True)
+    for t in range(3):
+        act(T.VC[:, t, :], T.VB[:], AF.Identity, ["VB"], ["VC%d" % t], bias=float(8 * (t % 2) + clients[t] - r))
+    act(T.FT[:, W:WD], T.IOT[:, W:WD], AF.Silu, ["IOT"], ["FT#d"])
+    act(xl(0), lanes(T.XR1, 0), AF.Copy, ["XR1#x"], ["XL1"])
+    for j in range(8):
+        act(T.XR0[:, j:W:16], T.XR1[:, j:W:16], AF.Copy, ["XR1#x"], ["XR0#%d" % j])
 
     for t in range(3):
         a = t % 2
-        MSG, LC, ALL, O2, PV = (T[n + str(t)] for n in ("MSG", "LC", "ALL", "O2", "PV"))
+        MSG, ALL = T.MSG[:, t, :], T["ALL%d" % t]
+        lc, ln = T.LC[:, t, 0:16], T.LC[:, t, 16:32]
         q, rho = voters[t], clients[t]
-        act(T.VC[:], T.VB[:], AF.Identity, ["VB"], ["VC"], bias=float(8 * a + rho - r))
-        best(0)
         best(1)
         for c in range(8):
             ts(T.RX[:, :, :, c], T.CN[:], -2048.0, T.B8[:, c:c + 1], A.add, A.mult, ["CN", "B8"], ["RX#%d" % c])
         for gg in range(8):
             mm(T.PS[:, 0:32], T.QW[:, 112 - 16 * gg:240 - 16 * gg], T.RX[:, :, gg, :], gg == 0, gg == 7,
                ["QW", "RX"], ["PS"])
-        ts(MSG[:], T.PS[:, 0:32], 2048.0, None, A.add, None, ["PS"], ["MSG"])
-        send(MSG[:], [(cores[q], LC[:])], "ac%d" % t, ["MSG"])
+        ts(MSG, T.PS[:, 0:32], 2048.0, None, A.add, None, ["PS"], ["MSG"])
+        send(MSG, [(cores[q], T.LC[:, t, :])], "ac%d" % t, ["MSG"])
         lands("ac%d" % t, share(cores[rho], [core]), ["LC"])
 
         if t == 0:
-            iota(T.FT[:, 0:2304], [[1, 2304]], -2048, 0, ["FT#a"])
             ts(T.BIAS[:, 0:1], T.LT[:, 0:1], -1.0, -64.0, A.mult, A.add, ["LT"], ["BIAS#0"])
             ts(T.BIAS[:, 4:6], T.LT[:, 4:12:4], -1.0, -64.0, A.mult, A.add, ["LT"], ["BIAS#4"])
-            ts(T.DUM[:], T.C6[:], PK, None, A.add, None, ["C6", "PF"], ["DUM"])
-            ms(T.EE[:, 256:257], 0.0, ["EE#s"])
-            ts(T.CT[:, 0, 0:1], PK, -2.0 ** 21, None, A.mult, None, ["PF"], ["CT#i0"])
-            ts(T.CT[:, 1, 0:1], PK, 16.0, -2.0 ** 21, A.add, A.mult, ["PF"], ["CT#i1"])
-            ts(T.T31[:, 0:1], PK, -1.0, 31.0, A.mult, A.add, ["PF"], ["T31#0"])
-            ts(T.T31[:, 1:2], PK, -1.0, 15.0, A.mult, A.add, ["PF"], ["T31#1"])
-            ms(T.STEP[:], 1.0, ["STEP"])
-            ms(T.ONE32[:], 1.0, ["ONE32"])
-            ms(T.STEP[:, 0:64:32], -1e4, ["STEP"])
-        else:
+        ts(T.SO[:, 0:16], T.PS[:, 16:32], 40.0 - 2048.0, 1e4, A.is_lt, A.mult, ["PS"], ["SO#0"])
+        if t > 0:
             ts(T.AI[:, 0:1], T.PA[:, 256:257], 0.5, 1024.0, A.mult, A.add, ["PA"], ["AI#0"])
+        tt(T.SO[:, 16:32], T.PS[:, 0:16], T.SO[:, 0:16], A.add, ["PS", "SO#0"], ["SO#1"])
+        if t > 0:
             ts(T.AI[:, 1:2], T.AI[:, 0:1], 3, None, A.bitwise_and, None, ["AI#0"], ["AI#1"])
+        tt(T.SO[:, 32:48], T.SO[:, 16:32], T.DUL[:], A.min, ["SO#1", "DUL"], ["SO#2"])
+        if t > 0:
             ts(T.BIAS[:, 0:1], T.AI[:, 1:2], -1.0, T.BIAS[:, 3 + t:4 + t], A.mult, A.add, ["AI#1", "BIAS#4"],
                ["BIAS#0"])
-        ts(T.SO[:, 0:16], T.PS[:, 16:32], 40.0 - 2048.0, 1e4, A.is_lt, A.mult, ["PS"], ["SO#0"])
-        tt(T.SO[:, 16:32], T.PS[:, 0:16], T.SO[:, 0:16], A.add, ["PS", "SO#0"], ["SO#1"])
-        tt(T.SO[:, 32:48], T.SO[:, 16:32], T.DUM[:, 32:48], A.min, ["SO#1", "DUM"], ["SO#2"])
         ts(T.SOF[:], T.SO[:, 32:48], 2048.0, None, A.add, None, ["SO#2"], ["SOF"])
-        act(T.XC[:], XR[1 - a][:].indirect(T.SOF[:]), AF.Copy, [XK[1 - a], XLK[1 - a], "SOF"], ["XC"])
         if t > 0:
-            tt(T.QY[:], xl(1 - a), T.QQ[:], A.max, [XLK[a], "QQ"], ["QY"])
-            if t == 1:
-                tt(xl(0), T.QY[:], lanes(T.XR0, 0), A.min, ["QY", "XR0"], ["XL1"])
-                xtrans(2, 0, T.PB, "PB")
-            else:
-                tt(T.YX[:, 1:512:2], T.QY[:], lanes(T.XR1, 1), A.min, ["QY", "XR1"], ["YX#b"])
-        tt(T.SI[:], T.XC[:], xl(a), A.add, ["XC", XLK[1 - a]], ["SI"])
-        ts(T.SJ[:], T.SI[:], 1, None, A.arith_shift_right, None, ["SI"], ["SJ"])
-        cp(T.SM[:], T.SJ[:], ["SJ"], ["SM"])
-        if t == 0:
-            cp(T.MF[:, 0:1024], T.MW[:, 0:1024], ["MW"], ["MF#0"])
+            tt(T.TC[:, 0:16], T.RR[:, 15:256:16], T.DL[:, :, 0:2], A.mult, ["RR", "DL"], ["TC#0"])
+            tt(T.TC[:, 16:32], T.TC[:, 0:16], T.VP[:, :, 0:2], A.add, ["TC#0", "VP"], ["TC#1"])
+            cp(T.O2C[:], T.TC[:, 16:32], ["TC#1"], ["O2C"])
 
         win, R = mwin(t)
-        tt(T.EV[:], win.indirect(LC[:, 0:16]), T.VC[:], A.is_equal, R + ["LC", "VC"], ["EV"])
-        act(T.NF[:], T.IOT[:, 0:512].indirect(LC[:, 16:32]), AF.Identity, ["IOT#0", "LC", "BIAS#0"], ["NF"],
+        tt(T.EV[:], win.indirect(lc), T.VC[:, t, :], A.is_equal, R + ["LC", "VC%d" % t], ["EV"])
+        act(T.NF[:], T.IOT[:, 0:512].indirect(ln), AF.Identity, ["IOT", "LC", "BIAS#0"], ["NF"],
             bias=T.BIAS[:, 0:1])
-        mm(T.PA[:, 0:256], T.ID[:], T.NF[:], True, False, ["ID", "NF"], ["PA"])
-        mm(T.PA[:, 0:256], T.BLK[:], T.EV[:], False, True, ["BLK", "EV"], ["PA"])
-        tt(T.EE[:, 0:256], T.IOT[:, 0:W].indirect(LC[:, 0:16]), T.EC[:], A.add, ["IOT", "LC", "EC"], ["EE#e"])
-        ts(T.S2[:], T.PA[:, 0:256], 0.0, 2.0 ** 21, A.is_ge, A.mult, ["PA"], ["S2"])
+        mms("PA", lo, [("BLK", T.EV[:], ["EV"]), ("ID", T.NF[:], ["NF"])])
+        tt(T.EE[:, 0, 0:256], T.IOT[:, 0:W].indirect(lc), T.EC[:], A.add, ["IOT", "LC", "EC"], ["EE#e"])
+        act(T.EE[:, 1, 0:257], T.EE[:, 0, 0:257], AF.Identity, ["EE#e", "EE#s"], ["EE#f"], bias=16.0 * STEPC)
+        ts(T.S2[:], T.PA[:, lo], 0.0, 1.0 * STEPC, A.is_ge, A.mult, ["PA"], ["S2"])
+        scan(T.CT[:, 1:257], T.ZERO[:], T.S2[:], T.CT[:, 0:1], A.add, A.add, ["ZERO", "S2", "CT#i"], ["CT#0"])
         for c in range(2):
-            scan(T.CT[:, c, 1:257], T.ZERO[:], T.S2[:], T.CT[:, c, 0:1], A.add, A.add,
-                 ["ZERO", "S2", "CT#i%d" % c], ["CT#%d" % c])
-        for c in range(2):
-            scan(T.SC[:, c, 0:257], T.CT[:, c, 0:257], T.EE[:, 0:257], 0.0, A.min, A.max,
-                 ["CT#%d" % c, "CT#i%d" % c, "EE"], ["SC#%d" % c])
-        cp(T.EI[:, 0:2], T.SC[:, :, 256], ["SC"], ["EI#0"])
+            scan(T.SC[:, c, 0:257], T.CT[:, 0:257], T.EE[:, c, 0:257], 0.0, A.min, A.max,
+                 ["CT", "EE#s", "EE#" + "ef"[c]], ["SC#%d" % c])
+        tt(T.EI[:, 0:2], T.SC[:, :, 256], T.OFS[:], A.add, ["SC", "OFS"], ["EI#0"])
         ts(T.EI[:, 2:4], T.EI[:, 0:2], 4095, None, A.bitwise_and, None, ["EI#0"], ["EI#1"])
         ts(T.EI[:, 4:6], T.EI[:, 0:2], 12, None, A.arith_shift_right, None, ["EI#0"], ["EI#2"])
         cp(T.C16[:], T.EI[:, 2:4], ["EI#1"], ["C16"])
-        cp(T.CV4[:, 0:2], T.EI[:, 2:4], ["EI#1"], ["CV4#c"])
-        ts(T.CV4[:, 4:6], T.EI[:, 4:6], 1e4, -5e3, A.mult, A.add, ["EI#2"], ["CV4#t"])
+        cp(T.CVF[:, 0:2], T.EI[:, 2:4], ["EI#1"], ["CVF#c"])
+        ts(T.NE[:, 0:35:34], T.EI[:, 0:2], 4096.0, B2, A.is_lt, A.mult, ["EI#0"], ["NE#e"])
         for c in range(2):
-            ts(T.NE[:, 32 * c:32 * c + 32], T.IOT[:, 0:W].indirect(T.C16[:]), T.CV4[:, c:c + 1], -1000.0,
-               A.not_equal, A.mult, ["IOT", "C16", "CV4#c"], ["NE#%d" % c])
-        tt(T.CV4[:, 6:8], T.CV4[:, 4:6], T.T31[:], A.min, ["CV4#t", "T31"], ["CV4#u"])
-        ts(T.CV4[:, 2:4], T.EI[:, 4:6], -16.0, float(W + 8 * a + rho), A.mult, A.add, ["EI#2"], ["CV4#v"])
-        scan(T.NE[:, 64:128], T.STEP[:], T.NE[:, 0:64], 0.0, A.add, A.max, ["STEP", "NE#0", "NE#1"], ["NE#s"])
-        tt(T.CV4[:, 8:10], T.NE[:, 95:128:32], T.CV4[:, 6:8], A.is_gt, ["NE#s", "CV4#u"], ["CV4#b"])
-        tt(T.CV4[:, 12:14], T.CV4[:, 8:10], T.DUM[:, 16 + 2 * rho:18 + 2 * rho], A.mult, ["CV4#b", "DUM"], ["CV4#x"])
-        tt(T.CV4[:, 14:16], T.CV4[:, 8:10], T.DUM[:, 2 * rho:2 * rho + 2], A.mult, ["CV4#b", "DUM"], ["CV4#y"])
-        tt(T.CV4[:, 16:20], T.CV4[:, 0:4], T.CV4[:, 12:16], A.max, ["CV4#c", "CV4#v", "CV4#x", "CV4#y"], ["CV4#z"])
-        cp(ALL[:, rho, 0:4], T.CV4[:, 16:20], ["CV4#z"], ["ALL#o"])
+            ts(T.NE[:, 1 + 34 * c:33 + 34 * c], T.IOT[:, 0:W].indirect(T.C16[:]), T.CVF[:, c:c + 1], B2,
+               A.is_equal, A.mult, ["IOT", "C16", "CVF#c"], ["NE#%d" % c])
+        ts(T.CVF[:, 2:4], T.EI[:, 4:6], -16.0, float(W + 8 * a + rho), A.mult, A.add, ["EI#2"], ["CVF#v"])
+        scan(T.NS[:, 0:67], T.NE[:, 0:67], T.STEP[:, 0:67], 0.0, A.max, A.add, ["STEP", "NE"], ["NS"])
+        for c in range(2):
+            ts(ALL[:, rho, c:4:2], T.CVF[:, c:4:2], T.NS[:, 32 + 34 * c:33 + 34 * c], T.DUM[:, rho, c:c + 1],
+               A.max, A.min, ["CVF", "NS", "DUM"], ["ALL#o%d" % c])
         others = [cores[(r + i) % N] for i in range(1, N)]
-        send(ALL[:, rho, 0:4], [(c, ALL[:, rho, 0:4]) for c in others], "aa%d" % t, ["ALL#o"])
+        send(ALL[:, rho, 0:4], [(c, ALL[:, rho, 0:4]) for c in others], "aa%d" % t, ["ALL#o0", "ALL#o1"])
         lands("aa%d" % t, sum(share(c, [d for d in cores if d != c]) for c in others), ["ALL#r"])
 
-        if t == 0:
-            iota(T.FT[:, 2304:WD], [[1, 2304]], 256, 0, ["FT#b"])
-            ms(T.MF[:, W:WD], 0.0, ["MFd"])
-            for b in range(1, 4):
-                cp(T.MF[:, 1024 * b:1024 * b + 1024], T.MW[:, 1024 * b:1024 * b + 1024], ["MW"], ["MF#%d" % b])
-            cp(T.OLD[:], lanes(T.MW, 1), ["MW"], ["OLD"])
-            cp(lanes(T.XR0, 0), T.SM[:], ["SM"], ["XR0"])
-            act(T.OWN[:], T.IOT[:], AF.Copy, ["IOT"], ["OWN"], scale=0.0)
-            act(T.VT[:], T.VT[:], AF.Identity, ["VT"], ["VT"], bias=8.0)
-        else:
-            cp(T.C1[:], T.OFF[:], ["OFF"], ["C1"])
-            tt(T.S2[:], lanes(T.MF, a), T.C1[:], A.subtract, ["MF", "C1"], ["S2"])
-            if t == 1:
-                act(lanes(T.MF, a), T.C1[:], AF.Copy, ["C1"], ["MF"])
-                act(T.VT[:], T.VT[:], AF.Identity, ["VT"], ["VT"], bias=-8.0)
-                cp(T.OLD[:], lanes(T.MW, 0), ["MW"], ["OLD"])
-                cp(lanes(T.XR1, 1), T.SM[:], ["SM"], ["XR1"])
-                cp(T.XR1[:, 0:WD].indirect(T.O20[:, 16:32]), T.BIGS[:], ["O20", "BIGS"], ["XR1"])
-            tt(T.S3[:], T.S2[:], T.PVN[:], A.mult, ["PVN", "S2"], ["S3"])
-            tt(T.YM[:, a:512:2], T.S3[:], T.C1[:], A.add, ["S3", "C1"], ["YM#%d" % a])
-            if t == 1:
-                cp(T.PI[:].indirect(T.O20[:]), T.PV0[:], ["O20", "PV0"], ["PI"])
-            else:
-                dma("y", "out", lambda: g.sync.dma_start(T.ym[:], T.YM[:]), ["YM"], [])
-                tt(T.C2[:], xl(0), T.SM[:], A.subtract, ["XL1", "SM"], ["C2"])
-                cp(T.PI[:].indirect(T.O21[:]), T.PV1[:], ["O21", "PV1"], ["PI"])
+        if t > 0:
+            SMo, so, xo = T["SM%d" % (t - 1)], "SM%d" % (t - 1), lanes(XR[1 - a], 1 - a)
+            mms("D1", lo, [("ID", xl(1 - a), [XLK[a]]), ("ID", xo, [XK[1 - a]]), ("NID", T.BIGS[:], ["BIGS"])])
+            mms("D1", hi, [("ID", SMo[:], [so]), ("ID", SMo[:], [so]), ("NID", xo, [XK[1 - a]])])
+            o16 = "O16%d" % a
+            mms("D3", lo, [("ID16", T[o16][:], [o16]), ("NID16", T.M16[:], ["M16"]), ("ID8K", T.PVN[:], ["PVN"])])
+        act(T.XC[:], XR[1 - a][:].indirect(T.SOF[:]), AF.Copy, [XK[1 - a], XLK[1 - a], "SOF"], ["XC"])
+        mms("D0", lo, [("ID", xl(a), [XLK[1 - a]]), ("ID", T.XC[:], ["XC"])])
+        if t > 0:
+            act(T.UU[:], T.D1[:], AF.Relu, ["D1"], ["UU"])
+            act(T.RY[:], T.D3[:, lo], AF.Relu, ["D3"], ["RY"], bias=-4096.0)
+            mms("D2", lo, [("ID", T.UU[:, lo], ["UU"]), ("ID", T.UU[:, hi], ["UU"])])
+            mms("D4", lo, [("ID16", T.M16[:], ["M16"]), ("NID4K", T.PVN[:], ["PVN"]), ("ID32", T.RY[:], ["RY"])])
+        act(T.T1[:], T.D0[:, lo], AF.Identity, ["D0"], ["T1"], bias=RND, scale=0.5 - 2.0 ** -13)
         if t < 2:
+            act(lanes(XR[a], a), T.T1[:], AF.Identity, ["T1"], [XK[a]], bias=-RND)
+            act(T["SM%d" % t][:], T.T1[:], AF.Identity, ["T1"], ["SM%d" % t], bias=-RND)
+        else:
+            act(T.YX[:, 0:512:2], T.T1[:], AF.Identity, ["T1"], ["YX#a"], bias=-RND)
+        if t == 0:
+            act(xl(1), lanes(T.XR1, 1), AF.Copy, ["XR1"], ["XL0"])
+            xtrans(1, raw(1), ["XR1"], "D1")
+            xtrans(2, [T.SM0[:, 0:128], T.SM0[:, 128:256]], ["SM0"], "D2")
+        if t == 1:
+            mms("D3", lo, [("ID16", T.M16[:], ["M16"])])
+            act(lanes(T.MF, 1), T.D3[:, lo], AF.Identity, ["D3"], ["MF"], bias=2048.0)
+            act(xl(0), T.D2[:, lo], AF.Copy, ["D2"], ["XL1"])
+        if t == 2:
+            act(T.YX[:, 1:512:2], T.D2[:, lo], AF.Copy, ["D2"], ["YX#b"])
+        if t > 0:
+            act(T.YM[:, a:512:2], T.D4[:, lo], AF.Identity, ["D4"], ["YM#%d" % a], bias=2048.0)
+        if t == 2:
+            dma("y", "out", lambda: g.sync.dma_start(T.ym[:], T.YM[:]), ["YM"], [])
+        if t < 2:
+            act(T.PB[:, hi], T.VB[:], AF.Identity, ["VB"], ["PB"], bias=8.0 * (1 - a) + FO)
             for j in range(5):
                 pre(t + 1, j)
 
+        if t == 0:
+            mfloat(3)
+            cp(T.OLD1[:], lanes(T.MW, 1), ["MW"], ["OLD1"])
+            ts(T.O161[:], lanes(T.MW, 1), -2048.0, None, A.add, None, ["MW"], ["O161"])
+            for b in range(4):
+                iota(T.MW[:, 1024 * b:1024 * b + 1024], [[16, 64], [0, 16]], 1024 * b + 8 + r, 0, ["MW#%d" % b], False)
+            iota(T.PI[:], [[0, WD]], -1, 0, ["PI"])
+        else:
+            cp(T.PI[:].indirect(T.O2V[:]), T.PV[:, lo], ["O2V", "PV"], ["PI"])
+            cp(T.PI[:].indirect(T.O2C[:]), T.PV[:, hi], ["O2C", "PV"], ["PI"])
+            if t == 1:
+                cp(T.XR1[:, 0:WD].indirect(T.O2C[:]), T.BIGS[:], ["O2C", "BIGS"], ["XR1"])
+
+        own, ok = (T.FT, "FT") if t < 2 else (T.PI, "PI")
+        src, sk = (T.MF, ["MF", "MFd"]) if t < 2 else (T.IOT, ["IOT"])
         cp(T.CVL[:, 0:16], ALL[:, :, 0:2], ["ALL"], ["CVL#c"])
         cp(T.CVL[:, 16:32], ALL[:, :, 2:4], ["ALL"], ["CVL#v"])
         if t < 2:
-            act(T.VAL[:], T.MF[:].indirect(T.CVL[:]), AF.Identity, ["MF", "MFd", "CVL"], ["VAL"], bias=-2047.9375)
-            act(T.C3[:], T.VB[:], AF.Identity, ["VB"], ["C3"], bias=8.0 * (1 - a) - 2048.0)
-        act(PV[:], T.IOT[:].indirect(T.CVL[:]), AF.Copy, ["IOT", "CVL"], ["PV%d" % t])
-        if t == 0:
-            for k in range(16):
-                act(T.DK32[:, 128 * k:128 * k + 128], T.ID[:], AF.Identity, ["ID", "KM"], ["DK32#%d" % k],
-                    scale=T.KM[:, k:k + 1])
+            cp(T.VCF[:], ALL[:, :, 0:4], ["ALL"], ["VCF"])
+            tt(T.DL[:], T.DUM[:], T.VCF[:], A.subtract, ["DUM", "VCF"], ["DL"])
+            tt(T.VP[:], T.DUM2[:], T.VCF[:], A.subtract, ["DUM2", "VCF"], ["VP"])
+        else:
+            ts(T.OI[:], ALL[:, r, 2:4], 1 / 16.0, 255.0, A.mult, A.min, ["ALL"], ["OI"])
+            ts(T.TY[:], ALL[:, r, 2:4], 0.125, -r / 8.0, A.mult, A.add, ["ALL"], ["TY"])
+            for c in range(2):
+                ts(T.OY[:, c:c + 1], ALL[:, r, 2 + c:3 + c], 512.0 - W, T.TY[:, c:c + 1], A.add, A.max,
+                   ["ALL", "TY"], ["OY#%d" % c])
         for p in range(N - 1, -1, -1):
-            cp(T.OWN[:].indirect(ALL[:, p, 0:2]), T.NSL[:, 32 * p:32 * p + 32], ["ALL", "NSL"], ["OWN"])
-            if p == N - 1:
-                cp(T.VCF[:, 0:16], ALL[:, :, 2:4], ["ALL"], ["VCF#v"])
-            if p == N - 2:
-                cp(T.VCF[:, 16:32], ALL[:, :, 0:2], ["ALL"], ["VCF#c"])
-        tt(T.S1[:], T.OWN[:].indirect(T.CVL[:, 0:16]), T.DIAG[:], A.add, ["OWN", "CVL#c", "DIAG"], ["S1"])
-        scan(T.S2[:], T.RST[:], T.S1[:], 0.0, A.add, A.max, ["RST", "S1"], ["S2"])
-        tt(T.VCF[:, 32:48], T.VCF[:, 0:16], T.S2[:, 15:256:16], A.max, ["VCF#v", "S2"], ["VCF#a"])
-        tt(T.VCF[:, 48:64], T.VCF[:, 16:32], T.S2[:, 15:256:16], A.max, ["VCF#c", "S2"], ["VCF#b"])
-        tt(T.VCF[:, 64:96], T.VCF[:, 32:64], T.DUM[:, 0:32], A.min, ["VCF#a", "VCF#b", "DUM"], ["VCF#2"])
-        ok = "O2%d" % t
-        cp(O2[:], T.VCF[:, 64:96], ["VCF#2"], [ok])
+            c = slice(32 * p, 32 * p + 32)
+            act(T.VALV[:, c], src[:].indirect(ALL[:, p, 2:4]), AF.Identity, sk + ["ALL"], ["VALV#%d" % p],
+                bias=FO + (p + 1) / 128.0 if t < 2 else 0.0)
+            cp(own[:].indirect(ALL[:, p, 0:2]), T.VALV[:, c], ["ALL", "VALV#%d" % p], [ok])
+        act(T.VALC[:], src[:].indirect(T.CVL[:, 0:16]), AF.Identity, sk + ["CVL#c"], ["VALC"],
+            bias=FO + 1 / 16.0 if t < 2 else 0.0)
         if t == 2:
-            cp(T.PI[:].indirect(O2[:]), PV[:], [ok, "PV2"], ["PI"])
+            act(T.OX[:, 0:32], xl(0).indirect(T.OI[:]), AF.Copy, ["XL1", "OI"], ["OX#0"])
+            act(T.OX[:, 32:64], T.YX[:].indirect(T.OY[:]), AF.Copy, ["YX", "OY"], ["OX#1"])
+            act(T.D0[:, lo], T.VALC[:], AF.Identity, ["VALC"], ["D0"], bias=1.0)
+            tt(T.OX[:, 64:96], T.OX[:, 32:64], T.OX[:, 0:32], A.subtract, ["OX#0", "OX#1"], ["OX#2"])
+        tt(T.S1[:], own[:].indirect(T.CVL[:, 0:16]), T.VALV[:], A.not_equal, [ok, "CVL#c", "VALV"], ["S1"])
+        if t == 2:
+            tt(T.OX[:, 96:128], T.S1[:, 32 * r:32 * r + 32], T.OX[:, 64:96], A.mult, ["S1", "OX#2"], ["OX#3"])
+            tt(T.S2[:], T.S1[:], T.D0[:, lo], A.mult, ["S1", "D0"], ["S2"])
+            tt(T.YX[:].indirect(T.OY[:]), T.OX[:, 0:32], T.OX[:, 96:128], A.add, ["OY", "OX"], ["YX"])
+            dma("s", "out", lambda: g.scalar.dma_start(T.yx[:], T.YX[:, 0:512]), ["YX"], [])
+            tt(T.PI[:].indirect(T.CVL[:, 16:32]), T.VALC[:], T.S2[:], A.subtract, ["CVL#v", "VALC", "S2"], ["PI"])
             dma("y", "out", lambda: g.sync.dma_start(T.yp[:], T.PI[0:128:16, 0:W]), ["PI"], [])
-            ts(T.S1[:], lanes(T.PI, 0), 0.0, None, A.is_ge, None, ["PI"], ["S1"])
-            tt(T.S3[:], T.S1[:], T.C2[:], A.mult, ["S1", "C2"], ["S3"])
-            tt(T.YX[:, 0:512:2], T.S3[:], T.SM[:], A.add, ["S3", "SM"], ["YX#a"])
-            dma("s", "out", lambda: g.scalar.dma_start(T.yx[:], T.YX[:]), ["YX"], [])
             break
-        cp(T.FT[:].indirect(O2[:]), T.VAL[:], [ok, "VAL"], ["FT"])
-        op("s", lambda: S.activation(T.WON[:], T.VCF[:, 64:80], AF.Sign, bias=T.BIAS[:, 10:11], scale=-1.0,
-                                     accum_out=T.AC[:, 0:1]), ["VCF#2", "BIAS#10"], ["WON", "AC"])
+        scan(T.RR[:], T.S1[:], T.SCN[:], 0.0, A.max, A.add, ["SCN", "S1"], ["RR"])
+        tt(T.TV[:, 0:16], T.RR[:, 15:256:16], T.DL[:, :, 2:4], A.mult, ["RR", "DL"], ["TV#0"])
+        tt(T.TV[:, 16:32], T.TV[:, 0:16], T.VP[:, :, 2:4], A.add, ["TV#0", "VP"], ["TV#1"])
+        cp(T.O2V[:], T.TV[:, 16:32], ["TV#1"], ["O2V"])
+        op("s", lambda: S.activation(T.FT[:].indirect(T.O2V[:]), T.VALC[:], AF.Silu), ["O2V", "VALC"], ["FT"])
+        cp(XR[a][:, 0:WD].indirect(T.O2V[:]), T.BIGS[:], ["O2V", "BIGS"], [XK[a]])
 
         u = t + 1
+        OLD, oldk = T["OLD%d" % (u % 2)], "OLD%d" % (u % 2)
 
-        def follow(q):
-            win = T.FT[:, 0:W].indirect(T.OLD[:, 64 * q:64 * q + 64])
-            if q == 1:
-                act(T.G32[:], win, AF.Copy, ["FT", "OLD"], ["G16#1"])
+        def follow(j0, j1, q="v"):
+            win = T.FT[:, 0:W].indirect(OLD[:, 32 * j0:32 * j1])
+            if q == "s":
+                act(T.G32[:, 0:512 * (j1 - j0)], win, AF.Identity, ["FT", oldk], ["G32"], bias=-2048.0 - FO)
             else:
-                cp(T.G16[:, 1024 * q:1024 * q + 1024], win, ["FT", "OLD"], ["G16#%d" % q])
+                ts(T.G16[:, 512 * j0:512 * j1], win, -2048.0 - FO, None, A.add, None, ["FT", oldk], ks("G16", j0, j1))
 
-        def keep(q):
-            bank, bk = (T.PA, "PA") if q % 2 == 0 else (T.PB, "PB")
-            for k in range(16):
-                if q == 1:
-                    mm(bank[:, 0:64], T.DK32[:, 128 * k:128 * k + 128], T.G32[:, k:1024:16], k == 0, k == 15,
-                       ["DK32", "G16#1"], [bk])
+        def keep(j0, j1, bk, q="v", k0=0, k1=16):
+            for k in range(k0, k1):
+                out = T[bk][:, 0:32 * (j1 - j0)]
+                if q == "s":
+                    mm(out, T.DK32[:, 128 * k:128 * k + 128], T.G32[:, k:512 * (j1 - j0):16], k == 0, k == 15,
+                       ["DK32", "G32"], [bk])
                 else:
-                    mm(bank[:, 0:64], T.DK16[:, 128 * k:128 * k + 128], T.G16[:, 1024 * q + k:1024 * q + 1024:16],
-                       k == 0, k == 15, ["DK16", "G16#%d" % q], [bk])
+                    mm(out, T.DK16[:, 128 * k:128 * k + 128], T.G16[:, 512 * j0 + k:512 * j1:16],
+                       k == 0, k == 15, ["DK16"] + ks("G16", j0, j1), [bk])
 
-        def offs(q):
-            bank, bk = (T.PA, "PA") if q % 2 == 0 else (T.PB, "PB")
-            ts(T.OFF[:, 64 * q:64 * q + 64], bank[:, 0:64], 2048.0, None, A.add, None, [bk], ["OFF#%d" % q])
+        def offs(j0, j1, bk):
+            ts(T.OFF[:, 32 * j0:32 * j1], T[bk][:, 0:32 * (j1 - j0)], 2048.0, None, A.add, None, [bk],
+               ks("OFF", j0, j1))
 
-        follow(0)
-        follow(1)
-        keep(0)
-        cp(XR[a][:, 0:WD].indirect(O2[:, 0:16]), T.BIGS[:], [ok, "BIGS"], [XK[a]])
-        offs(0)
-        keep(1)
-        gx(u, 0)
-        gx(u, 1)
-        follow(2)
-        offs(1)
-        dmm(u, 0)
+        def x(j):
+            gx(u, j)
+            dmm(u, j)
+
+        def won():
+            op("s", lambda: S.activation(T.WON[:], T.TV[:, 16:32], AF.Sign, bias=T.BIAS[:, 10:11], scale=-1.0,
+                                         accum_out=T.AC[:, 0:1]), ["TV#1", "BIAS#10"], ["WON", "AC"])
+
+        def pvn():
+            tt(T.PVN[:], lanes(T.FT, u % 2), T.PB[:, hi], A.not_equal, ["FT", "PB"], ["PVN"])
+
+        def m16():
+            ts(T.M16[:], T.OFF[:], -2048.0, None, A.add, None, ["OFF"], ["M16"])
+
+        def count():
+            names(u)
+            mm(T.PA[:, 256:257], T.ONE32[:], T.AC[:, 0:1], True, True, ["ONE32", "AC"], ["PA"])
+
+        follow(0, 2)
+        won()
+        keep(0, 2, "PA")
+        pvn()
+        follow(2, 3)
+        offs(0, 2, "PA")
+        follow(3, 4)
+        x(0)
+        keep(2, 4, "PB")
+        x(1)
+        follow(4, 5)
+        offs(2, 4, "PB")
         ab(0)
-        dmm(u, 1)
-        keep(2)
-        gx(u, 2)
+        follow(5, 6)
         ab(1)
-        eq(u, 0)
-        offs(2)
-        follow(3)
-        dmm(u, 2)
-        gx(u, 3)
+        keep(4, 6, "PA")
+        x(2)
+        follow(6, 8)
+        offs(4, 6, "PA")
+        x(3)
         ab(2)
-        dmm(u, 3)
-        keep(3)
-        gx(u, 4)
-        ab(3)
-        pvn(u)
-        offs(3)
+        keep(6, 8, "PB")
+        eq(u, 0, 2)
+        offs(6, 8, "PB")
         m16()
-        dmm(u, 4)
-        gx(u, 5)
+        x(4)
+        ab(3)
+        pen(u, 0)
+        pen(u, 1)
+        eq(u, 2, 4)
+        score(0, False, False)
+        x(5)
         ab(4)
-        dmm(u, 5)
-        eq(u, 1)
-        pen(0)
-        score(0, False)
-        gx(u, 6)
+        count()
+        x(6)
         ab(5)
-        dmm(u, 6)
-        names()
-        mm(T.PA[:, 256:257], T.ONE32[:], T.AC[:, 0:1], True, True, ["ONE32", "AC"], ["PA"])
-        score(0, True)
-        gx(u, 7)
+        eq(u, 4, 6)
+        x(7)
         ab(6)
-        dmm(u, 7)
+        score(0, True, True)
+        eq(u, 6, 8)
         ab(7)
-        eq(u, 2)
-        eq(u, 3)
-        pen(1)
-        score(1, False)
-        score(1, True)
-        act(T.QQ[:], lanes(XR[a], a), AF.Relu, [XK[a], "BIAS#9"], ["QQ"], bias=T.BIAS[:, 9:10], scale=-1.0)
+        best(0)
+        score(1, False, False)
+        score(1, True, True)
+        act(T.PV[:], T.IOT[:].indirect(T.CVL[:]), AF.Copy, ["IOT", "CVL"], ["PV"])
         if u == 1:
-            iota(T.PI[:], [[0, WD]], -1, 0, ["PI"])
+            for j in range(8):
+                act(T.XR1[:, j:W:16], T.BIGS[:], AF.Copy, ["BIGS"], ["XR1"] if j == 0 else ["XR1#%d" % j])
 
     for s, v in total.items():
         wait("g", s, v)

@@ -17,15 +17,16 @@ def sb(cols, dtype):
 
 
 SCRATCH = {
-    "MW": sb(W, I32), "MF": sb(WD, F32), "FT": sb(WD, F32), "IOT": sb(WD, F32), "PI": sb(WD, F32), "VT": sb(W, F32),
-    "XR0": sb(WX, BF), "XR1": sb(WX, BF), "G16": sb(W, F16), "G32": sb(1024, F32),
+    "MW": sb(W, I32), "MF": sb(WD, F32),
+    "FT": sb(WD, F32), "IOT": sb(WD, F32), "PI": sb(WD, F32), "VT": sb(W, F32),
+    "XR0": sb(WX, BF), "XR1": sb(WX, BF), "G16": sb(2048, F16), "G32": sb(2048, F32),
     "EQ": sb(W, BF), "GX": sb(W, BF), "AB": sb(W, BF),
-    "REP": sb(2048, BF), "DK16": sb(2048, F16), "DK32": sb(2048, F32),
-    "OFF": sb(256, U16), "M16": sb(256, F16), "OLD0": sb(256, U16), "OLD1": sb(256, U16),
+    "REP": sb(2048, BF), "DK16": sb(2048, F16), "KB": sb(128, F32), "XRP": sb(1024, BF),
+    "OFF": sb(256, U16), "M16": sb(256, F16), "OLD0": sb(256, U16), "OLD1": sb(128, U16), "OLDT": sb([2, 128], U16),
     "O160": sb(256, F16), "O161": sb(256, F16), "CLS": sb(256, I32), "NCL": sb(256, BF),
     "XT": sb([3, 256], BF),
     "SM0": sb(256, BF), "SM1": sb(256, BF), "XC": sb(256, BF), "T1": sb(256, F32), "UU": sb(512, BF), "RY": sb(256, F32),
-    "YX": sb(768, BF), "YM": sb(512, F32), "OX": sb(128, BF), "OI": sb(2, U16), "OY": sb(2, U16), "TY": sb(2, F32),
+    "YX": sb(768, BF), "YM": sb(512, F32), "OX": sb(128, BF), "OI": sb(4, U16),
     "VALV": sb(256, F32), "VALC": sb(256, F32), "PV": sb(512, F32),
     "ID": sb(128, BF), "NID": sb(128, BF), "ID8K": sb(128, BF), "NID4K": sb(128, BF),
     "ID16": sb(128, F16), "NID16": sb(128, F16), "ID32": sb(128, F32),
@@ -34,25 +35,25 @@ SCRATCH = {
     "KC": sb(128, BF), "QW": sb(240, F16),
     "B8": sb(8, F32), "B8E": sb(8, BF), "B8A": sb(8, BF),
     "KM": sb(16, F32), "PIDX": sb(4, I32), "PF": sb(4, F32),
-    "C2": sb(256, F32), "C4": sb(128, F32), "C5": sb(128, F32), "C6": sb([8, 4], F32), "C7": sb(16, F32),
-    "VB": sb(256, F32), "VC": sb([3, 256], F32),
+    "C2": sb(256, F32), "C4": sb(128, F32), "C5": sb(128, F32), "C6": sb([8, 4], F32), "L16": sb(128, F16),
+    "VB": sb(256, F32), "VC": sb([2, 256], BF),
     "RST": sb(128, F32), "ZERO": sb(256, F32), "SCN": sb(256, F32), "EC": sb(256, F32), "BIGS": sb(256, BF),
     "DUM": sb([8, 4], F32), "DUM2": sb([8, 4], F32), "DUL": sb(16, F32), "STEP": sb(68, F32), "OFS": sb(2, F32),
-    "THR": sb(8, I32), "THB": sb(8, I32), "TH8": sb(8, F32), "THC": sb(4, F32), "LT": sb(12, F32), "BIAS": sb(16, F32),
+    "THR": sb(8, I32), "THB": sb(8, I32), "THC": sb(4, F32), "BIAS": sb(16, F32),
     "PVN": sb(256, BF), "S1": sb(256, F32), "S2": sb(256, F32), "S3": sb(256, F32), "RR": sb(256, F32),
-    "CI": sb(16, I32), "CN": sb(32, I32), "RX": sb([4, 8, 8], F16),
-    "MSG": sb([3, 32], U16), "LC": sb([3, 32], U16),
+    "CI": sb(32, I32), "CN": sb(48, I32), "RX": sb([6, 8, 8], F16), "MSG": sb(48, U16),
+    "TBL": sb([3, 2048], BF), "TBS": sb([2, 2048], BF),
     "ALL0": sb([8, 8], U16), "ALL1": sb([8, 8], U16), "ALL2": sb([8, 8], U16),
     "EV": sb(256, BF), "NF": sb(256, BF), "EE": sb([2, 260], F32), "CT": sb(260, F32), "SC": sb([2, 260], F32),
     "EI": sb(8, I32), "C16": sb(2, U16), "CVF": sb(4, F32), "NE": sb(68, F32), "NS": sb(68, F32),
     "CVL": sb(32, U16), "VCF": sb([8, 4], F32), "DL": sb([8, 4], F32), "VP": sb([8, 4], F32),
-    "TV": sb(32, F32), "TC": sb(32, F32), "O2V": sb(16, U16), "O2C": sb(16, U16),
-    "WON": sb(16, F32), "AC": sb(4, F32), "AI": sb(4, I32), "SO": sb(48, F32), "SOF": sb(16, U16),
+    "TV": sb(32, F32), "TC": sb(48, F32), "O2V": sb(16, U16), "O2C": sb(16, U16),
+    "AC": sb(4, F32), "AI": sb(4, I32), "SO": sb(48, F32), "SOF": sb(16, U16),
 }
 PSUM = ("D0", "D1", "D2", "D3", "D4", "PS", "PA", "PB")
 SCRATCH.update({n: ("psum", [128, 512], F32) for n in PSUM})
-SEMAPHORES = ["qv", "qs", "qp", "qg", "lx", "lm0", "lm1", "lm2", "lm3", "lth", "out", "sent", "ath",
-              "ac0", "ac1", "ac2", "aa0", "aa1", "aa2"]
+SEMAPHORES = ["qv", "qs", "qp", "qg", "lx", "lm0", "lm1", "lm2", "lm3", "lth", "out", "sent",
+              "aa0", "aa1", "aa2", "at0", "at1", "at2", "left"]
 
 
 def bits(m):
@@ -70,7 +71,10 @@ def spread(topo, src, dsts):
             used &= topo.mask(src, d)
         res.append((used, far))
     if near:
-        res.append((topo.mask(src, near[0]) & ~used, near))
+        rest = [e for e in topo.engines(src, near[0]) if not used >> e & 1]
+        if far:
+            rest = rest[0:4:2]
+        res.append((sum(1 << e for e in rest), near))
     return res
 
 
@@ -182,7 +186,7 @@ def rank_program(g, core, T, topo):
         else:
             op("g", lambda: g.iota(out, pat, base, cm), [], Wr)
 
-    def send(src, pairs, sem, R):
+    def send(src, pairs, sem, R, gone="sent"):
         order("g", R, [])
         where = dict(pairs)
         trs = []
@@ -190,8 +194,8 @@ def rank_program(g, core, T, topo):
             ids = [DstId(rid=topo.addr(d)[0], pnc=topo.addr(d)[1]) for d in ds]
             trs.append(RemoteDMATransfer(dst_ids=ids, dma_engine_mask=m, remote_sem=T.sem[sem], srcs=[src],
                                          dsts=[where[d] for d in ds]))
-            total["sent"] = total.get("sent", 0) + bits(m)
-        g.remote_dma_fused(trs, local_sem=T.sem.sent)
+            total[gone] = total.get(gone, 0) + bits(m)
+        g.remote_dma_fused(trs, local_sem=T.sem[gone])
 
     def share(src, dsts):
         for m, ds in spread(topo, src, dsts):
@@ -208,6 +212,7 @@ def rank_program(g, core, T, topo):
     voters = [(r + 1 + t % (N - 1)) % N for t in range(3)]
     clients = [(r - 1 - t % (N - 1)) % N for t in range(3)]
     lo, hi = slice(0, 256), slice(256, 512)
+    XV = (1, 7)
 
     def ks(name, j0, j1):
         return ["%s#%d" % (name, j) for j in range(j0, j1)]
@@ -226,9 +231,30 @@ def rank_program(g, core, T, topo):
     def raw(a):
         return [T.XR1[:, 2048 * h + 8 * a + r:2048 * h + 2048:16] for h in range(2)]
 
-    def pre(t, j):
-        mm(DB[j % 5][:], T.XT[:, t, 128 * (j // 4):128 * (j // 4) + 128],
-           T.REP[:, 512 * (j % 4):512 * (j % 4) + 512], True, False, ["XT%d" % t, "REP"], ["D%d" % (j % 5)])
+    def slot(t, j):
+        return j if t == 0 else len([i for i in range(j) if i not in XV])
+
+    def pre(t, j, close=False, b=None):
+        b = slot(t, j) % 5 if b is None else b
+        mm(DB[b][:], T.XT[:, t, 128 * (j // 4):128 * (j // 4) + 128],
+           T.REP[:, 512 * (j % 4):512 * (j % 4) + 512], True, close, ["XT%d" % t, "REP"], ["D%d" % b])
+
+    def minus(t, banks):
+        for i, (j, b) in enumerate(zip(XV, banks)):
+            pre(t, j, True, b)
+            act(T.XRP[:, 512 * i:512 * i + 512], DB[b][:], AF.Copy, ["D%d" % b], ["XRP#%d" % j])
+
+    def bylane(a, step):
+        if step == 0:
+            mm(T.D3[:, 0:128], T["O16%d" % a][:, 128:256], T.ID16[:], True, True, ["O16%d" % a, "ID16"], ["D3"])
+            for c in range(8):
+                ts(T.G16[:, c:1024:8], T.D3[:, 0:128], T.B8[:, c:c + 1], None, A.mult, None, ["D3", "B8"], ["RT#%d" % c])
+        elif step == 1:
+            for gg in range(8):
+                mm(T.PS[:, 0:128], T.QW[:, 112 - 16 * gg:240 - 16 * gg], T.G16[:, 128 * gg:128 * gg + 128],
+                   gg == 0, gg == 7, ["QW", "RT", "G16"], ["PS"])
+        else:
+            ts(T.OLDT[:, a, :], T.PS[:, 0:128], 2048.0, None, A.add, None, ["PS"], ["OLDT%d" % a])
 
     def names_of(t):
         return (T.OLD0, "OLD0") if t == 0 else (T.OFF, "OFF")
@@ -244,33 +270,32 @@ def rank_program(g, core, T, topo):
             act(out, win, AF.Copy, [xk, "%s#%d" % (ok, j)], ["GX#%d" % j])
 
     def dmm(t, j):
-        if j >= 5:
+        b = slot(t, j) % 5
+        if slot(t, j) >= 5:
             pre(t, j)
-        mm(DB[j % 5][:], T.ID[:], T.GX[:, 512 * j:512 * j + 512], False, True, ["ID", "GX#%d" % j], ["D%d" % (j % 5)])
+        mm(DB[b][:], T.ID[:], T.GX[:, 512 * j:512 * j + 512], False, True, ["ID", "GX#%d" % j], ["D%d" % b])
 
-    def ab(j):
-        act(T.AB[:, 512 * j:512 * j + 512], DB[j % 5][:], AF.Abs, ["D%d" % (j % 5)], ["AB#%d" % j])
-
-    def mwin(t):
-        return (T.MW[:, 0:W], ["MW"]) if t == 0 else (T.MF[:, 0:W], ["MF"])
+    def ab(j, t=1):
+        b = slot(t, j) % 5
+        act(T.AB[:, 512 * j:512 * j + 512], DB[b][:], AF.Abs, ["D%d" % b], ["AB#%d" % j])
 
     def eq(t, j0, j1):
-        win, R = mwin(t)
+        win, R = (T.MW[:], ["MW"]) if t == 0 else (T.MF[:, 0:W], ["MF"])
         off, ok = names_of(t)
-        vt, vk = (T.VT, "VT") if t % 2 == 0 else (T.MW, "MW")
         c = slice(512 * j0, 512 * j1)
-        tt(T.EQ[:, c], win.indirect(off[:, 32 * j0:32 * j1]), vt[:, c], A.is_equal,
+        vt, vk = (T.VT[:, c], "VT") if t % 2 == 0 else (T.MW[:, c], "MW")
+        tt(T.EQ[:, c], win.indirect(off[:, 32 * j0:32 * j1]), vt, A.is_equal,
            R + ks(ok, j0, j1) + ["%s#%d" % (vk, q) for q in range(j0 // 2, (j1 + 1) // 2)], ks("EQ", j0, j1))
 
     def pen(t, h):
         src, wt = ("NCL", "PERMB") if t == 0 else ("PVN", "WP")
         mm(SB[h][0][:, 0:128], T[src][:, 128 * h:128 * h + 128], T[wt][:], True, False, [src, wt], [SB[h][1]])
 
-    def score(h, eqs, last):
-        src, wt = ("EQ", "B8E") if eqs else ("AB", "B8A")
+    def score(src, j0, j1, last=False):
+        h, wt = j0 // 4, {"EQ": "B8E", "AB": "B8A"}[src]
         for k in range(16):
-            mm(SB[h][0][:, 15 - k:128:16], T[src][:, 2048 * h + k:2048 * h + 2048:16], T[wt][:], False,
-               last and k == 15, ks(src, 4 * h, 4 * h + 4) + [wt], [SB[h][1]])
+            mm(SB[h][0][32 * (j0 - 4 * h):32 * (j1 - 4 * h), 15 - k:128:16], T[src][:, 512 * j0 + k:512 * j1:16],
+               T[wt][:], False, last and k == 15, ks(src, j0, j1) + [wt], [SB[h][1]])
 
     def names(t):
         src = "O160" if t == 0 else "M16"
@@ -289,8 +314,36 @@ def rank_program(g, core, T, topo):
             ts(T.CN[:, 16:32], T.S1[:, 15:256:16], 2.0 ** -28, 64.498, A.mult, A.add, ["S1"], ["CN#n"])
         scan(T.S3[:, c], T.S2[:, c], T.PA[:, c], 0.0, A.min, A.max, ["S2" + k, "PA"], ["S3" + k])
         if h == 1:
-            cp(T.CI[:], T.S3[:, 15:256:16], ["S3"], ["CI"])
-            ts(T.CN[:, 0:16], T.CI[:], 4095, None, A.bitwise_and, None, ["CI"], ["CN#c"])
+            cp(T.CI[:, 0:16], T.S3[:, 15:256:16], ["S3"], ["CI#0"])
+            ts(T.CI[:, 16:32], T.CI[:, 0:16], 1, 2040, A.arith_shift_right, A.bitwise_and, ["CI#0"], ["CI#1"])
+            ts(T.CN[:, 0:16], T.CI[:, 0:16], 4095, None, A.bitwise_and, None, ["CI#0"], ["CN#c"])
+            tt(T.CN[:, 32:48], T.CN[:, 0:16], T.CI[:, 16:32], A.subtract, ["CN#c", "CI#1"], ["CN#p"])
+
+    def code(out, ends, R, Wr, shift=0):
+        act(out, ends, AF.Silu, R, Wr, bias=-5.0 - shift / 64.0, scale=-1 / 64.0)
+
+    def table1(h0, h1, ls=range(8)):
+        for l in ls:
+            code(T.TBS[:, 1, 8 * h0 + l:8 * h1:8], T.MF[:, 16 * h0 + l:16 * h1:16],
+                 ["MF#%d" % q for q in range(h0 // 64, h1 // 64)], ["TBS1#%d.%d" % (h0, l)])
+
+    def table0(q):
+        for l in range(8):
+            cp(T.G32[:, 512 * q + l:512 * q + 512:8], T.MW[:, 1024 * q + 8 + l:1024 * q + 1024:16], ["MW#%d" % q],
+               ["G32#%d.%d" % (q, l)])
+        code(T.TBS[:, 0, 512 * q:512 * q + 512], T.G32[:, 512 * q:512 * q + 512],
+             ["G32#%d.%d" % (q, l) for l in range(8)], ["TBS0#%d" % q])
+
+    def offer(t, h0=0, h1=256):
+        send(T.TBS[:, t % 2, 8 * h0:8 * h1], [(cores[clients[t]], T.TBL[:, t, 8 * h0:8 * h1])], "at%d" % t,
+             ["TBS%d" % (t % 2)], "left" if t == 0 else "sent")
+
+    def pi(i):
+        off, ok = (T.O2V, "O2V") if i < 2 else (T.O2C, "O2C")
+        cp(T.PI[:].indirect(off[:, 8 * (i % 2):8 * (i % 2) + 8]), T.PV[:, 128 * i:128 * i + 128], [ok, "PV"], ["PI"])
+
+    def again(b):
+        iota(T.MW[:, 1024 * b:1024 * b + 1024], [[16, 64], [0, 16]], 1024 * b + 8 + r, 0, ["MW#%d" % b], False)
 
     def mfloat(q):
         cp(T.MF[:, 1024 * q:1024 * q + 1024], T.MW[:, 1024 * q:1024 * q + 1024], ["MW#%d" % q], ["MF#%d" % q])
@@ -298,7 +351,6 @@ def rank_program(g, core, T, topo):
     def block0(q):
         c = slice(64 * q, 64 * q + 64)
         src = T.MW[:, 1024 * q + r:1024 * q + 1024:16]
-        cp(T.OLD0[:, c], src, ["MW#%d" % q], ks("OLD0", 2 * q, 2 * q + 2))
         ts(T.CLS[:, c], src, 3, 1, A.arith_shift_right, A.bitwise_and, ["MW#%d" % q], ["CLS#%d" % q])
         ts(T.O160[:, c], src, -2048.0, None, A.add, None, ["MW#%d" % q], ["O160#%d" % q])
         ts(T.NCL[:, c], T.CLS[:, c], -1.0, None, A.add, None, ["CLS#%d" % q], ["NCL#%d" % q])
@@ -313,7 +365,6 @@ def rank_program(g, core, T, topo):
     iota(T.PIDX[:, 0:1], [[1, 1]], 0, 1, ["PIDX#0"], False)
     op("g", lambda: g.affine_select(T.ID[:], T.ONES[:], [[-1, 128]], A.is_equal, 0.0, 0, 1), ["ONES"], ["ID"])
     iota(T.IOT[:, 0:256], [[1, 256]], 0, 0, ["IOT#0"])
-    iota(T.VT[:, 0:512], [[16, 32], [0, 16]], r, 0, ["VT#a"])
     iota(T.C4[:], [[1, 8], [0, 16]], 0, 0, ["C4"])
     iota(T.C5[:], [[16, 8], [-1, 16]], 15, 0, ["C5"])
     iota(T.KC[:], [[0, 8], [-32, 16]], 496, 0, ["KC"])
@@ -342,22 +393,17 @@ def rank_program(g, core, T, topo):
     ts(T.KM[:], T.IOT[:, 0:16], PK, None, A.is_equal, None, ["IOT#0", "PF"], ["KM"])
     iota(T.C2[:], [[0, 16], [1, 16]], 0, 0, ["C2"])
     iota(T.C6[:], [[32, 8], [0, 2], [16, 2]], W, 0, ["C6"])
-    iota(T.C7[:], [[16, 16]], WD - 2048, 0, ["C7"])
+    iota(T.SO[:, 0:16], [[16, 16]], WD - 2048, 0, ["SO#0"])
     iota(T.EC[:], [[-4096, 256]], 4096 * 256 - 8 * STEPC, 0, ["EC"])
-    iota(T.FT[:, 0:2048], [[1, 2048]], int(FO), 0, ["FT#a"])
-    iota(T.FT[:, 2048:W], [[1, 2048]], 2048 + int(FO), 0, ["FT#b"])
-    op("g", lambda: g.partition_broadcast(T.THB[:], T.THR[0:1, :], 128), ["THR"], ["THB"])
+    for q in range(4):
+        iota(T.VT[:, 1024 * q:1024 * q + 1024], [[16, 64], [0, 16]], 1024 * q + r, 0, ["VT#%d" % q])
 
-    act(T.VT[:, 512:1024], T.VT[:, 0:512], AF.Identity, ["VT#a"], ["VT#0"], bias=512.0)
-    for q in range(1, 4):
-        act(T.VT[:, 1024 * q:1024 * q + 1024], T.VT[:, 0:1024], AF.Identity, ["VT#a", "VT#0"], ["VT#%d" % q],
-            bias=1024.0 * q)
-    n = 256
-    while n < WD:
+    act(T.VB[:], T.IOT[:, 0:256], AF.Identity, ["IOT#0"], ["VB"], bias=float(r), scale=16.0)
+    for n in (256, 512, 1024, 2048, W):
         m = min(n, WD - n)
         act(T.IOT[:, n:n + m], T.IOT[:, 0:m], AF.Identity, ["IOT"], ["IOT#%d" % n], bias=float(n))
-        n += m
-    ts(T.VB[:], T.IOT[:, 0:256], 16.0, float(r), A.mult, A.add, ["IOT#0"], ["VB"])
+    for a in range(2):
+        code(T.VC[:, a, :], T.VB[:], ["VB"], ["VC%d" % a], 8 * a)
 
     for name, f in (("NID", -1.0), ("ID8K", 8192.0), ("NID4K", -4096.0), ("ID16", 1.0), ("NID16", -1.0), ("ID32", 1.0)):
         ts(T[name][:], T.ID[:], f, None, A.mult, None, ["ID"], [name])
@@ -384,92 +430,111 @@ def rank_program(g, core, T, topo):
     tt(T.SCN[:], T.S1[:], T.S2[:], A.add, ["S1", "S2"], ["SCN"])
     ts(T.DUM[:], T.C6[:], PK, None, A.add, None, ["C6", "PF"], ["DUM"])
     ts(T.DUM2[:], T.C6[:], PK, 2.0, A.add, A.mult, ["C6", "PF"], ["DUM2"])
-    ts(T.DUL[:], T.C7[:], PK, None, A.add, None, ["C7", "PF"], ["DUL"])
+    ts(T.DUL[:], T.SO[:, 0:16], PK, None, A.add, None, ["SO#0", "PF"], ["DUL"])
+    for k in range(16):
+        ts(T.KB[:, 8 * k:8 * k + 8], T.B8[:], T.KM[:, k:k + 1], None, A.mult, None, ["B8", "KM"], ["KB#%d" % k])
     ts(T.SCN[:, 15:256:16], T.SCN[:, 15:256:16], -3.0, None, A.add, None, ["SCN"], ["SCN"])
 
     xtrans(0, raw(0), ["XR1#x"], "D4")
     for j in range(5):
         pre(0, j)
-    for q in range(4):
+    for q in range(3):
+        cp(T.OLD0[:, 64 * q:64 * q + 64], T.MW[:, 1024 * q + r:1024 * q + 1024:16], ["MW#%d" % q],
+           ks("OLD0", 2 * q, 2 * q + 2))
+        gx(0, 2 * q)
+        dmm(0, 2 * q)
+        table0(q)
+        gx(0, 2 * q + 1, "v" if q else "s")
         block0(q)
-        for j in (2 * q, 2 * q + 1):
-            gx(0, j)
-            dmm(0, j)
-        if q < 3:
-            mfloat(q)
-        else:
-            eq(0, 0, 2)
-            pen(0, 0)
-            pen(0, 1)
-            names(0)
-            score(0, False, False)
-        ab(2 * q)
-        ab(2 * q + 1)
-    tt(T.TH8[:], T.THB[:], T.B8[:], A.mult, ["THB", "B8"], ["TH8"])
-    op("v", lambda: V.tensor_reduce(T.THC[:, 0:1], T.TH8[:], AxisListType.X, A.add), ["TH8"], ["THC"])
-    send(T.THC[:, 0:1], [(cores[voters[t]], T.LT[:, 4 * t:4 * t + 1]) for t in range(3)], "ath", ["THC"])
-    lands("ath", sum(share(cores[c], [cores[(c + 1 + t % (N - 1)) % N] for t in range(3)]) for c in clients), ["LT"])
+        mfloat(q)
+        dmm(0, 2 * q + 1)
+        ab(2 * q, 0)
+        ab(2 * q + 1, 0)
+    offer(0, 0, 192)
+    table0(3)
+    cp(T.OLD0[:, 192:256], T.MW[:, 3072 + r:W:16], ["MW#3"], ks("OLD0", 6, 8))
+    offer(0, 192, 256)
+    op("g", lambda: g.partition_broadcast(T.THB[:], T.THR[0:1, :], 128), ["THR"], ["THB"])
+    eq(0, 0, 2)
+    block0(3)
+    for j in (6, 7):
+        gx(0, j)
+        dmm(0, j)
+    pen(0, 0)
+    pen(0, 1)
+    names(0)
+    score("AB", 0, 4)
+    ab(6, 0)
+    ab(7, 0)
+    for b in range(4):
+        iota(T.FT[:, 1024 * b:1024 * b + 1024], [[1, 1024]], 1024 * b + int(FO), 0, ["FT#%d" % b])
     eq(0, 2, 4)
-    score(0, True, True)
-    eq(0, 4, 6)
-    score(1, False, False)
-    eq(0, 6, 8)
+    score("EQ", 0, 4, True)
+    eq(0, 4, 7)
+    score("AB", 4, 8)
+    eq(0, 7, 8)
+    score("EQ", 4, 7, True)
+    tt(T.TV[:, 0:8], T.THB[:], T.B8[:], A.mult, ["THB", "B8"], ["TV#0"])
     best(0)
-    score(1, True, True)
-    for t in range(3):
-        act(T.VC[:, t, :], T.VB[:], AF.Identity, ["VB"], ["VC%d" % t], bias=float(8 * (t % 2) + clients[t] - r))
-    act(T.FT[:, W:WD], T.IOT[:, W:WD], AF.Silu, ["IOT"], ["FT#d"])
+    op("v", lambda: V.tensor_reduce(T.THC[:, 0:1], T.TV[:, 0:8], AxisListType.X, A.add), ["TV#0"], ["THC"])
+    score("EQ", 7, 8, True)
+    ts(T.BIAS[:, 0:5:4], T.ZERO[:, 0:2], T.THC[:, 0:1], -64.0, A.subtract, A.add, ["THC", "ZERO"], ["BIAS#0", "BIAS#4"])
+    act(T.FT[:, W:WD], T.IOT[:, W:WD], AF.Copy, ["IOT"], ["FT#d"])
     act(xl(0), lanes(T.XR1, 0), AF.Copy, ["XR1#x"], ["XL1"])
     for j in range(8):
         act(T.XR0[:, j:W:16], T.XR1[:, j:W:16], AF.Copy, ["XR1#x"], ["XR0#%d" % j])
+    act(xl(1), lanes(T.XR1, 1), AF.Copy, ["XR1#x"], ["XL0"])
+    xtrans(1, raw(1), ["XR1#x"], "D1")
+    table1(0, 192, range(6))
 
     for t in range(3):
         a = t % 2
-        MSG, ALL = T.MSG[:, t, :], T["ALL%d" % t]
-        lc, ln = T.LC[:, t, 0:16], T.LC[:, t, 16:32]
-        q, rho = voters[t], clients[t]
+        ALL = T["ALL%d" % t]
+        if t > 0:
+            SMo, so, xo = T["SM%d" % (t - 1)], "SM%d" % (t - 1), lanes(XR[1 - a], 1 - a)
+            mms("D1", lo, [("ID", xl(1 - a), [XLK[a]]), ("ID", xo, [XK[1 - a]]), ("NID", T.BIGS[:], ["BIGS"])])
+            mms("D1", hi, [("ID", SMo[:], [so]), ("ID", SMo[:], [so]), ("NID", xo, [XK[1 - a]])])
+            o16 = "O16%d" % a
+            mms("D3", lo, [("ID16", T[o16][:], [o16]), ("NID16", T.M16[:], ["M16"]), ("ID8K", T.PVN[:], ["PVN"])])
+            act(T.UU[:], T.D1[:], AF.Relu, ["D1"], ["UU"])
+            act(T.RY[:], T.D3[:, lo], AF.Relu, ["D3"], ["RY"], bias=-4096.0)
+            pi(0)
         best(1)
         for c in range(8):
             ts(T.RX[:, :, :, c], T.CN[:], -2048.0, T.B8[:, c:c + 1], A.add, A.mult, ["CN", "B8"], ["RX#%d" % c])
         for gg in range(8):
-            mm(T.PS[:, 0:32], T.QW[:, 112 - 16 * gg:240 - 16 * gg], T.RX[:, :, gg, :], gg == 0, gg == 7,
+            mm(T.PS[:, 0:48], T.QW[:, 112 - 16 * gg:240 - 16 * gg], T.RX[:, :, gg, :], gg == 0, gg == 7,
                ["QW", "RX"], ["PS"])
-        ts(MSG, T.PS[:, 0:32], 2048.0, None, A.add, None, ["PS"], ["MSG"])
-        send(MSG, [(cores[q], T.LC[:, t, :])], "ac%d" % t, ["MSG"])
-        lands("ac%d" % t, share(cores[rho], [core]), ["LC"])
+        if t > 0:
+            pi(1)
+        chores = [lambda: ts(T.SO[:, 0:16], T.PS[:, 16:32], 40.0 - 2048.0, 1e4, A.is_lt, A.mult, ["PS"], ["SO#0"]),
+                  lambda: tt(T.SO[:, 16:32], T.PS[:, 0:16], T.SO[:, 0:16], A.add, ["PS", "SO#0"], ["SO#1"]),
+                  lambda: tt(T.SO[:, 32:48], T.SO[:, 16:32], T.DUL[:], A.min, ["SO#1", "DUL"], ["SO#2"]),
+                  lambda: ts(T.SOF[:], T.SO[:, 32:48], 2048.0, None, A.add, None, ["SO#2"], ["SOF"])]
 
-        if t == 0:
-            ts(T.BIAS[:, 0:1], T.LT[:, 0:1], -1.0, -64.0, A.mult, A.add, ["LT"], ["BIAS#0"])
-            ts(T.BIAS[:, 4:6], T.LT[:, 4:12:4], -1.0, -64.0, A.mult, A.add, ["LT"], ["BIAS#4"])
-        ts(T.SO[:, 0:16], T.PS[:, 16:32], 40.0 - 2048.0, 1e4, A.is_lt, A.mult, ["PS"], ["SO#0"])
-        if t > 0:
-            ts(T.AI[:, 0:1], T.PA[:, 256:257], 0.5, 1024.0, A.mult, A.add, ["PA"], ["AI#0"])
-        tt(T.SO[:, 16:32], T.PS[:, 0:16], T.SO[:, 0:16], A.add, ["PS", "SO#0"], ["SO#1"])
-        if t > 0:
-            ts(T.AI[:, 1:2], T.AI[:, 0:1], 3, None, A.bitwise_and, None, ["AI#0"], ["AI#1"])
-        tt(T.SO[:, 32:48], T.SO[:, 16:32], T.DUL[:], A.min, ["SO#1", "DUL"], ["SO#2"])
-        if t > 0:
-            ts(T.BIAS[:, 0:1], T.AI[:, 1:2], -1.0, T.BIAS[:, 3 + t:4 + t], A.mult, A.add, ["AI#1", "BIAS#4"],
-               ["BIAS#0"])
-        ts(T.SOF[:], T.SO[:, 32:48], 2048.0, None, A.add, None, ["SO#2"], ["SOF"])
-        if t > 0:
-            tt(T.TC[:, 0:16], T.RR[:, 15:256:16], T.DL[:, :, 0:2], A.mult, ["RR", "DL"], ["TC#0"])
-            tt(T.TC[:, 16:32], T.TC[:, 0:16], T.VP[:, :, 0:2], A.add, ["TC#0", "VP"], ["TC#1"])
-            cp(T.O2C[:], T.TC[:, 16:32], ["TC#1"], ["O2C"])
+        def chore():
+            chores.pop(0)()
 
-        win, R = mwin(t)
-        tt(T.EV[:], win.indirect(lc), T.VC[:, t, :], A.is_equal, R + ["LC", "VC%d" % t], ["EV"])
-        act(T.NF[:], T.IOT[:, 0:512].indirect(ln), AF.Identity, ["IOT", "LC", "BIAS#0"], ["NF"],
+        lands("at%d" % t, (2 if t == 0 else 1) * share(cores[voters[t]], [core]), ["TBL"])
+        ts(T.MSG[:, 32:48], T.PS[:, 32:48], 2048.0 - 8 * (1 - a), 2047.0, A.add, A.min, ["PS"], ["MSG#p"])
+        ts(T.MSG[:, 0:32], T.PS[:, 0:32], 2048.0, None, A.add, None, ["PS"], ["MSG#c"])
+        tt(T.EV[:], T.TBL[:, t, :].indirect(T.MSG[:, 32:48]), T.VC[:, a, :], A.is_equal, ["TBL", "MSG#p", "VC%d" % a],
+           ["EV"])
+        act(T.NF[:], T.IOT[:, 0:512].indirect(T.MSG[:, 16:32]), AF.Identity, ["IOT", "MSG#c", "BIAS#0"], ["NF"],
             bias=T.BIAS[:, 0:1])
         mms("PA", lo, [("BLK", T.EV[:], ["EV"]), ("ID", T.NF[:], ["NF"])])
-        tt(T.EE[:, 0, 0:256], T.IOT[:, 0:W].indirect(lc), T.EC[:], A.add, ["IOT", "LC", "EC"], ["EE#e"])
+        tt(T.EE[:, 0, 0:256], T.IOT[:, 0:W].indirect(T.MSG[:, 0:16]), T.EC[:], A.add, ["IOT", "MSG#c", "EC"], ["EE#e"])
         act(T.EE[:, 1, 0:257], T.EE[:, 0, 0:257], AF.Identity, ["EE#e", "EE#s"], ["EE#f"], bias=16.0 * STEPC)
         ts(T.S2[:], T.PA[:, lo], 0.0, 1.0 * STEPC, A.is_ge, A.mult, ["PA"], ["S2"])
+        chore()
         scan(T.CT[:, 1:257], T.ZERO[:], T.S2[:], T.CT[:, 0:1], A.add, A.add, ["ZERO", "S2", "CT#i"], ["CT#0"])
+        chore()
         for c in range(2):
             scan(T.SC[:, c, 0:257], T.CT[:, 0:257], T.EE[:, c, 0:257], 0.0, A.min, A.max,
                  ["CT", "EE#s", "EE#" + "ef"[c]], ["SC#%d" % c])
+        chore()
         tt(T.EI[:, 0:2], T.SC[:, :, 256], T.OFS[:], A.add, ["SC", "OFS"], ["EI#0"])
+        chore()
         ts(T.EI[:, 2:4], T.EI[:, 0:2], 4095, None, A.bitwise_and, None, ["EI#0"], ["EI#1"])
         ts(T.EI[:, 4:6], T.EI[:, 0:2], 12, None, A.arith_shift_right, None, ["EI#0"], ["EI#2"])
         cp(T.C16[:], T.EI[:, 2:4], ["EI#1"], ["C16"])
@@ -478,28 +543,35 @@ def rank_program(g, core, T, topo):
         for c in range(2):
             ts(T.NE[:, 1 + 34 * c:33 + 34 * c], T.IOT[:, 0:W].indirect(T.C16[:]), T.CVF[:, c:c + 1], B2,
                A.is_equal, A.mult, ["IOT", "C16", "CVF#c"], ["NE#%d" % c])
-        ts(T.CVF[:, 2:4], T.EI[:, 4:6], -16.0, float(W + 8 * a + rho), A.mult, A.add, ["EI#2"], ["CVF#v"])
+        ts(T.CVF[:, 2:4], T.EI[:, 4:6], -16.0, float(W + 8 * a + r), A.mult, A.add, ["EI#2"], ["CVF#v"])
         scan(T.NS[:, 0:67], T.NE[:, 0:67], T.STEP[:, 0:67], 0.0, A.max, A.add, ["STEP", "NE"], ["NS"])
         for c in range(2):
-            ts(ALL[:, rho, c:4:2], T.CVF[:, c:4:2], T.NS[:, 32 + 34 * c:33 + 34 * c], T.DUM[:, rho, c:c + 1],
+            ts(ALL[:, r, c:4:2], T.CVF[:, c:4:2], T.NS[:, 32 + 34 * c:33 + 34 * c], T.DUM[:, r, c:c + 1],
                A.max, A.min, ["CVF", "NS", "DUM"], ["ALL#o%d" % c])
         others = [cores[(r + i) % N] for i in range(1, N)]
-        send(ALL[:, rho, 0:4], [(c, ALL[:, rho, 0:4]) for c in others], "aa%d" % t, ["ALL#o0", "ALL#o1"])
+        mine = ["ALL#o0", "ALL#o1"]
+        send(ALL[:, r, 0:4], [(c, ALL[:, r, 0:4]) for c in others], "aa%d" % t, mine)
         lands("aa%d" % t, sum(share(c, [d for d in cores if d != c]) for c in others), ["ALL#r"])
 
         if t > 0:
-            SMo, so, xo = T["SM%d" % (t - 1)], "SM%d" % (t - 1), lanes(XR[1 - a], 1 - a)
-            mms("D1", lo, [("ID", xl(1 - a), [XLK[a]]), ("ID", xo, [XK[1 - a]]), ("NID", T.BIGS[:], ["BIGS"])])
-            mms("D1", hi, [("ID", SMo[:], [so]), ("ID", SMo[:], [so]), ("NID", xo, [XK[1 - a]])])
-            o16 = "O16%d" % a
-            mms("D3", lo, [("ID16", T[o16][:], [o16]), ("NID16", T.M16[:], ["M16"]), ("ID8K", T.PVN[:], ["PVN"])])
+            mms("D1", lo, [("ID", T.UU[:, lo], ["UU"]), ("ID", T.UU[:, hi], ["UU"])])
+        if t == 1:
+            mms("D2", lo, [("ID16", T.M16[:], ["M16"])])
+            act(lanes(T.MF, 1), T.D2[:, lo], AF.Identity, ["D2"], ["MF"], bias=2048.0)
+            act(xl(0), T.D1[:, lo], AF.Copy, ["D1"], ["XL1"])
+        if t == 0:
+            minus(1, (2, 4))
         act(T.XC[:], XR[1 - a][:].indirect(T.SOF[:]), AF.Copy, [XK[1 - a], XLK[1 - a], "SOF"], ["XC"])
         mms("D0", lo, [("ID", xl(a), [XLK[1 - a]]), ("ID", T.XC[:], ["XC"])])
+        if t == 0:
+            ts(T.O161[:], lanes(T.MW, 1), -2048.0, None, A.add, None, ["MW"], ["O161"])
+            mfloat(3)
+        if t < 2:
+            bylane(1 - a, 0)
         if t > 0:
-            act(T.UU[:], T.D1[:], AF.Relu, ["D1"], ["UU"])
-            act(T.RY[:], T.D3[:, lo], AF.Relu, ["D3"], ["RY"], bias=-4096.0)
-            mms("D2", lo, [("ID", T.UU[:, lo], ["UU"]), ("ID", T.UU[:, hi], ["UU"])])
             mms("D4", lo, [("ID16", T.M16[:], ["M16"]), ("NID4K", T.PVN[:], ["PVN"]), ("ID32", T.RY[:], ["RY"])])
+        if t == 2:
+            act(T.YX[:, 1:512:2], T.D1[:, lo], AF.Copy, ["D1"], ["YX#b"])
         act(T.T1[:], T.D0[:, lo], AF.Identity, ["D0"], ["T1"], bias=RND, scale=0.5 - 2.0 ** -13)
         if t < 2:
             act(lanes(XR[a], a), T.T1[:], AF.Identity, ["T1"], [XK[a]], bias=-RND)
@@ -507,68 +579,78 @@ def rank_program(g, core, T, topo):
         else:
             act(T.YX[:, 0:512:2], T.T1[:], AF.Identity, ["T1"], ["YX#a"], bias=-RND)
         if t == 0:
-            act(xl(1), lanes(T.XR1, 1), AF.Copy, ["XR1"], ["XL0"])
-            xtrans(1, raw(1), ["XR1"], "D1")
             xtrans(2, [T.SM0[:, 0:128], T.SM0[:, 128:256]], ["SM0"], "D2")
-        if t == 1:
-            mms("D3", lo, [("ID16", T.M16[:], ["M16"])])
-            act(lanes(T.MF, 1), T.D3[:, lo], AF.Identity, ["D3"], ["MF"], bias=2048.0)
-            act(xl(0), T.D2[:, lo], AF.Copy, ["D2"], ["XL1"])
-        if t == 2:
-            act(T.YX[:, 1:512:2], T.D2[:, lo], AF.Copy, ["D2"], ["YX#b"])
         if t > 0:
             act(T.YM[:, a:512:2], T.D4[:, lo], AF.Identity, ["D4"], ["YM#%d" % a], bias=2048.0)
-        if t == 2:
-            dma("y", "out", lambda: g.sync.dma_start(T.ym[:], T.YM[:]), ["YM"], [])
         if t < 2:
             act(T.PB[:, hi], T.VB[:], AF.Identity, ["VB"], ["PB"], bias=8.0 * (1 - a) + FO)
-            for j in range(5):
+            if t == 0:
+                table1(0, 192, (6, 7))
+            else:
+                minus(2, (0, 1))
+            bylane(1 - a, 1)
+            for j in [j for j in range(8) if j not in XV][4::-1]:
                 pre(t + 1, j)
+        if t == 1:
+            wait("s", "left", total["left"])
+            code(T.TBS[:, 0, r:2048:8], lanes(T.MF, 1), ["MF"], ["TBS0"])
+            order("g", ["ALL"], [])
+            offer(2)
 
         if t == 0:
-            mfloat(3)
-            cp(T.OLD1[:], lanes(T.MW, 1), ["MW"], ["OLD1"])
-            ts(T.O161[:], lanes(T.MW, 1), -2048.0, None, A.add, None, ["MW"], ["O161"])
-            for b in range(4):
-                iota(T.MW[:, 1024 * b:1024 * b + 1024], [[16, 64], [0, 16]], 1024 * b + 8 + r, 0, ["MW#%d" % b], False)
-            iota(T.PI[:], [[0, WD]], -1, 0, ["PI"])
+            cp(T.OLD1[:], T.MW[:, 8 + r:2048:16], ["MW"], ["OLD1"])
+            again(0)
+            again(1)
+        elif t == 1:
+            pi(2)
+            pi(3)
+            cp(T.XR1[:, 0:WD].indirect(T.O2C[:]), T.BIGS[:], ["O2C", "BIGS"], ["XR1"])
         else:
-            cp(T.PI[:].indirect(T.O2V[:]), T.PV[:, lo], ["O2V", "PV"], ["PI"])
-            cp(T.PI[:].indirect(T.O2C[:]), T.PV[:, hi], ["O2C", "PV"], ["PI"])
-            if t == 1:
-                cp(T.XR1[:, 0:WD].indirect(T.O2C[:]), T.BIGS[:], ["O2C", "BIGS"], ["XR1"])
+            dma("y", "out", lambda: g.sync.dma_start(T.ym[:], T.YM[:]), ["YM"], [])
+            ts(T.OI[:, 0:2], ALL[:, r, 2:4], 1 / 16.0, 255.0, A.mult, A.min, mine, ["OI"])
+            ts(T.TV[:, 0:2], ALL[:, r, 2:4], 0.125, -r / 8.0, A.mult, A.add, mine, ["TV#0"])
+            pi(2)
+            for c in range(2):
+                ts(T.OI[:, 2 + c:3 + c], ALL[:, r, 2 + c:3 + c], 512.0 - W, T.TV[:, c:c + 1], A.add, A.max,
+                   mine + ["TV#0"], ["OY#%d" % c])
+            act(T.OX[:, 0:32], xl(0).indirect(T.OI[:, 0:2]), AF.Copy, ["XL1", "OI"], ["OX#0"])
+            act(T.OX[:, 32:64], T.YX[:].indirect(T.OI[:, 2:4]), AF.Copy, ["YX", "OY"], ["OX#1"])
+            pi(3)
+            tt(T.OX[:, 64:96], T.OX[:, 32:64], T.OX[:, 0:32], A.subtract, ["OX#0", "OX#1"], ["OX#2"])
 
         own, ok = (T.FT, "FT") if t < 2 else (T.PI, "PI")
         src, sk = (T.MF, ["MF", "MFd"]) if t < 2 else (T.IOT, ["IOT"])
-        cp(T.CVL[:, 0:16], ALL[:, :, 0:2], ["ALL"], ["CVL#c"])
-        cp(T.CVL[:, 16:32], ALL[:, :, 2:4], ["ALL"], ["CVL#v"])
+        fill = [lambda: cp(T.CVL[:, 0:16], ALL[:, :, 0:2], ["ALL"], ["CVL#c"]),
+                lambda: cp(T.CVL[:, 16:32], ALL[:, :, 2:4], ["ALL"], ["CVL#v"])]
         if t < 2:
-            cp(T.VCF[:], ALL[:, :, 0:4], ["ALL"], ["VCF"])
-            tt(T.DL[:], T.DUM[:], T.VCF[:], A.subtract, ["DUM", "VCF"], ["DL"])
-            tt(T.VP[:], T.DUM2[:], T.VCF[:], A.subtract, ["DUM2", "VCF"], ["VP"])
-        else:
-            ts(T.OI[:], ALL[:, r, 2:4], 1 / 16.0, 255.0, A.mult, A.min, ["ALL"], ["OI"])
-            ts(T.TY[:], ALL[:, r, 2:4], 0.125, -r / 8.0, A.mult, A.add, ["ALL"], ["TY"])
-            for c in range(2):
-                ts(T.OY[:, c:c + 1], ALL[:, r, 2 + c:3 + c], 512.0 - W, T.TY[:, c:c + 1], A.add, A.max,
-                   ["ALL", "TY"], ["OY#%d" % c])
+            fill += [lambda: bylane(1 - a, 2),
+                     lambda: cp(T.VCF[:], ALL[:, :, 0:4], ["ALL"], ["VCF"]),
+                     lambda: tt(T.DL[:], T.DUM[:], T.VCF[:], A.subtract, ["DUM", "VCF"], ["DL"]),
+                     lambda: tt(T.VP[:], T.DUM2[:], T.VCF[:], A.subtract, ["DUM2", "VCF"], ["VP"])]
         for p in range(N - 1, -1, -1):
             c = slice(32 * p, 32 * p + 32)
             act(T.VALV[:, c], src[:].indirect(ALL[:, p, 2:4]), AF.Identity, sk + ["ALL"], ["VALV#%d" % p],
                 bias=FO + (p + 1) / 128.0 if t < 2 else 0.0)
+            if fill:
+                fill.pop(0)()
             cp(own[:].indirect(ALL[:, p, 0:2]), T.VALV[:, c], ["ALL", "VALV#%d" % p], [ok])
         act(T.VALC[:], src[:].indirect(T.CVL[:, 0:16]), AF.Identity, sk + ["CVL#c"], ["VALC"],
             bias=FO + 1 / 16.0 if t < 2 else 0.0)
-        if t == 2:
-            act(T.OX[:, 0:32], xl(0).indirect(T.OI[:]), AF.Copy, ["XL1", "OI"], ["OX#0"])
-            act(T.OX[:, 32:64], T.YX[:].indirect(T.OY[:]), AF.Copy, ["YX", "OY"], ["OX#1"])
+        if t < 2:
+            act(T.PV[:], T.IOT[:].indirect(T.CVL[:]), AF.Copy, ["IOT", "CVL"], ["PV"])
+        else:
             act(T.D0[:, lo], T.VALC[:], AF.Identity, ["VALC"], ["D0"], bias=1.0)
-            tt(T.OX[:, 64:96], T.OX[:, 32:64], T.OX[:, 0:32], A.subtract, ["OX#0", "OX#1"], ["OX#2"])
+        if t == 0:
+            table1(192, 256)
+            offer(1)
+            again(2)
+            again(3)
+            iota(T.PI[:], [[0, WD]], -1, 0, ["PI"])
         tt(T.S1[:], own[:].indirect(T.CVL[:, 0:16]), T.VALV[:], A.not_equal, [ok, "CVL#c", "VALV"], ["S1"])
         if t == 2:
             tt(T.OX[:, 96:128], T.S1[:, 32 * r:32 * r + 32], T.OX[:, 64:96], A.mult, ["S1", "OX#2"], ["OX#3"])
             tt(T.S2[:], T.S1[:], T.D0[:, lo], A.mult, ["S1", "D0"], ["S2"])
-            tt(T.YX[:].indirect(T.OY[:]), T.OX[:, 0:32], T.OX[:, 96:128], A.add, ["OY", "OX"], ["YX"])
+            tt(T.YX[:].indirect(T.OI[:, 2:4]), T.OX[:, 0:32], T.OX[:, 96:128], A.add, ["OY", "OX"], ["YX"])
             dma("s", "out", lambda: g.scalar.dma_start(T.yx[:], T.YX[:, 0:512]), ["YX"], [])
             tt(T.PI[:].indirect(T.CVL[:, 16:32]), T.VALC[:], T.S2[:], A.subtract, ["CVL#v", "VALC", "S2"], ["PI"])
             dma("y", "out", lambda: g.sync.dma_start(T.yp[:], T.PI[0:128:16, 0:W]), ["PI"], [])
@@ -583,22 +665,36 @@ def rank_program(g, core, T, topo):
         u = t + 1
         OLD, oldk = T["OLD%d" % (u % 2)], "OLD%d" % (u % 2)
 
-        def follow(j0, j1, q="v"):
-            win = T.FT[:, 0:W].indirect(OLD[:, 32 * j0:32 * j1])
-            if q == "s":
-                act(T.G32[:, 0:512 * (j1 - j0)], win, AF.Identity, ["FT", oldk], ["G32"], bias=-2048.0 - FO)
-            else:
-                ts(T.G16[:, 512 * j0:512 * j1], win, -2048.0 - FO, None, A.add, None, ["FT", oldk], ks("G16", j0, j1))
+        def follow(j0, j1):
+            ts(T.G16[:, 512 * j0:512 * j1], T.FT[:, 0:W].indirect(OLD[:, 32 * j0:32 * j1]), -2048.0 - FO, None, A.add,
+               None, ["FT", oldk], ks("G16", j0, j1))
 
-        def keep(j0, j1, bk, q="v", k0=0, k1=16):
+        def follows(k0, k1):
+            act(T.G32[:, 128 * k0:128 * k1], T.FT[:, 0:W].indirect(T.OLDT[:, u % 2, 8 * k0:8 * k1]), AF.Identity,
+                ["FT", "OLDT%d" % (u % 2)], ks("G32", k0, k1), bias=-2048.0 - FO)
+
+        def keep(j0, j1, bk):
+            for k in range(16):
+                mm(T[bk][:, 0:32 * (j1 - j0)], T.DK16[:, 128 * k:128 * k + 128], T.G16[:, 512 * j0 + k:512 * j1:16],
+                   k == 0, k == 15, ["DK16"] + ks("G16", j0, j1), [bk])
+
+        def keepl(k0, k1):
             for k in range(k0, k1):
-                out = T[bk][:, 0:32 * (j1 - j0)]
-                if q == "s":
-                    mm(out, T.DK32[:, 128 * k:128 * k + 128], T.G32[:, k:512 * (j1 - j0):16], k == 0, k == 15,
-                       ["DK32", "G32"], [bk])
-                else:
-                    mm(out, T.DK16[:, 128 * k:128 * k + 128], T.G16[:, 512 * j0 + k:512 * j1:16],
-                       k == 0, k == 15, ["DK16"] + ks("G16", j0, j1), [bk])
+                mm(T.PS[:, k:128:16], T.G32[:, 128 * k:128 * k + 128], T.KB[:, 8 * k:8 * k + 8], True, True,
+                   ["KB", "G32#%d" % k], ["PS"])
+
+        def turn(bk):
+            cp(T.L16[:], T.PS[:, 0:128], ["PS"], ["L16"])
+            mm(T[bk][:, 0:128], T.L16[:], T.ID16[:], True, True, ["L16", "ID16"], [bk])
+
+        def xv(j):
+            i = XV.index(j)
+            tt(T.GX[:, 512 * j:512 * j + 512], XR[1 - u % 2][:, 0:W].indirect(T.OFF[:, 32 * j:32 * j + 32]),
+               T.XRP[:, 512 * i:512 * i + 512], A.add, [XK[1 - u % 2], "OFF#%d" % j, "XRP#%d" % j], ["GX#%d" % j])
+
+        def abv(j):
+            c = slice(512 * j, 512 * j + 512)
+            act(T.AB[:, c], T.GX[:, c], AF.Abs, ["GX#%d" % j], ["AB#%d" % j])
 
         def offs(j0, j1, bk):
             ts(T.OFF[:, 32 * j0:32 * j1], T[bk][:, 0:32 * (j1 - j0)], 2048.0, None, A.add, None, [bk],
@@ -609,8 +705,16 @@ def rank_program(g, core, T, topo):
             dmm(u, j)
 
         def won():
-            op("s", lambda: S.activation(T.WON[:], T.TV[:, 16:32], AF.Sign, bias=T.BIAS[:, 10:11], scale=-1.0,
+            op("s", lambda: S.activation(T.TC[:, 32:48], T.TV[:, 16:32], AF.Sign, bias=T.BIAS[:, 10:11], scale=-1.0,
                                          accum_out=T.AC[:, 0:1]), ["TV#1", "BIAS#10"], ["WON", "AC"])
+
+        def partners(step):
+            if step == 0:
+                tt(T.TC[:, 0:16], T.RR[:, 15:256:16], T.DL[:, :, 0:2], A.mult, ["RR", "DL"], ["TC#0"])
+            elif step == 1:
+                tt(T.TC[:, 16:32], T.TC[:, 0:16], T.VP[:, :, 0:2], A.add, ["TC#0", "VP"], ["TC#1"])
+            else:
+                cp(T.O2C[:], T.TC[:, 16:32], ["TC#1"], ["O2C"])
 
         def pvn():
             tt(T.PVN[:], lanes(T.FT, u % 2), T.PB[:, hi], A.not_equal, ["FT", "PB"], ["PVN"])
@@ -618,59 +722,75 @@ def rank_program(g, core, T, topo):
         def m16():
             ts(T.M16[:], T.OFF[:], -2048.0, None, A.add, None, ["OFF"], ["M16"])
 
-        def count():
-            names(u)
-            mm(T.PA[:, 256:257], T.ONE32[:], T.AC[:, 0:1], True, True, ["ONE32", "AC"], ["PA"])
+        def count(step):
+            if step == 0:
+                mm(T.PS[:, 256:257], T.ONE32[:], T.AC[:, 0:1], True, True, ["ONE32", "AC"], ["PS"])
+            elif step == 1:
+                ts(T.AI[:, 0:1], T.PS[:, 256:257], 0.5, 1024.0, A.mult, A.add, ["PS"], ["AI#0"])
+            elif step == 2:
+                ts(T.AI[:, 1:2], T.AI[:, 0:1], 3, None, A.bitwise_and, None, ["AI#0"], ["AI#1"])
+            else:
+                ts(T.BIAS[:, 0:1], T.AI[:, 1:2], -1.0, T.BIAS[:, 4:5], A.mult, A.add, ["AI#1", "BIAS#4"], ["BIAS#0"])
 
         follow(0, 2)
-        won()
+        for k0, k1 in ((0, 2), (2, 6)):
+            follows(k0, k1)
+            keepl(k0, k1)
+        follows(6, 11)
         keep(0, 2, "PA")
         pvn()
         follow(2, 3)
+        keepl(6, 11)
+        follows(11, 16)
+        partners(0)
         offs(0, 2, "PA")
         follow(3, 4)
-        x(0)
+        keepl(11, 13)
         keep(2, 4, "PB")
-        x(1)
-        follow(4, 5)
+        keepl(13, 16)
+        won()
+        count(0)
+        gx(u, 0)
+        xv(1)
+        dmm(u, 0)
+        partners(1)
         offs(2, 4, "PB")
-        ab(0)
-        follow(5, 6)
-        ab(1)
-        keep(4, 6, "PA")
-        x(2)
-        follow(6, 8)
-        offs(4, 6, "PA")
-        x(3)
-        ab(2)
-        keep(6, 8, "PB")
-        eq(u, 0, 2)
-        offs(6, 8, "PB")
+        partners(2)
+        turn("PA")
+        count(1)
+        abv(1)
+        eq(u, 0, 1)
+        offs(4, 8, "PA")
+        count(2)
         m16()
-        x(4)
-        ab(3)
+        count(3)
+        x(2)
+        ab(0)
         pen(u, 0)
         pen(u, 1)
-        eq(u, 2, 4)
-        score(0, False, False)
+        names(u)
+        eq(u, 1, 4)
+        x(3)
+        ab(2)
+        x(4)
+        score("EQ", 0, 4)
+        ab(3)
         x(5)
+        score("AB", 0, 4, True)
         ab(4)
-        count()
+        eq(u, 4, 8)
         x(6)
         ab(5)
-        eq(u, 4, 6)
-        x(7)
+        xv(7)
+        score("EQ", 4, 8)
         ab(6)
-        score(0, True, True)
-        eq(u, 6, 8)
-        ab(7)
+        score("AB", 4, 7, True)
+        abv(7)
         best(0)
-        score(1, False, False)
-        score(1, True, True)
-        act(T.PV[:], T.IOT[:].indirect(T.CVL[:]), AF.Copy, ["IOT", "CVL"], ["PV"])
+        score("AB", 7, 8, True)
         if u == 1:
             for j in range(8):
-                act(T.XR1[:, j:W:16], T.BIGS[:], AF.Copy, ["BIGS"], ["XR1"] if j == 0 else ["XR1#%d" % j])
+                iota(T.XR1[:, j:W:16], [[0, 256]], int(BIG), 0, ["XR1"] if j == 0 else ["XR1#%d" % j])
 
     for s, v in total.items():
         wait("g", s, v)

@@ -35,7 +35,7 @@ SCRATCH = {
     "KC": sb(128, BF), "QW": sb(240, F16),
     "B8": sb(8, F32), "B8E": sb(8, BF), "B8A": sb(8, BF),
     "KM": sb(16, F32), "PIDX": sb(4, I32), "PF": sb(4, F32),
-    "C2": sb(256, F32), "C4": sb(128, F32), "C5": sb(128, F32), "C6": sb([8, 4], F32), "L16": sb(128, F16),
+    "C4": sb(128, F32), "C5": sb(128, F32), "C6": sb([8, 4], F32), "L16": sb(128, F16),
     "VB": sb(256, F32), "VC": sb([2, 256], BF),
     "RST": sb(128, F32), "ZERO": sb(256, F32), "SCN": sb(256, F32), "EC": sb(256, F32), "BIGS": sb(256, BF),
     "DUM": sb([8, 4], F32), "DUM2": sb([8, 4], F32), "DUL": sb(16, F32), "STEP": sb(68, F32), "OFS": sb(2, F32),
@@ -45,15 +45,15 @@ SCRATCH = {
     "TBL": sb([3, 2048], BF), "TBS": sb([2, 2048], BF),
     "ALL0": sb([8, 8], U16), "ALL1": sb([8, 8], U16), "ALL2": sb([8, 8], U16),
     "EV": sb(256, BF), "NF": sb(256, BF), "EE": sb([2, 260], F32), "CT": sb(260, F32), "SC": sb([2, 260], F32),
-    "EI": sb(8, I32), "C16": sb(2, U16), "CVF": sb(4, F32), "NE": sb(68, F32), "NS": sb(68, F32),
+    "EI": sb(8, I32), "C16": sb(2, U16), "CVF": sb(6, F32), "NE": sb(68, F32), "NS": sb(68, F32),
     "CVL": sb(32, U16), "VCF": sb([8, 4], F32), "DL": sb([8, 4], F32), "VP": sb([8, 4], F32),
     "TV": sb(32, F32), "TC": sb(48, F32), "O2V": sb(16, U16), "O2C": sb(16, U16),
-    "AC": sb(4, F32), "AI": sb(4, I32), "SO": sb(48, F32), "SOF": sb(16, U16),
+    "AC": sb(4, F32), "SO": sb(48, F32), "SOF": sb(16, U16),
 }
 PSUM = ("D0", "D1", "D2", "D3", "D4", "PS", "PA", "PB")
 SCRATCH.update({n: ("psum", [128, 512], F32) for n in PSUM})
-SEMAPHORES = ["qv", "qs", "qp", "qg", "lx", "lm0", "lm1", "lm2", "lm3", "lth", "out", "sent",
-              "aa0", "aa1", "aa2", "at0", "at1", "at2", "left"]
+SEMAPHORES = ["qv", "qs", "qp", "qg", "lx", "lm0", "lm1", "lm2", "lm3", "lth", "out", "sent", "left",
+              "fx", "ff0", "ff1", "ff2", "fr", "fp", "aa0", "aa1", "aa2", "at0", "at1", "at2"]
 
 
 def bits(m):
@@ -150,6 +150,11 @@ def rank_program(g, core, T, topo):
         total[sem] = val
         note(("d", sem, val), [], keys)
 
+    def copies(sem, jobs):
+        for out, in_, R, Wr in jobs:
+            dma("y", sem, lambda: g.sync.dma_start(out, in_), R, [])
+        lands(sem, total[sem], [job[3] for job in jobs])
+
     V, S, P = g.vector, g.scalar, g.tensor
 
     def ts(out, in0, s1, s2, o0, o1, R, Wr):
@@ -185,6 +190,9 @@ def rank_program(g, core, T, topo):
             op("g", lambda: g.iota(out, pat, base, cm, allow_small_or_imprecise_dtypes=True), [], Wr)
         else:
             op("g", lambda: g.iota(out, pat, base, cm), [], Wr)
+
+    def select(out, in_, pat, base, cm, R, Wr):
+        op("g", lambda: g.affine_select(out, in_, pat, A.is_equal, 0.0, base, cm), R, Wr)
 
     def send(src, pairs, sem, R, gone="sent"):
         order("g", R, [])
@@ -245,16 +253,18 @@ def rank_program(g, core, T, topo):
             act(T.XRP[:, 512 * i:512 * i + 512], DB[b][:], AF.Copy, ["D%d" % b], ["XRP#%d" % j])
 
     def bylane(a, step):
+        b1, b2, c0 = ("D1", "D3")[a], ("PA", "PS")[a], 1024 * a
         if step == 0:
-            mm(T.D3[:, 0:128], T["O16%d" % a][:, 128:256], T.ID16[:], True, True, ["O16%d" % a, "ID16"], ["D3"])
+            mm(T[b1][:, 0:128], T["O16%d" % a][:, 128:256], T.ID16[:], True, True, ["O16%d" % a, "ID16"], [b1])
             for c in range(8):
-                ts(T.G16[:, c:1024:8], T.D3[:, 0:128], T.B8[:, c:c + 1], None, A.mult, None, ["D3", "B8"], ["RT#%d" % c])
+                ts(T.G16[:, c0 + c:c0 + 1024:8], T[b1][:, 0:128], T.B8[:, c:c + 1], None, A.mult, None, [b1, "B8"],
+                   ["RT%d#%d" % (a, c)])
         elif step == 1:
             for gg in range(8):
-                mm(T.PS[:, 0:128], T.QW[:, 112 - 16 * gg:240 - 16 * gg], T.G16[:, 128 * gg:128 * gg + 128],
-                   gg == 0, gg == 7, ["QW", "RT", "G16"], ["PS"])
+                mm(T[b2][:, 0:128], T.QW[:, 112 - 16 * gg:240 - 16 * gg], T.G16[:, c0 + 128 * gg:c0 + 128 * gg + 128],
+                   gg == 0, gg == 7, ["QW", "RT%d" % a, "G16"], [b2])
         else:
-            ts(T.OLDT[:, a, :], T.PS[:, 0:128], 2048.0, None, A.add, None, ["PS"], ["OLDT%d" % a])
+            ts(T.OLDT[:, a, :], T[b2][:, 0:128], 2048.0, None, A.add, None, [b2], ["OLDT%d" % a])
 
     def names_of(t):
         return (T.OLD0, "OLD0") if t == 0 else (T.OFF, "OFF")
@@ -280,12 +290,11 @@ def rank_program(g, core, T, topo):
         act(T.AB[:, 512 * j:512 * j + 512], DB[b][:], AF.Abs, ["D%d" % b], ["AB#%d" % j])
 
     def eq(t, j0, j1):
-        win, R = (T.MW[:], ["MW"]) if t == 0 else (T.MF[:, 0:W], ["MF"])
+        win, R = (T.MW[:], ["MW"]) if t % 2 == 0 else (T.MF[:, 0:W], ["MF"])
         off, ok = names_of(t)
         c = slice(512 * j0, 512 * j1)
-        vt, vk = (T.VT[:, c], "VT") if t % 2 == 0 else (T.MW[:, c], "MW")
-        tt(T.EQ[:, c], win.indirect(off[:, 32 * j0:32 * j1]), vt, A.is_equal,
-           R + ks(ok, j0, j1) + ["%s#%d" % (vk, q) for q in range(j0 // 2, (j1 + 1) // 2)], ks("EQ", j0, j1))
+        tt(T.EQ[:, c], win.indirect(off[:, 32 * j0:32 * j1]), T.VT[:, c], A.is_equal,
+           R + ks(ok, j0, j1) + ks("VT", j0 // 2, (j1 + 1) // 2), ks("EQ", j0, j1))
 
     def pen(t, h):
         src, wt = ("NCL", "PERMB") if t == 0 else ("PVN", "WP")
@@ -322,10 +331,10 @@ def rank_program(g, core, T, topo):
     def code(out, ends, R, Wr, shift=0):
         act(out, ends, AF.Silu, R, Wr, bias=-5.0 - shift / 64.0, scale=-1 / 64.0)
 
-    def table1(h0, h1, ls=range(8)):
-        for l in ls:
+    def table1(h0, h1):
+        for l in range(8):
             code(T.TBS[:, 1, 8 * h0 + l:8 * h1:8], T.MF[:, 16 * h0 + l:16 * h1:16],
-                 ["MF#%d" % q for q in range(h0 // 64, h1 // 64)], ["TBS1#%d.%d" % (h0, l)])
+                 ["MF#%d" % q for q in range(h0 // 64, h1 // 64)], ["TBS1#%d.%d" % (h0, l)], 8)
 
     def table0(q):
         for l in range(8):
@@ -342,11 +351,13 @@ def rank_program(g, core, T, topo):
         off, ok = (T.O2V, "O2V") if i < 2 else (T.O2C, "O2C")
         cp(T.PI[:].indirect(off[:, 8 * (i % 2):8 * (i % 2) + 8]), T.PV[:, 128 * i:128 * i + 128], [ok, "PV"], ["PI"])
 
-    def again(b):
-        iota(T.MW[:, 1024 * b:1024 * b + 1024], [[16, 64], [0, 16]], 1024 * b + 8 + r, 0, ["MW#%d" % b], False)
+    def picks(i):
+        c = slice(512 * i, 512 * i + 512)
+        select(T.DK16[:, c], T.DK16[:, c], [[1, 4], [0, 8], [-1, 16]], 4 * i, 0, ["DK16#%d" % i], ["DK16#%d" % i])
 
     def mfloat(q):
-        cp(T.MF[:, 1024 * q:1024 * q + 1024], T.MW[:, 1024 * q:1024 * q + 1024], ["MW#%d" % q], ["MF#%d" % q])
+        c = slice(1024 * q, 1024 * q + 1024)
+        ts(T.MF[:, c], T.MW[:, c], -8.0, None, A.add, None, ["MW#%d" % q], ["MF#%d" % q])
 
     def block0(q):
         c = slice(64 * q, 64 * q + 64)
@@ -363,25 +374,21 @@ def rank_program(g, core, T, topo):
 
     ms(T.ONES[:], 1.0, ["ONES"])
     iota(T.PIDX[:, 0:1], [[1, 1]], 0, 1, ["PIDX#0"], False)
-    op("g", lambda: g.affine_select(T.ID[:], T.ONES[:], [[-1, 128]], A.is_equal, 0.0, 0, 1), ["ONES"], ["ID"])
-    iota(T.IOT[:, 0:256], [[1, 256]], 0, 0, ["IOT#0"])
-    iota(T.C4[:], [[1, 8], [0, 16]], 0, 0, ["C4"])
+    select(T.ID[:], T.ONES[:], [[-1, 128]], 0, 1, ["ONES"], ["ID"])
+    iota(T.IOT[:, 0:256], [[1, 256]], int(FO), 0, ["IOT#0"])
     iota(T.C5[:], [[16, 8], [-1, 16]], 15, 0, ["C5"])
+    iota(T.C4[:], [[1, 8], [0, 16]], 0, 0, ["C4"])
+    for q in range(4):
+        iota(T.VT[:, 1024 * q:1024 * q + 1024], [[16, 64], [0, 16]], 1024 * q + r, 0, ["VT#%d" % q])
     iota(T.KC[:], [[0, 8], [-32, 16]], 496, 0, ["KC"])
 
     ts(T.PIDX[:, 1:2], T.PIDX[:, 0:1], 15, None, A.bitwise_and, None, ["PIDX#0"], ["PIDX#1"])
     ts(T.PIDX[:, 2:3], T.PIDX[:, 0:1], 4, None, A.arith_shift_right, None, ["PIDX#0"], ["PIDX#2"])
+    ms(T.BIGS[:], BIG, ["BIGS"])
+    ms(T.ZERO[:], 0.0, ["ZERO"])
     cp(T.PF[:, 2:3], T.PIDX[:, 0:1], ["PIDX#0"], ["PF#2"])
     cp(T.PF[:, 0:2], T.PIDX[:, 1:3], ["PIDX#1", "PIDX#2"], ["PF#0"])
-    for j in range(8, 16):
-        ms(T.XR0[:, j:W:16], BIG, ["XR0#%d" % j])
-    ms(T.XR0[:, W:WD], BIG, ["XR0#d"])
-    ms(T.XR1[:, W:WD], BIG, ["XR1#d"])
-    ms(T.MF[:, W:WD], 0.0, ["MFd"])
-    ms(T.YX[:, 512:768], 0.0, ["YX#d"])
     ms(T.RST[:], 0.0, ["RST"])
-    ms(T.ZERO[:], 0.0, ["ZERO"])
-    ms(T.BIGS[:], BIG, ["BIGS"])
     ms(T.ONE32[:], 1.0, ["ONE32"])
     ms(T.STEP[:], 0.0, ["STEP"])
     ms(T.NE[:], 0.0, ["NE"])
@@ -389,51 +396,43 @@ def rank_program(g, core, T, topo):
     ms(T.RST[:, 0:128:16], -1e20, ["RST"])
     for k in range(16):
         ts(T.REP[:, k:2048:16], T.ID[:], -1.0, None, A.mult, None, ["ID"], ["REP#%d" % k])
-    ts(T.B8[:], T.IOT[:, 0:8], PG, None, A.is_equal, None, ["IOT#0", "PF"], ["B8"])
-    ts(T.KM[:], T.IOT[:, 0:16], PK, None, A.is_equal, None, ["IOT#0", "PF"], ["KM"])
-    iota(T.C2[:], [[0, 16], [1, 16]], 0, 0, ["C2"])
-    iota(T.C6[:], [[32, 8], [0, 2], [16, 2]], W, 0, ["C6"])
-    iota(T.SO[:, 0:16], [[16, 16]], WD - 2048, 0, ["SO#0"])
-    iota(T.EC[:], [[-4096, 256]], 4096 * 256 - 8 * STEPC, 0, ["EC"])
-    for q in range(4):
-        iota(T.VT[:, 1024 * q:1024 * q + 1024], [[16, 64], [0, 16]], 1024 * q + r, 0, ["VT#%d" % q])
+    ts(T.B8[:], T.IOT[:, 0:8], -FO, PG, A.add, A.is_equal, ["IOT#0", "PF"], ["B8"])
+    ts(T.KM[:], T.IOT[:, 0:16], -FO, PK, A.add, A.is_equal, ["IOT#0", "PF"], ["KM"])
+    for name, f in (("ID16", 1.0), ("NID16", -1.0)):
+        ts(T[name][:], T.ID[:], f, None, A.mult, None, ["ID"], [name])
 
-    act(T.VB[:], T.IOT[:, 0:256], AF.Identity, ["IOT#0"], ["VB"], bias=float(r), scale=16.0)
-    for n in (256, 512, 1024, 2048, W):
-        m = min(n, WD - n)
-        act(T.IOT[:, n:n + m], T.IOT[:, 0:m], AF.Identity, ["IOT"], ["IOT#%d" % n], bias=float(n))
+    act(T.VB[:], T.IOT[:, 0:256], AF.Identity, ["IOT#0"], ["VB"], bias=r - 16 * FO, scale=16.0)
     for a in range(2):
         code(T.VC[:, a, :], T.VB[:], ["VB"], ["VC%d" % a], 8 * a)
+    for n in (256, 512, 1024):
+        act(T.IOT[:, n:2 * n], T.IOT[:, 0:n], AF.Identity, ["IOT"], ["IOT#%d" % n], bias=float(n))
 
-    for name, f in (("NID", -1.0), ("ID8K", 8192.0), ("NID4K", -4096.0), ("ID16", 1.0), ("NID16", -1.0), ("ID32", 1.0)):
-        ts(T[name][:], T.ID[:], f, None, A.mult, None, ["ID"], [name])
+    copies("fx", [(T.XR1[:, W:WD], T.BIGS[:], ["BIGS"], "XR1#d"), (T.YX[:, 512:768], T.BIGS[:], ["BIGS"], "YX#d"),
+                  (T.MF[:, W:WD], T.ZERO[:], ["ZERO"], "MFd"), (T.XR0[:, W:WD], T.BIGS[:], ["BIGS"], "XR0#d")] +
+           [(T.DK16[:, 128 * k:128 * k + 128], T.ID16[:], ["ID16"], "DK16") for k in range(16)])
+    copies("ff0", [(T.FT[:, 0:2048], T.IOT[:, 0:2048], ["IOT#0", "IOT#256", "IOT#512", "IOT#1024"], "FT#0")])
+    copies("fr", [(T.XR0[:, 0:W], T.XR1[:, 0:W], ["XR1#x"], "XR0#x")])
+
     ts(T.B8E[:], T.B8[:], 2.0 ** 28, None, A.mult, None, ["B8"], ["B8E"])
     ts(T.B8A[:], T.B8[:], -2.0 ** 16, None, A.mult, None, ["B8"], ["B8A"])
     ts(T.WP[:], T.C4[:], PG, -2.0 ** 37, A.is_equal, A.mult, ["C4", "PF"], ["WP"])
     ts(T.BLK[:], T.C4[:], PG, None, A.is_equal, None, ["C4", "PF"], ["BLK"])
-    ts(T.QW[:], T.IOT[:, 0:240], -112.0, PK, A.add, A.is_equal, ["IOT#0", "PF"], ["QW"])
+    ts(T.QW[:], T.IOT[:, 0:240], -112.0 - FO, PK, A.add, A.is_equal, ["IOT#0", "PF"], ["QW"])
     ts(T.PERM[:], T.C5[:], T.PF[:, 2:3], None, A.is_equal, None, ["C5", "PF"], ["PERM"])
     ts(T.PERMB[:], T.C5[:], T.PF[:, 2:3], 2.0 ** 37, A.is_equal, A.mult, ["C5", "PF"], ["PERMB"])
-    for k in range(16):
-        ts(T.DK16[:, 128 * k:128 * k + 128], T.ID[:], T.KM[:, k:k + 1], None, A.mult, None, ["ID", "KM"],
-           ["DK16#%d" % k])
-    ts(T.STEP[:, 0:16], T.KM[:], 2 * B2, None, A.mult, None, ["KM"], ["STEP"])
-    ts(T.STEP[:, 50:66], T.KM[:], 2 * B2, None, A.mult, None, ["KM"], ["STEP"])
-    ms(T.STEP[:, 32:67:34], -2 * B2, ["STEP"])
-    ms(T.STEP[:, 33:34], -4 * B2, ["STEP"])
+    ts(T.STEP[:, 0:16], T.KM[:], 2 * B2, None, A.mult, None, ["KM"], ["STEP#a"])
+    ts(T.STEP[:, 50:66], T.KM[:], 2 * B2, None, A.mult, None, ["KM"], ["STEP#b"])
+    ms(T.STEP[:, 32:67:34], -2 * B2, ["STEP#c"])
+    ms(T.STEP[:, 33:34], -4 * B2, ["STEP#d"])
     ms(T.EE[:, 0, 256:257], -8.0 * STEPC, ["EE#s"])
     ms(T.OFS[:, 0:1], 8.0 * STEPC, ["OFS#0"])
     ms(T.OFS[:, 1:2], -8.0 * STEPC, ["OFS#1"])
     ts(T.CT[:, 0:1], PK, 8.0, -1.0 * STEPC, A.add, A.mult, ["PF"], ["CT#i"])
-    ts(T.S1[:], T.C2[:], PK, -1.0, A.is_lt, A.mult, ["C2", "PF"], ["S1"])
-    ts(T.S2[:], T.C2[:], PK, None, A.is_equal, None, ["C2", "PF"], ["S2"])
-    tt(T.SCN[:], T.S1[:], T.S2[:], A.add, ["S1", "S2"], ["SCN"])
-    ts(T.DUM[:], T.C6[:], PK, None, A.add, None, ["C6", "PF"], ["DUM"])
-    ts(T.DUM2[:], T.C6[:], PK, 2.0, A.add, A.mult, ["C6", "PF"], ["DUM2"])
-    ts(T.DUL[:], T.SO[:, 0:16], PK, None, A.add, None, ["SO#0", "PF"], ["DUL"])
-    for k in range(16):
-        ts(T.KB[:, 8 * k:8 * k + 8], T.B8[:], T.KM[:, k:k + 1], None, A.mult, None, ["B8", "KM"], ["KB#%d" % k])
-    ts(T.SCN[:, 15:256:16], T.SCN[:, 15:256:16], -3.0, None, A.add, None, ["SCN"], ["SCN"])
+    ts(T.S1[:, 0:16], T.IOT[:, 0:16], -FO, PK, A.add, A.is_lt, ["IOT#0", "PF"], ["S1"])
+    tt(T.SCN[:, 0:16], T.KM[:], T.S1[:, 0:16], A.subtract, ["S1", "KM"], ["SCN"])
+    for name, f in (("NID", -1.0), ("ID8K", 8192.0), ("NID4K", -4096.0), ("ID32", 1.0)):
+        ts(T[name][:], T.ID[:], f, None, A.mult, None, ["ID"], [name])
+    ts(T.SCN[:, 15:16], T.SCN[:, 15:16], -3.0, None, A.add, None, ["SCN"], ["SCN"])
 
     xtrans(0, raw(0), ["XR1#x"], "D4")
     for j in range(5):
@@ -441,6 +440,7 @@ def rank_program(g, core, T, topo):
     for q in range(3):
         cp(T.OLD0[:, 64 * q:64 * q + 64], T.MW[:, 1024 * q + r:1024 * q + 1024:16], ["MW#%d" % q],
            ks("OLD0", 2 * q, 2 * q + 2))
+        cp(T.SCN[:, 16 << q:32 << q], T.SCN[:, 0:16 << q], ["SCN"], ["SCN"])
         gx(0, 2 * q)
         dmm(0, 2 * q)
         table0(q)
@@ -450,6 +450,8 @@ def rank_program(g, core, T, topo):
         dmm(0, 2 * q + 1)
         ab(2 * q, 0)
         ab(2 * q + 1, 0)
+    cp(T.SCN[:, 128:256], T.SCN[:, 0:128], ["SCN"], ["SCN"])
+    cp(T.OLD1[:], T.MW[:, 8 + r:2048:16], ["MW#0", "MW#1"], ["OLD1"])
     offer(0, 0, 192)
     table0(3)
     cp(T.OLD0[:, 192:256], T.MW[:, 3072 + r:W:16], ["MW#3"], ks("OLD0", 6, 8))
@@ -457,17 +459,23 @@ def rank_program(g, core, T, topo):
     op("g", lambda: g.partition_broadcast(T.THB[:], T.THR[0:1, :], 128), ["THR"], ["THB"])
     eq(0, 0, 2)
     block0(3)
-    for j in (6, 7):
-        gx(0, j)
-        dmm(0, j)
     pen(0, 0)
     pen(0, 1)
     names(0)
     score("AB", 0, 4)
+    for j in (6, 7):
+        gx(0, j)
+        dmm(0, j)
     ab(6, 0)
     ab(7, 0)
-    for b in range(4):
-        iota(T.FT[:, 1024 * b:1024 * b + 1024], [[1, 1024]], 1024 * b + int(FO), 0, ["FT#%d" % b])
+    iota(T.EC[:], [[-4096, 256]], 4096 * 256 - 8 * STEPC - int(FO), 0, ["EC"])
+    for n0, n1, k in ((2048, 3328, "1"), (3328, WD, "2")):
+        iota(T.IOT[:, n0:n1], [[1, n1 - n0]], n0 + int(FO), 0, ["IOT#b" + k])
+        copies("ff" + k, [(T.FT[:, n0:n1], T.IOT[:, n0:n1], ["IOT#b" + k], "FT#" + k)])
+    iota(T.C6[:], [[32, 8], [0, 2], [16, 2]], W, 0, ["C6"])
+    iota(T.SO[:, 0:16], [[16, 16]], WD - 2048, 0, ["SO#0"])
+    select(T.KB[:], T.ONE32[:], [[-1, 16], [-16, 8]], 0, 1, ["ONE32"], ["KB"])
+    picks(0)
     eq(0, 2, 4)
     score("EQ", 0, 4, True)
     eq(0, 4, 7)
@@ -478,14 +486,10 @@ def rank_program(g, core, T, topo):
     best(0)
     op("v", lambda: V.tensor_reduce(T.THC[:, 0:1], T.TV[:, 0:8], AxisListType.X, A.add), ["TV#0"], ["THC"])
     score("EQ", 7, 8, True)
-    ts(T.BIAS[:, 0:5:4], T.ZERO[:, 0:2], T.THC[:, 0:1], -64.0, A.subtract, A.add, ["THC", "ZERO"], ["BIAS#0", "BIAS#4"])
-    act(T.FT[:, W:WD], T.IOT[:, W:WD], AF.Copy, ["IOT"], ["FT#d"])
     act(xl(0), lanes(T.XR1, 0), AF.Copy, ["XR1#x"], ["XL1"])
-    for j in range(8):
-        act(T.XR0[:, j:W:16], T.XR1[:, j:W:16], AF.Copy, ["XR1#x"], ["XR0#%d" % j])
     act(xl(1), lanes(T.XR1, 1), AF.Copy, ["XR1#x"], ["XL0"])
     xtrans(1, raw(1), ["XR1#x"], "D1")
-    table1(0, 192, range(6))
+    table1(0, 192)
 
     for t in range(3):
         a = t % 2
@@ -503,14 +507,24 @@ def rank_program(g, core, T, topo):
         for c in range(8):
             ts(T.RX[:, :, :, c], T.CN[:], -2048.0, T.B8[:, c:c + 1], A.add, A.mult, ["CN", "B8"], ["RX#%d" % c])
         for gg in range(8):
-            mm(T.PS[:, 0:48], T.QW[:, 112 - 16 * gg:240 - 16 * gg], T.RX[:, :, gg, :], gg == 0, gg == 7,
-               ["QW", "RX"], ["PS"])
-        if t > 0:
-            pi(1)
+            mm(T.PS[32 * (gg // 2):32 * (gg // 2) + 32, 0:48], T.QW[:, 112 - 16 * (gg % 2):144 - 16 * (gg % 2)],
+               T.RX[:, :, gg, :], gg % 2 == 0, gg % 2 == 1, ["QW", "RX"], ["PS"])
+        if t == 0:
+            ts(T.O161[:], lanes(T.MW, 1), -2048.0, None, A.add, None, ["MW"], ["O161"])
+            ts(T.BIAS[:, 0:5:4], T.ZERO[:, 0:2], T.THC[:, 0:1], -64.0 - FO, A.subtract, A.add, ["THC", "ZERO"],
+               ["BIAS#0", "BIAS#4"])
         chores = [lambda: ts(T.SO[:, 0:16], T.PS[:, 16:32], 40.0 - 2048.0, 1e4, A.is_lt, A.mult, ["PS"], ["SO#0"]),
                   lambda: tt(T.SO[:, 16:32], T.PS[:, 0:16], T.SO[:, 0:16], A.add, ["PS", "SO#0"], ["SO#1"]),
                   lambda: tt(T.SO[:, 32:48], T.SO[:, 16:32], T.DUL[:], A.min, ["SO#1", "DUL"], ["SO#2"]),
                   lambda: ts(T.SOF[:], T.SO[:, 32:48], 2048.0, None, A.add, None, ["SO#2"], ["SOF"])]
+        if t == 0:
+            chores = [lambda: ts(T.DUL[:], T.SO[:, 0:16], PK, None, A.add, None, ["SO#0", "PF"], ["DUL"]),
+                      lambda: ts(T.DUM[:], T.C6[:], PK, None, A.add, None, ["C6", "PF"], ["DUM"])] + chores + [
+                      lambda: ts(T.DUM2[:], T.C6[:], PK, 2.0, A.add, A.mult, ["C6", "PF"], ["DUM2"])]
+        else:
+            chores += [lambda: tt(T.TC[:, 0:16], T.RR[:, 15:256:16], T.DL[:, :, 0:2], A.mult, ["RR", "DL"], ["TC#0"]),
+                       lambda: tt(T.TC[:, 16:32], T.TC[:, 0:16], T.VP[:, :, 0:2], A.add, ["TC#0", "VP"], ["TC#1"]),
+                       lambda: cp(T.O2C[:], T.TC[:, 16:32], ["TC#1"], ["O2C"])]
 
         def chore():
             chores.pop(0)()
@@ -520,11 +534,12 @@ def rank_program(g, core, T, topo):
         ts(T.MSG[:, 0:32], T.PS[:, 0:32], 2048.0, None, A.add, None, ["PS"], ["MSG#c"])
         tt(T.EV[:], T.TBL[:, t, :].indirect(T.MSG[:, 32:48]), T.VC[:, a, :], A.is_equal, ["TBL", "MSG#p", "VC%d" % a],
            ["EV"])
-        act(T.NF[:], T.IOT[:, 0:512].indirect(T.MSG[:, 16:32]), AF.Identity, ["IOT", "MSG#c", "BIAS#0"], ["NF"],
-            bias=T.BIAS[:, 0:1])
+        act(T.NF[:], T.IOT[:, 0:512].indirect(T.MSG[:, 16:32]), AF.Identity, ["IOT#0", "IOT#256", "MSG#c", "BIAS#0"],
+            ["NF"], bias=T.BIAS[:, 0:1])
         mms("PA", lo, [("BLK", T.EV[:], ["EV"]), ("ID", T.NF[:], ["NF"])])
         tt(T.EE[:, 0, 0:256], T.IOT[:, 0:W].indirect(T.MSG[:, 0:16]), T.EC[:], A.add, ["IOT", "MSG#c", "EC"], ["EE#e"])
         act(T.EE[:, 1, 0:257], T.EE[:, 0, 0:257], AF.Identity, ["EE#e", "EE#s"], ["EE#f"], bias=16.0 * STEPC)
+        chore()
         ts(T.S2[:], T.PA[:, lo], 0.0, 1.0 * STEPC, A.is_ge, A.mult, ["PA"], ["S2"])
         chore()
         scan(T.CT[:, 1:257], T.ZERO[:], T.S2[:], T.CT[:, 0:1], A.add, A.add, ["ZERO", "S2", "CT#i"], ["CT#0"])
@@ -538,13 +553,14 @@ def rank_program(g, core, T, topo):
         ts(T.EI[:, 2:4], T.EI[:, 0:2], 4095, None, A.bitwise_and, None, ["EI#0"], ["EI#1"])
         ts(T.EI[:, 4:6], T.EI[:, 0:2], 12, None, A.arith_shift_right, None, ["EI#0"], ["EI#2"])
         cp(T.C16[:], T.EI[:, 2:4], ["EI#1"], ["C16"])
-        cp(T.CVF[:, 0:2], T.EI[:, 2:4], ["EI#1"], ["CVF#c"])
+        ts(T.CVF[:, 4:6], T.EI[:, 2:4], FO, None, A.add, None, ["EI#1"], ["CVF#f"])
         ts(T.NE[:, 0:35:34], T.EI[:, 0:2], 4096.0, B2, A.is_lt, A.mult, ["EI#0"], ["NE#e"])
         for c in range(2):
-            ts(T.NE[:, 1 + 34 * c:33 + 34 * c], T.IOT[:, 0:W].indirect(T.C16[:]), T.CVF[:, c:c + 1], B2,
-               A.is_equal, A.mult, ["IOT", "C16", "CVF#c"], ["NE#%d" % c])
+            ts(T.NE[:, 1 + 34 * c:33 + 34 * c], T.IOT[:, 0:W].indirect(T.C16[:]), T.CVF[:, 4 + c:5 + c], B2,
+               A.is_equal, A.mult, ["IOT", "C16", "CVF#f"], ["NE#%d" % c])
         ts(T.CVF[:, 2:4], T.EI[:, 4:6], -16.0, float(W + 8 * a + r), A.mult, A.add, ["EI#2"], ["CVF#v"])
         scan(T.NS[:, 0:67], T.NE[:, 0:67], T.STEP[:, 0:67], 0.0, A.max, A.add, ["STEP", "NE"], ["NS"])
+        cp(T.CVF[:, 0:2], T.EI[:, 2:4], ["EI#1"], ["CVF#c"])
         for c in range(2):
             ts(ALL[:, r, c:4:2], T.CVF[:, c:4:2], T.NS[:, 32 + 34 * c:33 + 34 * c], T.DUM[:, r, c:c + 1],
                A.max, A.min, ["CVF", "NS", "DUM"], ["ALL#o%d" % c])
@@ -552,63 +568,70 @@ def rank_program(g, core, T, topo):
         mine = ["ALL#o0", "ALL#o1"]
         send(ALL[:, r, 0:4], [(c, ALL[:, r, 0:4]) for c in others], "aa%d" % t, mine)
         lands("aa%d" % t, sum(share(c, [d for d in cores if d != c]) for c in others), ["ALL#r"])
+        while chores:
+            chore()
+        if t == 0:
+            order("g", ["XR0#x"], [])
+            for j in range(8, 16):
+                iota(T.XR0[:, j:W:16], [[0, 256]], int(BIG), 0, ["XR0#%d" % j])
 
         if t > 0:
             mms("D1", lo, [("ID", T.UU[:, lo], ["UU"]), ("ID", T.UU[:, hi], ["UU"])])
         if t == 1:
             mms("D2", lo, [("ID16", T.M16[:], ["M16"])])
-            act(lanes(T.MF, 1), T.D2[:, lo], AF.Identity, ["D2"], ["MF"], bias=2048.0)
+            act(lanes(T.MF, 1), T.D2[:, lo], AF.Identity, ["D2"], ["MF"], bias=2040.0)
             act(xl(0), T.D1[:, lo], AF.Copy, ["D1"], ["XL1"])
         if t == 0:
             minus(1, (2, 4))
         act(T.XC[:], XR[1 - a][:].indirect(T.SOF[:]), AF.Copy, [XK[1 - a], XLK[1 - a], "SOF"], ["XC"])
         mms("D0", lo, [("ID", xl(a), [XLK[1 - a]]), ("ID", T.XC[:], ["XC"])])
         if t == 0:
-            ts(T.O161[:], lanes(T.MW, 1), -2048.0, None, A.add, None, ["MW"], ["O161"])
             mfloat(3)
-        if t < 2:
-            bylane(1 - a, 0)
-        if t > 0:
+            bylane(1, 0)
+            bylane(0, 0)
+        else:
             mms("D4", lo, [("ID16", T.M16[:], ["M16"]), ("NID4K", T.PVN[:], ["PVN"]), ("ID32", T.RY[:], ["RY"])])
         if t == 2:
             act(T.YX[:, 1:512:2], T.D1[:, lo], AF.Copy, ["D1"], ["YX#b"])
         act(T.T1[:], T.D0[:, lo], AF.Identity, ["D0"], ["T1"], bias=RND, scale=0.5 - 2.0 ** -13)
         if t < 2:
-            act(lanes(XR[a], a), T.T1[:], AF.Identity, ["T1"], [XK[a]], bias=-RND)
+            act(lanes(XR[a], a), T.T1[:], AF.Identity, ["T1"], [("XR0#x", "XR1")[a]], bias=-RND)
             act(T["SM%d" % t][:], T.T1[:], AF.Identity, ["T1"], ["SM%d" % t], bias=-RND)
         else:
             act(T.YX[:, 0:512:2], T.T1[:], AF.Identity, ["T1"], ["YX#a"], bias=-RND)
         if t == 0:
             xtrans(2, [T.SM0[:, 0:128], T.SM0[:, 128:256]], ["SM0"], "D2")
-        if t > 0:
+        else:
             act(T.YM[:, a:512:2], T.D4[:, lo], AF.Identity, ["D4"], ["YM#%d" % a], bias=2048.0)
         if t < 2:
             act(T.PB[:, hi], T.VB[:], AF.Identity, ["VB"], ["PB"], bias=8.0 * (1 - a) + FO)
             if t == 0:
-                table1(0, 192, (6, 7))
+                bylane(1, 1)
+                bylane(0, 1)
             else:
                 minus(2, (0, 1))
-            bylane(1 - a, 1)
             for j in [j for j in range(8) if j not in XV][4::-1]:
                 pre(t + 1, j)
         if t == 1:
             wait("s", "left", total["left"])
-            code(T.TBS[:, 0, r:2048:8], lanes(T.MF, 1), ["MF"], ["TBS0"])
+            code(T.TBS[:, 0, r:2048:8], lanes(T.MF, 1), ["MF"], ["TBS0"], 8)
             order("g", ["ALL"], [])
             offer(2)
 
         if t == 0:
-            cp(T.OLD1[:], T.MW[:, 8 + r:2048:16], ["MW"], ["OLD1"])
-            again(0)
-            again(1)
+            for i in range(1, 4):
+                picks(i)
         elif t == 1:
+            pi(1)
             pi(2)
             pi(3)
+            cp(lanes(T.MW, 1), T.OFF[:], ["OFF"], ["MW"])
             cp(T.XR1[:, 0:WD].indirect(T.O2C[:]), T.BIGS[:], ["O2C", "BIGS"], ["XR1"])
         else:
             dma("y", "out", lambda: g.sync.dma_start(T.ym[:], T.YM[:]), ["YM"], [])
             ts(T.OI[:, 0:2], ALL[:, r, 2:4], 1 / 16.0, 255.0, A.mult, A.min, mine, ["OI"])
             ts(T.TV[:, 0:2], ALL[:, r, 2:4], 0.125, -r / 8.0, A.mult, A.add, mine, ["TV#0"])
+            pi(1)
             pi(2)
             for c in range(2):
                 ts(T.OI[:, 2 + c:3 + c], ALL[:, r, 2 + c:3 + c], 512.0 - W, T.TV[:, c:c + 1], A.add, A.max,
@@ -623,29 +646,30 @@ def rank_program(g, core, T, topo):
         fill = [lambda: cp(T.CVL[:, 0:16], ALL[:, :, 0:2], ["ALL"], ["CVL#c"]),
                 lambda: cp(T.CVL[:, 16:32], ALL[:, :, 2:4], ["ALL"], ["CVL#v"])]
         if t < 2:
-            fill += [lambda: bylane(1 - a, 2),
-                     lambda: cp(T.VCF[:], ALL[:, :, 0:4], ["ALL"], ["VCF"]),
+            fill += [lambda: cp(T.VCF[:], ALL[:, :, 0:4], ["ALL"], ["VCF"]),
                      lambda: tt(T.DL[:], T.DUM[:], T.VCF[:], A.subtract, ["DUM", "VCF"], ["DL"]),
                      lambda: tt(T.VP[:], T.DUM2[:], T.VCF[:], A.subtract, ["DUM2", "VCF"], ["VP"])]
+        if t == 0:
+            fill += [lambda: ms(T.PI[:, 0:256], -1.0, ["PI"]), lambda: bylane(1, 2), lambda: bylane(0, 2)]
         for p in range(N - 1, -1, -1):
             c = slice(32 * p, 32 * p + 32)
             act(T.VALV[:, c], src[:].indirect(ALL[:, p, 2:4]), AF.Identity, sk + ["ALL"], ["VALV#%d" % p],
-                bias=FO + (p + 1) / 128.0 if t < 2 else 0.0)
+                bias=FO + 8 + (p + 1) / 128.0 if t < 2 else -FO)
             if fill:
                 fill.pop(0)()
             cp(own[:].indirect(ALL[:, p, 0:2]), T.VALV[:, c], ["ALL", "VALV#%d" % p], [ok])
         act(T.VALC[:], src[:].indirect(T.CVL[:, 0:16]), AF.Identity, sk + ["CVL#c"], ["VALC"],
-            bias=FO + 1 / 16.0 if t < 2 else 0.0)
+            bias=FO + 8 + 1 / 16.0 if t < 2 else -FO)
         if t < 2:
-            act(T.PV[:], T.IOT[:].indirect(T.CVL[:]), AF.Copy, ["IOT", "CVL"], ["PV"])
+            act(T.PV[:], T.IOT[:].indirect(T.CVL[:]), AF.Identity, ["IOT", "CVL"], ["PV"], bias=-FO)
         else:
             act(T.D0[:, lo], T.VALC[:], AF.Identity, ["VALC"], ["D0"], bias=1.0)
         if t == 0:
             table1(192, 256)
             offer(1)
-            again(2)
-            again(3)
-            iota(T.PI[:], [[0, WD]], -1, 0, ["PI"])
+            copies("fp", [(T.PI[:, 256:512], T.PI[:, 0:256], ["PI"], "PI"), (T.PI[:, W:WD], T.PI[:, 0:256], ["PI"], "PI")])
+            for n in (512, 1024, 2048):
+                copies("fp", [(T.PI[:, n:2 * n], T.PI[:, 0:n], ["PI"], "PI")])
         tt(T.S1[:], own[:].indirect(T.CVL[:, 0:16]), T.VALV[:], A.not_equal, [ok, "CVL#c", "VALV"], ["S1"])
         if t == 2:
             tt(T.OX[:, 96:128], T.S1[:, 32 * r:32 * r + 32], T.OX[:, 64:96], A.mult, ["S1", "OX#2"], ["OX#3"])
@@ -687,14 +711,16 @@ def rank_program(g, core, T, topo):
             cp(T.L16[:], T.PS[:, 0:128], ["PS"], ["L16"])
             mm(T[bk][:, 0:128], T.L16[:], T.ID16[:], True, True, ["L16", "ID16"], [bk])
 
-        def xv(j):
+        def xv(j, n0=0, n1=32):
             i = XV.index(j)
-            tt(T.GX[:, 512 * j:512 * j + 512], XR[1 - u % 2][:, 0:W].indirect(T.OFF[:, 32 * j:32 * j + 32]),
-               T.XRP[:, 512 * i:512 * i + 512], A.add, [XK[1 - u % 2], "OFF#%d" % j, "XRP#%d" % j], ["GX#%d" % j])
+            tt(T.GX[:, 512 * j + 16 * n0:512 * j + 16 * n1],
+               XR[1 - u % 2][:, 0:W].indirect(T.OFF[:, 32 * j + n0:32 * j + n1]),
+               T.XRP[:, 512 * i + 16 * n0:512 * i + 16 * n1], A.add, [XK[1 - u % 2], "OFF#%d" % j, "XRP#%d" % j],
+               ["GX#%d" % j if n0 == 0 else "GY"])
 
-        def abv(j):
-            c = slice(512 * j, 512 * j + 512)
-            act(T.AB[:, c], T.GX[:, c], AF.Abs, ["GX#%d" % j], ["AB#%d" % j])
+        def abv(j, n0=0, n1=32):
+            c = slice(512 * j + 16 * n0, 512 * j + 16 * n1)
+            act(T.AB[:, c], T.GX[:, c], AF.Abs, ["GX#%d" % j if n0 == 0 else "GY"], ["AB#%d" % j])
 
         def offs(j0, j1, bk):
             ts(T.OFF[:, 32 * j0:32 * j1], T[bk][:, 0:32 * (j1 - j0)], 2048.0, None, A.add, None, [bk],
@@ -704,33 +730,11 @@ def rank_program(g, core, T, topo):
             gx(u, j)
             dmm(u, j)
 
-        def won():
-            op("s", lambda: S.activation(T.TC[:, 32:48], T.TV[:, 16:32], AF.Sign, bias=T.BIAS[:, 10:11], scale=-1.0,
-                                         accum_out=T.AC[:, 0:1]), ["TV#1", "BIAS#10"], ["WON", "AC"])
-
-        def partners(step):
-            if step == 0:
-                tt(T.TC[:, 0:16], T.RR[:, 15:256:16], T.DL[:, :, 0:2], A.mult, ["RR", "DL"], ["TC#0"])
-            elif step == 1:
-                tt(T.TC[:, 16:32], T.TC[:, 0:16], T.VP[:, :, 0:2], A.add, ["TC#0", "VP"], ["TC#1"])
-            else:
-                cp(T.O2C[:], T.TC[:, 16:32], ["TC#1"], ["O2C"])
-
         def pvn():
             tt(T.PVN[:], lanes(T.FT, u % 2), T.PB[:, hi], A.not_equal, ["FT", "PB"], ["PVN"])
 
         def m16():
             ts(T.M16[:], T.OFF[:], -2048.0, None, A.add, None, ["OFF"], ["M16"])
-
-        def count(step):
-            if step == 0:
-                mm(T.PS[:, 256:257], T.ONE32[:], T.AC[:, 0:1], True, True, ["ONE32", "AC"], ["PS"])
-            elif step == 1:
-                ts(T.AI[:, 0:1], T.PS[:, 256:257], 0.5, 1024.0, A.mult, A.add, ["PS"], ["AI#0"])
-            elif step == 2:
-                ts(T.AI[:, 1:2], T.AI[:, 0:1], 3, None, A.bitwise_and, None, ["AI#0"], ["AI#1"])
-            else:
-                ts(T.BIAS[:, 0:1], T.AI[:, 1:2], -1.0, T.BIAS[:, 4:5], A.mult, A.add, ["AI#1", "BIAS#4"], ["BIAS#0"])
 
         follow(0, 2)
         for k0, k1 in ((0, 2), (2, 6)):
@@ -742,34 +746,27 @@ def rank_program(g, core, T, topo):
         follow(2, 3)
         keepl(6, 11)
         follows(11, 16)
-        partners(0)
         offs(0, 2, "PA")
         follow(3, 4)
         keepl(11, 13)
         keep(2, 4, "PB")
         keepl(13, 16)
-        won()
-        count(0)
         gx(u, 0)
         xv(1)
         dmm(u, 0)
-        partners(1)
         offs(2, 4, "PB")
-        partners(2)
-        turn("PA")
-        count(1)
-        abv(1)
         eq(u, 0, 1)
+        turn("PA")
+        abv(1)
+        eq(u, 1, 2)
         offs(4, 8, "PA")
-        count(2)
         m16()
-        count(3)
         x(2)
         ab(0)
         pen(u, 0)
         pen(u, 1)
         names(u)
-        eq(u, 1, 4)
+        eq(u, 2, 4)
         x(3)
         ab(2)
         x(4)
@@ -781,13 +778,23 @@ def rank_program(g, core, T, topo):
         eq(u, 4, 8)
         x(6)
         ab(5)
-        xv(7)
+        xv(7, 0, 20)
+        xv(7, 20, 32)
         score("EQ", 4, 8)
         ab(6)
         score("AB", 4, 7, True)
-        abv(7)
+        abv(7, 0, 20)
+        abv(7, 20, 32)
         best(0)
         score("AB", 7, 8, True)
+        op("s", lambda: S.activation(T.TC[:, 32:48], T.TV[:, 16:32], AF.Sign, bias=T.BIAS[:, 10:11], scale=-1.0,
+                                     accum_out=T.AC[:, 0:1]), ["TV#1", "BIAS#10"], ["WON", "AC#0"])
+        mm(T.D0[:, 0:1], T.ONE32[:], T.AC[:, 0:1], True, True, ["ONE32", "AC#0"], ["D0"])
+        act(T.AC[:, 1:2], T.D0[:, 0:1], AF.Identity, ["D0", "BIAS#4"], ["AC#1"], bias=T.BIAS[:, 4:5], scale=-0.5)
+        act(T.AC[:, 2:3], T.D0[:, 0:1], AF.Identity, ["D0"], ["AC#2"], bias=-3.0)
+        act(T.AC[:, 3:4], T.AC[:, 2:3], AF.Identity, ["AC#2"], ["AC#3"], bias=RND, scale=0.125)
+        act(T.AC[:, 2:3], T.AC[:, 3:4], AF.Identity, ["AC#3"], ["AC#2"], bias=-RND)
+        act(T.BIAS[:, 0:1], T.AC[:, 2:3], AF.Identity, ["AC#1", "AC#2"], ["BIAS#0"], bias=T.AC[:, 1:2], scale=4.0)
         if u == 1:
             for j in range(8):
                 iota(T.XR1[:, j:W:16], [[0, 256]], int(BIG), 0, ["XR1"] if j == 0 else ["XR1#%d" % j])

from concourse.bass import DstId, RemoteDMATransfer
from concourse.mybir import AluOpType as A, AxisListType, ActivationFunctionType as AF

W = 4096
WD = 4352
WX = 4608
BIG = 16384.0
FO = 32.0
STEPC = 4096 * 257
B2 = 8192.0
RND = 12582912.0
F32, BF, F16, I32, U16 = "float32", "bfloat16", "float16", "int32", "uint16"


def sb(cols, dtype):
    return ("sbuf", [128] + (cols if isinstance(cols, list) else [cols]), dtype)


SCRATCH = {
    "MW": sb(W, I32), "MF": sb(WD, F32),
    "FT": sb(WD, F32), "IOT": sb(WD, F32), "PI": sb(WD, F32), "VT": sb(W, F32),
    "XR0": sb(WX, BF), "XR1": sb(WX, BF), "G16": sb(2048, F16), "G32": sb(2048, F32),
    "EQ": sb(W, BF), "GX": sb(W, BF), "AB": sb(W, BF),
    "REP": sb(2048, BF), "DK16": sb(2048, F16), "KB": sb(128, F32), "XRP": sb(1024, BF),
    "OFF": sb(256, U16), "M16": sb(256, F16), "OLD0": sb(256, U16), "OLD1": sb(128, U16), "OLDT": sb([2, 128], U16),
    "O160": sb(256, F16), "O161": sb(256, F16), "CLS": sb(256, I32), "NCL": sb(256, BF),
    "XT": sb([3, 256], BF),
    "SM0": sb(256, BF), "SM1": sb(256, BF), "XC": sb(256, BF), "T1": sb(256, F32), "UU": sb(512, BF), "RY": sb(256, F32),
    "YX": sb(768, BF), "YM": sb(512, F32), "OX": sb(128, BF), "OI": sb(4, U16),
    "VALV": sb(256, F32), "VALC": sb(256, F32), "PV": sb(512, F32),
    "ID": sb(128, BF), "NID": sb(128, BF), "ID8K": sb(128, BF), "NID4K": sb(128, BF),
    "ID16": sb(128, F16), "NID16": sb(128, F16), "ID32": sb(128, F32),
    "ONES": sb(128, BF), "ONE32": sb(128, F32),
    "BLK": sb(128, BF), "WP": sb(128, BF), "PERM": sb(128, F16), "PERMB": sb(128, BF),
    "KC": sb(128, BF), "QW": sb(240, F16),
    "B8": sb(8, F32), "B8E": sb(8, BF), "B8A": sb(8, BF),
    "KM": sb(16, F32), "PIDX": sb(4, I32), "PF": sb(4, F32),
    "C4": sb(128, F32), "C5": sb(128, F32), "C6": sb([8, 4], F32), "L16": sb(128, F16),
    "VB": sb(256, F32), "VC": sb([2, 256], BF),
    "RST": sb(128, F32), "ZERO": sb(256, F32), "SCN": sb(256, F32), "EC": sb(256, F32), "BIGS": sb(256, BF),
    "DUM": sb([8, 4], F32), "DUM2": sb([8, 4], F32), "DUL": sb(16, F32), "STEP": sb(68, F32), "OFS": sb(2, F32),
    "THR": sb(8, I32), "THB": sb(8, I32), "THC": sb(4, F32), "BIAS": sb(16, F32),
    "PVN": sb(256, BF), "S1": sb(256, F32), "S2": sb(256, F32), "S3": sb(256, F32), "RR": sb(256, F32),
    "CI": sb(32, I32), "CN": sb(48, I32), "RX": sb([6, 8, 8], F16), "MSG": sb(48, U16),
    "TBL": sb([3, 2048], BF), "TBS": sb([2, 2048], BF),
    "ALL0": sb([8, 8], U16), "ALL1": sb([8, 8], U16), "ALL2": sb([8, 8], U16),
    "EV": sb(256, BF), "NF": sb(256, BF), "EE": sb([2, 260], F32), "CT": sb(260, F32), "SC": sb([2, 260], F32),
    "EI": sb(8, I32), "C16": sb(2, U16), "CVF": sb(6, F32), "NE": sb(68, F32), "NS": sb(68, F32),
    "CVL": sb(32, U16), "VCF": sb([8, 4], F32), "DL": sb([8, 4], F32), "VP": sb([8, 4], F32),
    "TV": sb(32, F32), "TC": sb(48, F32), "O2V": sb(16, U16), "O2C": sb(16, U16),
    "AC": sb(4, F32), "SO": sb(48, F32), "SOF": sb(16, U16),
}
PSUM = ("D0", "D1", "D2", "D3", "D4", "PS", "PA", "PB")
SCRATCH.update({n: ("psum", [128, 512], F32) for n in PSUM})
SEMAPHORES = ["qv", "qs", "qp", "qg", "lx", "lm0", "lm1", "lm2", "lm3", "lth", "out", "sent", "left",
              "fx", "ff0", "ff1", "ff2", "fr", "fp", "aa0", "aa1", "aa2", "at0", "at1", "at2"]


def bits(m):
    return bin(m).count("1")


def spread(topo, src, dsts):
    far = [d for d in dsts if topo.chip(d) != topo.chip(src)]
    near = [d for d in dsts if topo.chip(d) == topo.chip(src)]
    res = []
    used = 0
    if far:
        used = topo.mask(src, far[0])
        for d in far:
            used &= topo.mask(src, d)
        res.append((used, far))
    if near:
        rest = [e for e in topo.engines(src, near[0]) if not used >> e & 1]
        if far:
            rest = rest[0:4:2]
        res.append((sum(1 << e for e in rest), near))
    return res


def rank_program(g, core, T, topo):
    r = T.rank_of(core)
    if r is None:
        return
    cores = list(T.cores)
    N = len(cores)
    eng = {"v": g.vector, "s": g.scalar, "p": g.tensor, "g": g, "y": g.sync}
    cnt = {"v": 0, "s": 0, "p": 0, "g": 0}
    seen = {q: {} for q in eng}
    wr, rd = {}, {}
    total = {}

    def wait(q, sem, val):
        if seen[q].get(sem, 0) < val:
            eng[q].wait_ge(T.sem[sem], val)
            seen[q][sem] = val

    def parts(k):
        b = k.split("#")
        return b[0], (b[1] if len(b) > 1 else None)

    def meet(table, k):
        b, p = parts(k)
        return [e for pp, es in table.get(b, {}).items() if p is None or pp is None or pp == p for e in es]

    def order(q, reads, writes):
        need = {}

        def add(e):
            need[e[1]] = max(need.get(e[1], 0), e[2])
        for k in reads:
            for e in meet(wr, k):
                add(e)
            if parts(k)[0] in PSUM:
                for e in meet(rd, parts(k)[0]) + meet(wr, parts(k)[0]):
                    if e[0] != q:
                        add(e)
        for k in writes:
            for e in meet(wr, k) + meet(rd, k):
                if not e[0] == q == "p":
                    add(e)
        for s, v in need.items():
            wait(q, s, v)

    def note(e, reads, writes):
        for k in reads:
            b, p = parts(k)
            rd.setdefault(b, {}).setdefault(p, []).append(e)
        for k in writes:
            b, p = parts(k)
            if p is None:
                wr[b], rd[b] = {None: [e]}, {}
            else:
                wr.setdefault(b, {})[p] = [e]

    def op(q, fn, reads, writes):
        order(q, reads, writes)
        cnt[q] += 1
        fn().then_inc(T.sem["q" + q], 1)
        total["q" + q] = cnt[q]
        note((q, "q" + q, cnt[q]), reads, writes)

    def dma(q, sem, fn, reads, writes):
        order(q, reads, writes)
        fn().then_inc(T.sem[sem], 16)
        total[sem] = total.get(sem, 0) + 16
        note(("d", sem, total[sem]), reads, writes)

    def lands(sem, val, keys):
        total[sem] = val
        note(("d", sem, val), [], keys)

    def copies(sem, jobs):
        for out, in_, R, Wr in jobs:
            dma("y", sem, lambda: g.sync.dma_start(out, in_), R, [])
        lands(sem, total[sem], [job[3] for job in jobs])

    V, S, P = g.vector, g.scalar, g.tensor

    def ts(out, in0, s1, s2, o0, o1, R, Wr):
        if s2 is None:
            op("v", lambda: V.tensor_scalar(out, in0, s1, None, o0), R, Wr)
        else:
            op("v", lambda: V.tensor_scalar(out, in0, s1, s2, o0, o1), R, Wr)

    def tt(out, a, b, o, R, Wr):
        op("v", lambda: V.tensor_tensor(out, a, b, o), R, Wr)

    def cp(out, a, R, Wr):
        op("v", lambda: V.tensor_copy(out, a), R, Wr)

    def ms(out, c, Wr):
        op("v", lambda: V.memset(out, c), [], Wr)

    def scan(out, d0, d1, init, o0, o1, R, Wr):
        op("v", lambda: V.tensor_tensor_scan(out, d0, d1, init, o0, o1), R, Wr)

    def act(out, a, f, R, Wr, bias=0.0, scale=1.0):
        op("s", lambda: S.activation(out, a, f, bias=bias, scale=scale), R, Wr)

    def mm(out, l, rh, st, sp, R, Wr):
        op("p", lambda: P.matmul(out, l, rh, st, sp), R, Wr)

    def mms(bank, cols, terms):
        for i, (wt, data, keys) in enumerate(terms):
            mm(T[bank][:, cols], T[wt][:], data, i == 0, i == len(terms) - 1, [wt] + keys, [bank])

    def iota(out, pat, base, cm, Wr, flag=True):
        if flag:
            op("g", lambda: g.iota(out, pat, base, cm, allow_small_or_imprecise_dtypes=True), [], Wr)
        else:
            op("g", lambda: g.iota(out, pat, base, cm), [], Wr)

    def select(out, in_, pat, base, cm, R, Wr):
        op("g", lambda: g.affine_select(out, in_, pat, A.is_equal, 0.0, base, cm), R, Wr)

    def send(src, pairs, sem, R, gone="sent"):
        order("g", R, [])
        where = dict(pairs)
        trs = []
        for m, ds in spread(topo, core, [c for c, _ in pairs]):
            ids = [DstId(rid=topo.addr(d)[0], pnc=topo.addr(d)[1]) for d in ds]
            trs.append(RemoteDMATransfer(dst_ids=ids, dma_engine_mask=m, remote_sem=T.sem[sem], srcs=[src],
                                         dsts=[where[d] for d in ds]))
            total[gone] = total.get(gone, 0) + bits(m)
        g.remote_dma_fused(trs, local_sem=T.sem[gone])

    def share(src, dsts):
        for m, ds in spread(topo, src, dsts):
            if core in ds:
                return bits(m)
        return 0

    XR = [T.XR0, T.XR1]
    XK = ["XR0", "XR1"]
    XLK = ["XL0", "XL1"]
    DB = [T.D0, T.D1, T.D2, T.D3, T.D4]
    SB = [(T.PS, "PS"), (T.PB, "PB")]
    PK, PG = T.PF[:, 0:1], T.PF[:, 1:2]
    voters = [(r + 1 + t % (N - 1)) % N for t in range(3)]
    clients = [(r - 1 - t % (N - 1)) % N for t in range(3)]
    lo, hi = slice(0, 256), slice(256, 512)
    XV = (1, 7)

    def ks(name, j0, j1):
        return ["%s#%d" % (name, j) for j in range(j0, j1)]

    def lanes(buf, a):
        return buf[:, 8 * a + r:W:16]

    def xl(a):
        return XR[1 - a][:, WD:WX]

    def xtrans(t, halves, R, bank):
        for h in range(2):
            mm(T[bank][:, 128 * h:128 * h + 128], halves[h], T.ID[:], True, True, R + ["ID"], [bank])
        act(T.XT[:, t, :], T[bank][:, lo], AF.Copy, [bank], ["XT%d" % t])

    def raw(a):
        return [T.XR1[:, 2048 * h + 8 * a + r:2048 * h + 2048:16] for h in range(2)]

    def slot(t, j):
        return j if t == 0 else len([i for i in range(j) if i not in XV])

    def pre(t, j, close=False, b=None):
        b = slot(t, j) % 5 if b is None else b
        mm(DB[b][:], T.XT[:, t, 128 * (j // 4):128 * (j // 4) + 128],
           T.REP[:, 512 * (j % 4):512 * (j % 4) + 512], True, close, ["XT%d" % t, "REP"], ["D%d" % b])

    def minus(t, banks):
        for i, (j, b) in enumerate(zip(XV, banks)):
            pre(t, j, True, b)
            act(T.XRP[:, 512 * i:512 * i + 512], DB[b][:], AF.Copy, ["D%d" % b], ["XRP#%d" % j])

    def bylane(a, step):
        b1, b2, c0 = ("D1", "D3")[a], ("PA", "PS")[a], 1024 * a
        if step == 0:
            mm(T[b1][:, 0:128], T["O16%d" % a][:, 128:256], T.ID16[:], True, True, ["O16%d" % a, "ID16"], [b1])
            for c in range(8):
                ts(T.G16[:, c0 + c:c0 + 1024:8], T[b1][:, 0:128], T.B8[:, c:c + 1], None, A.mult, None, [b1, "B8"],
                   ["RT%d#%d" % (a, c)])
        elif step == 1:
            for gg in range(8):
                mm(T[b2][:, 0:128], T.QW[:, 112 - 16 * gg:240 - 16 * gg], T.G16[:, c0 + 128 * gg:c0 + 128 * gg + 128],
                   gg == 0, gg == 7, ["QW", "RT%d" % a, "G16"], [b2])
        else:
            ts(T.OLDT[:, a, :], T[b2][:, 0:128], 2048.0, None, A.add, None, [b2], ["OLDT%d" % a])

    def names_of(t):
        return (T.OLD0, "OLD0") if t == 0 else (T.OFF, "OFF")

    def gx(t, j, q="s"):
        off, ok = names_of(t)
        xk = "XR1#x" if t == 0 else XK[1 - t % 2]
        win = XR[1 - t % 2][:, 0:W].indirect(off[:, 32 * j:32 * j + 32])
        out = T.GX[:, 512 * j:512 * j + 512]
        if q == "v":
            cp(out, win, [xk, "%s#%d" % (ok, j)], ["GX#%d" % j])
        else:
            act(out, win, AF.Copy, [xk, "%s#%d" % (ok, j)], ["GX#%d" % j])

    def dmm(t, j):
        b = slot(t, j) % 5
        if slot(t, j) >= 5:
            pre(t, j)
        mm(DB[b][:], T.ID[:], T.GX[:, 512 * j:512 * j + 512], False, True, ["ID", "GX#%d" % j], ["D%d" % b])

    def ab(j, t=1):
        b = slot(t, j) % 5
        act(T.AB[:, 512 * j:512 * j + 512], DB[b][:], AF.Abs, ["D%d" % b], ["AB#%d" % j])

    def eq(t, j0, j1):
        win, R = (T.MW[:], ["MW"]) if t % 2 == 0 else (T.MF[:, 0:W], ["MF"])
        off, ok = names_of(t)
        c = slice(512 * j0, 512 * j1)
        tt(T.EQ[:, c], win.indirect(off[:, 32 * j0:32 * j1]), T.VT[:, c], A.is_equal,
           R + ks(ok, j0, j1) + ks("VT", j0 // 2, (j1 + 1) // 2), ks("EQ", j0, j1))

    def pen(t, h):
        src, wt = ("NCL", "PERMB") if t == 0 else ("PVN", "WP")
        mm(SB[h][0][:, 0:128], T[src][:, 128 * h:128 * h + 128], T[wt][:], True, False, [src, wt], [SB[h][1]])

    def score(src, j0, j1, last=False):
        h, wt = j0 // 4, {"EQ": "B8E", "AB": "B8A"}[src]
        for k in range(16):
            mm(SB[h][0][32 * (j0 - 4 * h):32 * (j1 - 4 * h), 15 - k:128:16], T[src][:, 512 * j0 + k:512 * j1:16],
               T[wt][:], False, last and k == 15, ks(src, j0, j1) + [wt], [SB[h][1]])

    def names(t):
        src = "O160" if t == 0 else "M16"
        for h in range(2):
            mm(T.PA[:, 128 * h:128 * h + 128], T.ONES[:], T.KC[:], True, False, ["ONES", "KC"], ["PA"])
            mm(T.PA[:, 128 * h:128 * h + 128], T[src][:, 128 * h:128 * h + 128], T.PERM[:], False, True,
               [src, "PERM"], ["PA"])

    def best(h):
        c = slice(128 * h, 128 * h + 128)
        bank, bk = SB[h]
        k = "#%d" % h
        scan(T.S1[:, c], T.RST[:], bank[:, 0:128], 0.0, A.add, A.max, ["RST", bk], ["S1" + k])
        tt(T.S2[:, c], T.S1[:, c], bank[:, 0:128], A.subtract, ["S1" + k, bk], ["S2" + k])
        if h == 1:
            ts(T.CN[:, 16:32], T.S1[:, 15:256:16], 2.0 ** -28, 64.498, A.mult, A.add, ["S1"], ["CN#n"])
        scan(T.S3[:, c], T.S2[:, c], T.PA[:, c], 0.0, A.min, A.max, ["S2" + k, "PA"], ["S3" + k])
        if h == 1:
            cp(T.CI[:, 0:16], T.S3[:, 15:256:16], ["S3"], ["CI#0"])
            ts(T.CI[:, 16:32], T.CI[:, 0:16], 1, 2040, A.arith_shift_right, A.bitwise_and, ["CI#0"], ["CI#1"])
            ts(T.CN[:, 0:16], T.CI[:, 0:16], 4095, None, A.bitwise_and, None, ["CI#0"], ["CN#c"])
            tt(T.CN[:, 32:48], T.CN[:, 0:16], T.CI[:, 16:32], A.subtract, ["CN#c", "CI#1"], ["CN#p"])

    def code(out, ends, R, Wr, shift=0):
        act(out, ends, AF.Silu, R, Wr, bias=-5.0 - shift / 64.0, scale=-1 / 64.0)

    def table1(h0, h1):
        for l in range(8):
            code(T.TBS[:, 1, 8 * h0 + l:8 * h1:8], T.MF[:, 16 * h0 + l:16 * h1:16],
                 ["MF#%d" % q for q in range(h0 // 64, h1 // 64)], ["TBS1#%d.%d" % (h0, l)], 8)

    def table0(q):
        for l in range(8):
            cp(T.G32[:, 512 * q + l:512 * q + 512:8], T.MW[:, 1024 * q + 8 + l:1024 * q + 1024:16], ["MW#%d" % q],
               ["G32#%d.%d" % (q, l)])
        code(T.TBS[:, 0, 512 * q:512 * q + 512], T.G32[:, 512 * q:512 * q + 512],
             ["G32#%d.%d" % (q, l) for l in range(8)], ["TBS0#%d" % q])

    def offer(t, h0=0, h1=256):
        send(T.TBS[:, t % 2, 8 * h0:8 * h1], [(cores[clients[t]], T.TBL[:, t, 8 * h0:8 * h1])], "at%d" % t,
             ["TBS%d" % (t % 2)], "left" if t == 0 else "sent")

    def pi(i):
        off, ok = (T.O2V, "O2V") if i < 2 else (T.O2C, "O2C")
        cp(T.PI[:].indirect(off[:, 8 * (i % 2):8 * (i % 2) + 8]), T.PV[:, 128 * i:128 * i + 128], [ok, "PV"], ["PI"])

    def picks(i):
        c = slice(512 * i, 512 * i + 512)
        select(T.DK16[:, c], T.DK16[:, c], [[1, 4], [0, 8], [-1, 16]], 4 * i, 0, ["DK16#%d" % i], ["DK16#%d" % i])

    def mfloat(q):
        c = slice(1024 * q, 1024 * q + 1024)
        ts(T.MF[:, c], T.MW[:, c], -8.0, None, A.add, None, ["MW#%d" % q], ["MF#%d" % q])

    def block0(q):
        c = slice(64 * q, 64 * q + 64)
        src = T.MW[:, 1024 * q + r:1024 * q + 1024:16]
        ts(T.CLS[:, c], src, 3, 1, A.arith_shift_right, A.bitwise_and, ["MW#%d" % q], ["CLS#%d" % q])
        ts(T.O160[:, c], src, -2048.0, None, A.add, None, ["MW#%d" % q], ["O160#%d" % q])
        ts(T.NCL[:, c], T.CLS[:, c], -1.0, None, A.add, None, ["CLS#%d" % q], ["NCL#%d" % q])

    dma("y", "lx", lambda: g.sync.dma_start(T.XR1[:, 0:W], T.xv[:]), [], ["XR1#x"])
    for q in range(4):
        dma("y", "lm%d" % q, lambda q=q: g.sync.dma_start(T.MW[:, 1024 * q:1024 * q + 1024],
                                                         T.mt[:, 1024 * q:1024 * q + 1024]), [], ["MW#%d" % q])
    dma("g", "lth", lambda: g.dma_start(T.THR[0:1, 0:8], T.th[:], allow_slow_non_contiguous=True), [], ["THR"])

    ms(T.ONES[:], 1.0, ["ONES"])
    iota(T.PIDX[:, 0:1], [[1, 1]], 0, 1, ["PIDX#0"], False)
    select(T.ID[:], T.ONES[:], [[-1, 128]], 0, 1, ["ONES"], ["ID"])
    iota(T.IOT[:, 0:256], [[1, 256]], int(FO), 0, ["IOT#0"])
    iota(T.C5[:], [[16, 8], [-1, 16]], 15, 0, ["C5"])
    iota(T.C4[:], [[1, 8], [0, 16]], 0, 0, ["C4"])
    for q in range(4):
        iota(T.VT[:, 1024 * q:1024 * q + 1024], [[16, 64], [0, 16]], 1024 * q + r, 0, ["VT#%d" % q])
    iota(T.KC[:], [[0, 8], [-32, 16]], 496, 0, ["KC"])

    ts(T.PIDX[:, 1:2], T.PIDX[:, 0:1], 15, None, A.bitwise_and, None, ["PIDX#0"], ["PIDX#1"])
    ts(T.PIDX[:, 2:3], T.PIDX[:, 0:1], 4, None, A.arith_shift_right, None, ["PIDX#0"], ["PIDX#2"])
    ms(T.BIGS[:], BIG, ["BIGS"])
    ms(T.ZERO[:], 0.0, ["ZERO"])
    cp(T.PF[:, 2:3], T.PIDX[:, 0:1], ["PIDX#0"], ["PF#2"])
    cp(T.PF[:, 0:2], T.PIDX[:, 1:3], ["PIDX#1", "PIDX#2"], ["PF#0"])
    ms(T.RST[:], 0.0, ["RST"])
    ms(T.ONE32[:], 1.0, ["ONE32"])
    ms(T.STEP[:], 0.0, ["STEP"])
    ms(T.NE[:], 0.0, ["NE"])
    ms(T.BIAS[:, 10:11], W - 0.5, ["BIAS#10"])
    ms(T.RST[:, 0:128:16], -1e20, ["RST"])
    for k in range(16):
        ts(T.REP[:, k:2048:16], T.ID[:], -1.0, None, A.mult, None, ["ID"], ["REP#%d" % k])
    ts(T.B8[:], T.IOT[:, 0:8], -FO, PG, A.add, A.is_equal, ["IOT#0", "PF"], ["B8"])
    ts(T.KM[:], T.IOT[:, 0:16], -FO, PK, A.add, A.is_equal, ["IOT#0", "PF"], ["KM"])
    for name, f in (("ID16", 1.0), ("NID16", -1.0)):
        ts(T[name][:], T.ID[:], f, None, A.mult, None, ["ID"], [name])

    act(T.VB[:], T.IOT[:, 0:256], AF.Identity, ["IOT#0"], ["VB"], bias=r - 16 * FO, scale=16.0)
    for a in range(2):
        code(T.VC[:, a, :], T.VB[:], ["VB"], ["VC%d" % a], 8 * a)
    for n in (256, 512, 1024):
        act(T.IOT[:, n:2 * n], T.IOT[:, 0:n], AF.Identity, ["IOT"], ["IOT#%d" % n], bias=float(n))

    copies("fx", [(T.XR1[:, W:WD], T.BIGS[:], ["BIGS"], "XR1#d"), (T.YX[:, 512:768], T.BIGS[:], ["BIGS"], "YX#d"),
                  (T.MF[:, W:WD], T.ZERO[:], ["ZERO"], "MFd"), (T.XR0[:, W:WD], T.BIGS[:], ["BIGS"], "XR0#d")] +
           [(T.DK16[:, 128 * k:128 * k + 128], T.ID16[:], ["ID16"], "DK16") for k in range(16)])
    copies("ff0", [(T.FT[:, 0:2048], T.IOT[:, 0:2048], ["IOT#0", "IOT#256", "IOT#512", "IOT#1024"], "FT#0")])
    copies("fr", [(T.XR0[:, 0:W], T.XR1[:, 0:W], ["XR1#x"], "XR0#x")])

    ts(T.B8E[:], T.B8[:], 2.0 ** 28, None, A.mult, None, ["B8"], ["B8E"])
    ts(T.B8A[:], T.B8[:], -2.0 ** 16, None, A.mult, None, ["B8"], ["B8A"])
    ts(T.WP[:], T.C4[:], PG, -2.0 ** 37, A.is_equal, A.mult, ["C4", "PF"], ["WP"])
    ts(T.BLK[:], T.C4[:], PG, None, A.is_equal, None, ["C4", "PF"], ["BLK"])
    ts(T.QW[:], T.IOT[:, 0:240], -112.0 - FO, PK, A.add, A.is_equal, ["IOT#0", "PF"], ["QW"])
    ts(T.PERM[:], T.C5[:], T.PF[:, 2:3], None, A.is_equal, None, ["C5", "PF"], ["PERM"])
    ts(T.PERMB[:], T.C5[:], T.PF[:, 2:3], 2.0 ** 37, A.is_equal, A.mult, ["C5", "PF"], ["PERMB"])
    ts(T.STEP[:, 0:16], T.KM[:], 2 * B2, None, A.mult, None, ["KM"], ["STEP#a"])
    ts(T.STEP[:, 50:66], T.KM[:], 2 * B2, None, A.mult, None, ["KM"], ["STEP#b"])
    ms(T.STEP[:, 32:67:34], -2 * B2, ["STEP#c"])
    ms(T.STEP[:, 33:34], -4 * B2, ["STEP#d"])
    ms(T.EE[:, 0, 256:257], -8.0 * STEPC, ["EE#s"])
    ms(T.OFS[:, 0:1], 8.0 * STEPC, ["OFS#0"])
    ms(T.OFS[:, 1:2], -8.0 * STEPC, ["OFS#1"])
    ts(T.CT[:, 0:1], PK, 8.0, -1.0 * STEPC, A.add, A.mult, ["PF"], ["CT#i"])
    ts(T.S1[:, 0:16], T.IOT[:, 0:16], -FO, PK, A.add, A.is_lt, ["IOT#0", "PF"], ["S1"])
    tt(T.SCN[:, 0:16], T.KM[:], T.S1[:, 0:16], A.subtract, ["S1", "KM"], ["SCN"])
    for name, f in (("NID", -1.0), ("ID8K", 8192.0), ("NID4K", -4096.0), ("ID32", 1.0)):
        ts(T[name][:], T.ID[:], f, None, A.mult, None, ["ID"], [name])
    ts(T.SCN[:, 15:16], T.SCN[:, 15:16], -3.0, None, A.add, None, ["SCN"], ["SCN"])

    xtrans(0, raw(0), ["XR1#x"], "D4")
    for j in range(5):
        pre(0, j)
    for q in range(3):
        cp(T.OLD0[:, 64 * q:64 * q + 64], T.MW[:, 1024 * q + r:1024 * q + 1024:16], ["MW#%d" % q],
           ks("OLD0", 2 * q, 2 * q + 2))
        cp(T.SCN[:, 16 << q:32 << q], T.SCN[:, 0:16 << q], ["SCN"], ["SCN"])
        gx(0, 2 * q)
        dmm(0, 2 * q)
        table0(q)
        gx(0, 2 * q + 1, "v" if q else "s")
        block0(q)
        mfloat(q)
        dmm(0, 2 * q + 1)
        ab(2 * q, 0)
        ab(2 * q + 1, 0)
    cp(T.SCN[:, 128:256], T.SCN[:, 0:128], ["SCN"], ["SCN"])
    cp(T.OLD1[:], T.MW[:, 8 + r:2048:16], ["MW#0", "MW#1"], ["OLD1"])
    offer(0, 0, 192)
    table0(3)
    cp(T.OLD0[:, 192:256], T.MW[:, 3072 + r:W:16], ["MW#3"], ks("OLD0", 6, 8))
    offer(0, 192, 256)
    op("g", lambda: g.partition_broadcast(T.THB[:], T.THR[0:1, :], 128), ["THR"], ["THB"])
    eq(0, 0, 2)
    block0(3)
    pen(0, 0)
    pen(0, 1)
    names(0)
    score("AB", 0, 4)
    for j in (6, 7):
        gx(0, j)
        dmm(0, j)
    ab(6, 0)
    ab(7, 0)
    iota(T.EC[:], [[-4096, 256]], 4096 * 256 - 8 * STEPC - int(FO), 0, ["EC"])
    for n0, n1, k in ((2048, 3328, "1"), (3328, WD, "2")):
        iota(T.IOT[:, n0:n1], [[1, n1 - n0]], n0 + int(FO), 0, ["IOT#b" + k])
        copies("ff" + k, [(T.FT[:, n0:n1], T.IOT[:, n0:n1], ["IOT#b" + k], "FT#" + k)])
    iota(T.C6[:], [[32, 8], [0, 2], [16, 2]], W, 0, ["C6"])
    iota(T.SO[:, 0:16], [[16, 16]], WD - 2048, 0, ["SO#0"])
    select(T.KB[:], T.ONE32[:], [[-1, 16], [-16, 8]], 0, 1, ["ONE32"], ["KB"])
    picks(0)
    eq(0, 2, 4)
    score("EQ", 0, 4, True)
    eq(0, 4, 7)
    score("AB", 4, 8)
    eq(0, 7, 8)
    score("EQ", 4, 7, True)
    tt(T.TV[:, 0:8], T.THB[:], T.B8[:], A.mult, ["THB", "B8"], ["TV#0"])
    best(0)
    op("v", lambda: V.tensor_reduce(T.THC[:, 0:1], T.TV[:, 0:8], AxisListType.X, A.add), ["TV#0"], ["THC"])
    score("EQ", 7, 8, True)
    act(xl(0), lanes(T.XR1, 0), AF.Copy, ["XR1#x"], ["XL1"])
    act(xl(1), lanes(T.XR1, 1), AF.Copy, ["XR1#x"], ["XL0"])
    xtrans(1, raw(1), ["XR1#x"], "D1")
    table1(0, 192)

    for t in range(3):
        a = t % 2
        ALL = T["ALL%d" % t]
        if t > 0:
            SMo, so, xo = T["SM%d" % (t - 1)], "SM%d" % (t - 1), lanes(XR[1 - a], 1 - a)
            mms("D1", lo, [("ID", xl(1 - a), [XLK[a]]), ("ID", xo, [XK[1 - a]]), ("NID", T.BIGS[:], ["BIGS"])])
            mms("D1", hi, [("ID", SMo[:], [so]), ("ID", SMo[:], [so]), ("NID", xo, [XK[1 - a]])])
            o16 = "O16%d" % a
            mms("D3", lo, [("ID16", T[o16][:], [o16]), ("NID16", T.M16[:], ["M16"]), ("ID8K", T.PVN[:], ["PVN"])])
            act(T.UU[:], T.D1[:], AF.Relu, ["D1"], ["UU"])
            act(T.RY[:], T.D3[:, lo], AF.Relu, ["D3"], ["RY"], bias=-4096.0)
            pi(0)
        best(1)
        for c in range(8):
            ts(T.RX[:, :, :, c], T.CN[:], -2048.0, T.B8[:, c:c + 1], A.add, A.mult, ["CN", "B8"], ["RX#%d" % c])
        for gg in range(8):
            mm(T.PS[32 * (gg // 2):32 * (gg // 2) + 32, 0:48], T.QW[:, 112 - 16 * (gg % 2):144 - 16 * (gg % 2)],
               T.RX[:, :, gg, :], gg % 2 == 0, gg % 2 == 1, ["QW", "RX"], ["PS"])
        if t == 0:
            ts(T.O161[:], lanes(T.MW, 1), -2048.0, None, A.add, None, ["MW"], ["O161"])
            ts(T.BIAS[:, 0:5:4], T.ZERO[:, 0:2], T.THC[:, 0:1], -64.0 - FO, A.subtract, A.add, ["THC", "ZERO"],
               ["BIAS#0", "BIAS#4"])
        chores = [lambda: ts(T.SO[:, 0:16], T.PS[:, 16:32], 40.0 - 2048.0, 1e4, A.is_lt, A.mult, ["PS"], ["SO#0"]),
                  lambda: tt(T.SO[:, 16:32], T.PS[:, 0:16], T.SO[:, 0:16], A.add, ["PS", "SO#0"], ["SO#1"]),
                  lambda: tt(T.SO[:, 32:48], T.SO[:, 16:32], T.DUL[:], A.min, ["SO#1", "DUL"], ["SO#2"]),
                  lambda: ts(T.SOF[:], T.SO[:, 32:48], 2048.0, None, A.add, None, ["SO#2"], ["SOF"])]
        if t == 0:
            chores = [lambda: ts(T.DUL[:], T.SO[:, 0:16], PK, None, A.add, None, ["SO#0", "PF"], ["DUL"]),
                      lambda: ts(T.DUM[:], T.C6[:], PK, None, A.add, None, ["C6", "PF"], ["DUM"])] + chores + [
                      lambda: ts(T.DUM2[:], T.C6[:], PK, 2.0, A.add, A.mult, ["C6", "PF"], ["DUM2"])]
        else:
            chores += [lambda: tt(T.TC[:, 0:16], T.RR[:, 15:256:16], T.DL[:, :, 0:2], A.mult, ["RR", "DL"], ["TC#0"]),
                       lambda: tt(T.TC[:, 16:32], T.TC[:, 0:16], T.VP[:, :, 0:2], A.add, ["TC#0", "VP"], ["TC#1"]),
                       lambda: cp(T.O2C[:], T.TC[:, 16:32], ["TC#1"], ["O2C"])]

        def chore():
            chores.pop(0)()

        lands("at%d" % t, (2 if t == 0 else 1) * share(cores[voters[t]], [core]), ["TBL"])
        ts(T.MSG[:, 32:48], T.PS[:, 32:48], 2048.0 - 8 * (1 - a), 2047.0, A.add, A.min, ["PS"], ["MSG#p"])
        ts(T.MSG[:, 0:32], T.PS[:, 0:32], 2048.0, None, A.add, None, ["PS"], ["MSG#c"])
        tt(T.EV[:], T.TBL[:, t, :].indirect(T.MSG[:, 32:48]), T.VC[:, a, :], A.is_equal, ["TBL", "MSG#p", "VC%d" % a],
           ["EV"])
        act(T.NF[:], T.IOT[:, 0:512].indirect(T.MSG[:, 16:32]), AF.Identity, ["IOT#0", "IOT#256", "MSG#c", "BIAS#0"],
            ["NF"], bias=T.BIAS[:, 0:1])
        mms("PA", lo, [("BLK", T.EV[:], ["EV"]), ("ID", T.NF[:], ["NF"])])
        tt(T.EE[:, 0, 0:256], T.IOT[:, 0:W].indirect(T.MSG[:, 0:16]), T.EC[:], A.add, ["IOT", "MSG#c", "EC"], ["EE#e"])
        act(T.EE[:, 1, 0:257], T.EE[:, 0, 0:257], AF.Identity, ["EE#e", "EE#s"], ["EE#f"], bias=16.0 * STEPC)
        chore()
        ts(T.S2[:], T.PA[:, lo], 0.0, 1.0 * STEPC, A.is_ge, A.mult, ["PA"], ["S2"])
        chore()
        scan(T.CT[:, 1:257], T.ZERO[:], T.S2[:], T.CT[:, 0:1], A.add, A.add, ["ZERO", "S2", "CT#i"], ["CT#0"])
        chore()
        for c in range(2):
            scan(T.SC[:, c, 0:257], T.CT[:, 0:257], T.EE[:, c, 0:257], 0.0, A.min, A.max,
                 ["CT", "EE#s", "EE#" + "ef"[c]], ["SC#%d" % c])
        chore()
        tt(T.EI[:, 0:2], T.SC[:, :, 256], T.OFS[:], A.add, ["SC", "OFS"], ["EI#0"])
        chore()
        ts(T.EI[:, 2:4], T.EI[:, 0:2], 4095, None, A.bitwise_and, None, ["EI#0"], ["EI#1"])
        ts(T.EI[:, 4:6], T.EI[:, 0:2], 12, None, A.arith_shift_right, None, ["EI#0"], ["EI#2"])
        cp(T.C16[:], T.EI[:, 2:4], ["EI#1"], ["C16"])
        ts(T.CVF[:, 4:6], T.EI[:, 2:4], FO, None, A.add, None, ["EI#1"], ["CVF#f"])
        ts(T.NE[:, 0:35:34], T.EI[:, 0:2], 4096.0, B2, A.is_lt, A.mult, ["EI#0"], ["NE#e"])
        for c in range(2):
            ts(T.NE[:, 1 + 34 * c:33 + 34 * c], T.IOT[:, 0:W].indirect(T.C16[:]), T.CVF[:, 4 + c:5 + c], B2,
               A.is_equal, A.mult, ["IOT", "C16", "CVF#f"], ["NE#%d" % c])
        ts(T.CVF[:, 2:4], T.EI[:, 4:6], -16.0, float(W + 8 * a + r), A.mult, A.add, ["EI#2"], ["CVF#v"])
        scan(T.NS[:, 0:67], T.NE[:, 0:67], T.STEP[:, 0:67], 0.0, A.max, A.add, ["STEP", "NE"], ["NS"])
        cp(T.CVF[:, 0:2], T.EI[:, 2:4], ["EI#1"], ["CVF#c"])
        for c in range(2):
            ts(ALL[:, r, c:4:2], T.CVF[:, c:4:2], T.NS[:, 32 + 34 * c:33 + 34 * c], T.DUM[:, r, c:c + 1],
               A.max, A.min, ["CVF", "NS", "DUM"], ["ALL#o%d" % c])
        others = [cores[(r + i) % N] for i in range(1, N)]
        mine = ["ALL#o0", "ALL#o1"]
        send(ALL[:, r, 0:4], [(c, ALL[:, r, 0:4]) for c in others], "aa%d" % t, mine)
        lands("aa%d" % t, sum(share(c, [d for d in cores if d != c]) for c in others), ["ALL#r"])
        while chores:
            chore()
        if t == 0:
            order("g", ["XR0#x"], [])
            for j in range(8, 16):
                iota(T.XR0[:, j:W:16], [[0, 256]], int(BIG), 0, ["XR0#%d" % j])

        if t > 0:
            mms("D1", lo, [("ID", T.UU[:, lo], ["UU"]), ("ID", T.UU[:, hi], ["UU"])])
        if t == 1:
            mms("D2", lo, [("ID16", T.M16[:], ["M16"])])
            act(lanes(T.MF, 1), T.D2[:, lo], AF.Identity, ["D2"], ["MF"], bias=2040.0)
            act(xl(0), T.D1[:, lo], AF.Copy, ["D1"], ["XL1"])
        if t == 0:
            minus(1, (2, 4))
        act(T.XC[:], XR[1 - a][:].indirect(T.SOF[:]), AF.Copy, [XK[1 - a], XLK[1 - a], "SOF"], ["XC"])
        mms("D0", lo, [("ID", xl(a), [XLK[1 - a]]), ("ID", T.XC[:], ["XC"])])
        if t == 0:
            mfloat(3)
            bylane(1, 0)
            bylane(0, 0)
        else:
            mms("D4", lo, [("ID16", T.M16[:], ["M16"]), ("NID4K", T.PVN[:], ["PVN"]), ("ID32", T.RY[:], ["RY"])])
        if t == 2:
            act(T.YX[:, 1:512:2], T.D1[:, lo], AF.Copy, ["D1"], ["YX#b"])
        act(T.T1[:], T.D0[:, lo], AF.Identity, ["D0"], ["T1"], bias=RND, scale=0.5 - 2.0 ** -13)
        if t < 2:
            act(lanes(XR[a], a), T.T1[:], AF.Identity, ["T1"], [("XR0#x", "XR1")[a]], bias=-RND)
            act(T["SM%d" % t][:], T.T1[:], AF.Identity, ["T1"], ["SM%d" % t], bias=-RND)
        else:
            act(T.YX[:, 0:512:2], T.T1[:], AF.Identity, ["T1"], ["YX#a"], bias=-RND)
        if t == 0:
            xtrans(2, [T.SM0[:, 0:128], T.SM0[:, 128:256]], ["SM0"], "D2")
        else:
            act(T.YM[:, a:512:2], T.D4[:, lo], AF.Identity, ["D4"], ["YM#%d" % a], bias=2048.0)
        if t < 2:
            act(T.PB[:, hi], T.VB[:], AF.Identity, ["VB"], ["PB"], bias=8.0 * (1 - a) + FO)
            if t == 0:
                bylane(1, 1)
                bylane(0, 1)
            else:
                minus(2, (0, 1))
            for j in [j for j in range(8) if j not in XV][4::-1]:
                pre(t + 1, j)
        if t == 1:
            wait("s", "left", total["left"])
            code(T.TBS[:, 0, r:2048:8], lanes(T.MF, 1), ["MF"], ["TBS0"], 8)
            order("g", ["ALL"], [])
            offer(2)

        if t == 0:
            for i in range(1, 4):
                picks(i)
        elif t == 1:
            pi(1)
            pi(2)
            pi(3)
            cp(lanes(T.MW, 1), T.OFF[:], ["OFF"], ["MW"])
            cp(T.XR1[:, 0:WD].indirect(T.O2C[:]), T.BIGS[:], ["O2C", "BIGS"], ["XR1"])
        else:
            dma("y", "out", lambda: g.sync.dma_start(T.ym[:], T.YM[:]), ["YM"], [])
            ts(T.OI[:, 0:2], ALL[:, r, 2:4], 1 / 16.0, 255.0, A.mult, A.min, mine, ["OI"])
            ts(T.TV[:, 0:2], ALL[:, r, 2:4], 0.125, -r / 8.0, A.mult, A.add, mine, ["TV#0"])
            pi(1)
            pi(2)
            for c in range(2):
                ts(T.OI[:, 2 + c:3 + c], ALL[:, r, 2 + c:3 + c], 512.0 - W, T.TV[:, c:c + 1], A.add, A.max,
                   mine + ["TV#0"], ["OY#%d" % c])
            act(T.OX[:, 0:32], xl(0).indirect(T.OI[:, 0:2]), AF.Copy, ["XL1", "OI"], ["OX#0"])
            act(T.OX[:, 32:64], T.YX[:].indirect(T.OI[:, 2:4]), AF.Copy, ["YX", "OY"], ["OX#1"])
            pi(3)
            tt(T.OX[:, 64:96], T.OX[:, 32:64], T.OX[:, 0:32], A.subtract, ["OX#0", "OX#1"], ["OX#2"])

        own, ok = (T.FT, "FT") if t < 2 else (T.PI, "PI")
        src, sk = (T.MF, ["MF", "MFd"]) if t < 2 else (T.IOT, ["IOT"])
        fill = [lambda: cp(T.CVL[:, 0:16], ALL[:, :, 0:2], ["ALL"], ["CVL#c"]),
                lambda: cp(T.CVL[:, 16:32], ALL[:, :, 2:4], ["ALL"], ["CVL#v"])]
        if t < 2:
            fill += [lambda: cp(T.VCF[:], ALL[:, :, 0:4], ["ALL"], ["VCF"]),
                     lambda: tt(T.DL[:], T.DUM[:], T.VCF[:], A.subtract, ["DUM", "VCF"], ["DL"]),
                     lambda: tt(T.VP[:], T.DUM2[:], T.VCF[:], A.subtract, ["DUM2", "VCF"], ["VP"])]
        if t == 0:
            fill += [lambda: ms(T.PI[:, 0:256], -1.0, ["PI"]), lambda: bylane(1, 2), lambda: bylane(0, 2)]
        for p in range(N - 1, -1, -1):
            c = slice(32 * p, 32 * p + 32)
            act(T.VALV[:, c], src[:].indirect(ALL[:, p, 2:4]), AF.Identity, sk + ["ALL"], ["VALV#%d" % p],
                bias=FO + 8 + (p + 1) / 128.0 if t < 2 else -FO)
            if fill:
                fill.pop(0)()
            cp(own[:].indirect(ALL[:, p, 0:2]), T.VALV[:, c], ["ALL", "VALV#%d" % p], [ok])
        act(T.VALC[:], src[:].indirect(T.CVL[:, 0:16]), AF.Identity, sk + ["CVL#c"], ["VALC"],
            bias=FO + 8 + 1 / 16.0 if t < 2 else -FO)
        if t < 2:
            act(T.PV[:], T.IOT[:].indirect(T.CVL[:]), AF.Identity, ["IOT", "CVL"], ["PV"], bias=-FO)
        else:
            act(T.D0[:, lo], T.VALC[:], AF.Identity, ["VALC"], ["D0"], bias=1.0)
        if t == 0:
            table1(192, 256)
            offer(1)
            copies("fp", [(T.PI[:, 256:512], T.PI[:, 0:256], ["PI"], "PI"), (T.PI[:, W:WD], T.PI[:, 0:256], ["PI"], "PI")])
            for n in (512, 1024, 2048):
                copies("fp", [(T.PI[:, n:2 * n], T.PI[:, 0:n], ["PI"], "PI")])
        tt(T.S1[:], own[:].indirect(T.CVL[:, 0:16]), T.VALV[:], A.not_equal, [ok, "CVL#c", "VALV"], ["S1"])
        if t == 2:
            tt(T.OX[:, 96:128], T.S1[:, 32 * r:32 * r + 32], T.OX[:, 64:96], A.mult, ["S1", "OX#2"], ["OX#3"])
            tt(T.S2[:], T.S1[:], T.D0[:, lo], A.mult, ["S1", "D0"], ["S2"])
            tt(T.YX[:].indirect(T.OI[:, 2:4]), T.OX[:, 0:32], T.OX[:, 96:128], A.add, ["OY", "OX"], ["YX"])
            dma("s", "out", lambda: g.scalar.dma_start(T.yx[:], T.YX[:, 0:512]), ["YX"], [])
            tt(T.PI[:].indirect(T.CVL[:, 16:32]), T.VALC[:], T.S2[:], A.subtract, ["CVL#v", "VALC", "S2"], ["PI"])
            dma("y", "out", lambda: g.sync.dma_start(T.yp[:], T.PI[0:128:16, 0:W]), ["PI"], [])
            break
        scan(T.RR[:], T.S1[:], T.SCN[:], 0.0, A.max, A.add, ["SCN", "S1"], ["RR"])
        tt(T.TV[:, 0:16], T.RR[:, 15:256:16], T.DL[:, :, 2:4], A.mult, ["RR", "DL"], ["TV#0"])
        tt(T.TV[:, 16:32], T.TV[:, 0:16], T.VP[:, :, 2:4], A.add, ["TV#0", "VP"], ["TV#1"])
        cp(T.O2V[:], T.TV[:, 16:32], ["TV#1"], ["O2V"])
        op("s", lambda: S.activation(T.FT[:].indirect(T.O2V[:]), T.VALC[:], AF.Silu), ["O2V", "VALC"], ["FT"])
        cp(XR[a][:, 0:WD].indirect(T.O2V[:]), T.BIGS[:], ["O2V", "BIGS"], [XK[a]])

        u = t + 1
        OLD, oldk = T["OLD%d" % (u % 2)], "OLD%d" % (u % 2)

        def follow(j0, j1):
            ts(T.G16[:, 512 * j0:512 * j1], T.FT[:, 0:W].indirect(OLD[:, 32 * j0:32 * j1]), -2048.0 - FO, None, A.add,
               None, ["FT", oldk], ks("G16", j0, j1))

        def follows(k0, k1):
            act(T.G32[:, 128 * k0:128 * k1], T.FT[:, 0:W].indirect(T.OLDT[:, u % 2, 8 * k0:8 * k1]), AF.Identity,
                ["FT", "OLDT%d" % (u % 2)], ks("G32", k0, k1), bias=-2048.0 - FO)

        def keep(j0, j1, bk):
            for k in range(16):
                mm(T[bk][:, 0:32 * (j1 - j0)], T.DK16[:, 128 * k:128 * k + 128], T.G16[:, 512 * j0 + k:512 * j1:16],
                   k == 0, k == 15, ["DK16"] + ks("G16", j0, j1), [bk])

        def keepl(k0, k1):
            for k in range(k0, k1):
                mm(T.PS[:, k:128:16], T.G32[:, 128 * k:128 * k + 128], T.KB[:, 8 * k:8 * k + 8], True, True,
                   ["KB", "G32#%d" % k], ["PS"])

        def turn(bk):
            cp(T.L16[:], T.PS[:, 0:128], ["PS"], ["L16"])
            mm(T[bk][:, 0:128], T.L16[:], T.ID16[:], True, True, ["L16", "ID16"], [bk])

        def xv(j, n0=0, n1=32):
            i = XV.index(j)
            tt(T.GX[:, 512 * j + 16 * n0:512 * j + 16 * n1],
               XR[1 - u % 2][:, 0:W].indirect(T.OFF[:, 32 * j + n0:32 * j + n1]),
               T.XRP[:, 512 * i + 16 * n0:512 * i + 16 * n1], A.add, [XK[1 - u % 2], "OFF#%d" % j, "XRP#%d" % j],
               ["GX#%d" % j if n0 == 0 else "GY"])

        def abv(j, n0=0, n1=32):
            c = slice(512 * j + 16 * n0, 512 * j + 16 * n1)
            act(T.AB[:, c], T.GX[:, c], AF.Abs, ["GX#%d" % j if n0 == 0 else "GY"], ["AB#%d" % j])

        def offs(j0, j1, bk):
            ts(T.OFF[:, 32 * j0:32 * j1], T[bk][:, 0:32 * (j1 - j0)], 2048.0, None, A.add, None, [bk],
               ks("OFF", j0, j1))

        def x(j):
            gx(u, j)
            dmm(u, j)

        def pvn():
            tt(T.PVN[:], lanes(T.FT, u % 2), T.PB[:, hi], A.not_equal, ["FT", "PB"], ["PVN"])

        def m16():
            ts(T.M16[:], T.OFF[:], -2048.0, None, A.add, None, ["OFF"], ["M16"])

        follow(0, 2)
        for k0, k1 in ((0, 2), (2, 6)):
            follows(k0, k1)
            keepl(k0, k1)
        follows(6, 11)
        keep(0, 2, "PA")
        pvn()
        follow(2, 3)
        keepl(6, 11)
        follows(11, 16)
        offs(0, 2, "PA")
        follow(3, 4)
        keepl(11, 13)
        keep(2, 4, "PB")
        keepl(13, 16)
        gx(u, 0)
        xv(1)
        dmm(u, 0)
        offs(2, 4, "PB")
        eq(u, 0, 1)
        turn("PA")
        abv(1)
        eq(u, 1, 2)
        offs(4, 8, "PA")
        m16()
        x(2)
        ab(0)
        pen(u, 0)
        pen(u, 1)
        names(u)
        eq(u, 2, 4)
        x(3)
        ab(2)
        x(4)
        score("EQ", 0, 4)
        ab(3)
        x(5)
        score("AB", 0, 4, True)
        ab(4)
        eq(u, 4, 8)
        x(6)
        ab(5)
        xv(7, 0, 20)
        xv(7, 20, 32)
        score("EQ", 4, 8)
        ab(6)
        score("AB", 4, 7, True)
        abv(7, 0, 20)
        abv(7, 20, 32)
        best(0)
        score("AB", 7, 8, True)
        op("s", lambda: S.activation(T.TC[:, 32:48], T.TV[:, 16:32], AF.Sign, bias=T.BIAS[:, 10:11], scale=-1.0,
                                     accum_out=T.AC[:, 0:1]), ["TV#1", "BIAS#10"], ["WON", "AC#0"])
        mm(T.D0[:, 0:1], T.ONE32[:], T.AC[:, 0:1], True, True, ["ONE32", "AC#0"], ["D0"])
        act(T.AC[:, 1:2], T.D0[:, 0:1], AF.Identity, ["D0", "BIAS#4"], ["AC#1"], bias=T.BIAS[:, 4:5], scale=-0.5)
        act(T.AC[:, 2:3], T.D0[:, 0:1], AF.Identity, ["D0"], ["AC#2"], bias=-3.0)
        act(T.AC[:, 3:4], T.AC[:, 2:3], AF.Identity, ["AC#2"], ["AC#3"], bias=RND, scale=0.125)
        act(T.AC[:, 2:3], T.AC[:, 3:4], AF.Identity, ["AC#3"], ["AC#2"], bias=-RND)
        act(T.BIAS[:, 0:1], T.AC[:, 2:3], AF.Identity, ["AC#1", "AC#2"], ["BIAS#0"], bias=T.AC[:, 1:2], scale=4.0)
        if u == 1:
            for j in range(8):
                iota(T.XR1[:, j:W:16], [[0, 256]], int(BIG), 0, ["XR1"] if j == 0 else ["XR1#%d" % j])

    for s, v in total.items():
        wait("g", s, v)
